import numpy as np, ml_dtypes
CORES = [5,29,101,125,133,157,229,253]
N = 8
BF = ml_dtypes.bfloat16
M, P, T, H, C, HM = 1152, 128, 4, 3, 32, 1024
E = M + T * P
def crowd(rng, cen, s, n):
    pick = (rng.random((N, 8, 1, n)) * s).astype(np.int64)
    return np.clip(np.take_along_axis(cen, pick, 3) + rng.integers(-1, 2, (N, 8, 16, n)), 0, 15)
def rows(rng):
    v = np.arange(M); i = np.arange(16)[:, None]
    a = np.where(i < rng.integers(2, 17, (N, 8, 1, M)), rng.integers(0, M, (N, 8, 16, M)), E)
    a[:, :, 1] = np.where(v < M - P, v + P, E)
    own = v - P * (1 + (rng.random((N, 8, M)) * (v // P)).astype(np.int64)); low = (rng.random((N, 8, M)) * v).astype(np.int64)
    k = np.where(rng.random((N, 8, M)) < 0.6, own, low)
    a[:, :, 0] = np.where((v < P) | (rng.random((N, 8, M)) < 0.04), E, k)
    return a
def base(rng):
    s = rng.choice(np.array([4, 8, 12, 16, 32]), (N, 8, 1, 1)); cen = np.repeat(rng.integers(0, 16, (1, 8, 16, 32)), N, 0)
    return crowd(rng, cen, s, M), rows(rng), crowd(rng, cen, s, T * P), rng.integers(0, 256, (N, 8, 16, 1)), rng.integers(10, 30, (N, 8, 16, 1))
def pack(f, a, x, w, t):
    return {"fr": np.ascontiguousarray(f.reshape(N, 128, M)).astype(np.float32).astype(BF), "ptr": np.ascontiguousarray(a.reshape(N, 128, M)).astype(np.int32),
            "nw": np.ascontiguousarray(x.reshape(N, 128, T * P)).astype(np.float32).astype(BF),
            "hw": np.ascontiguousarray(w.reshape(N, 128, 1)).astype(np.int32), "th": np.ascontiguousarray(t.reshape(N, 128, 1)).astype(np.int32)}
def setup_inputs(rng):
    return pack(*base(rng))
def setup_inputs_room(rng):
    f, a, x, w, t = base(rng); f = np.minimum(f, 10)
    for q in range(N):
        for g in range(8):
            n = int(rng.choice(np.array([0, 1, C - 1, C, C + 1, P])))
            if q == 0: n = (C, C + 1, P, C - 1, 1, 0, C, C + 1)[g]
            o = rng.permutation(P); esc, rest = o[:n], o[n:]
            k = rng.integers(0, M - P, P - n); a[q, g, 0, M - P + rest] = k; x[q, g][:, rest] = f[q, g][:, k + P]
            a[q, g, 0, M - P + esc] = E
            far = esc[:n // 2]; k = P * rng.integers(1, M // P - 1, len(far)) + far
            a[q, g, 0, M - P + far] = k; a[q, g, 0, k] = k - P; a[q, g, 0, k - P] = E
            x[q, g][:, far] = 15 - rng.integers(0, 2, (16, len(far)))
    return pack(f, a, x, w, t)
def jog(rng, n):
    return (np.arange(16)[:, None] == rng.integers(0, 16, (N, 8, 1, n))) * rng.choice(np.array([-4, 4]), (N, 8, 1, n))
def setup_inputs_ties(rng):
    f, a, x, w, t = base(rng); cen = np.repeat(rng.integers(4, 12, (1, 8, 16, 1)), N, 0)
    f = cen + jog(rng, M); x = cen + jog(rng, T * P) * ((np.arange(T * P) // P) & 1)
    t = rng.integers(3, 6, (N, 8, 16, 1)); t[:, 1::2] = 3
    return pack(f, a, x, w, t)
def setup_inputs_loops(rng):
    f, a, x, w, t = base(rng); v = np.arange(M)
    a[:, :, 2:] = np.where(rng.random((N, 8, 14, M)) < 0.5, rng.integers(0, M, (N, 8, 14, M)), E)
    mate = np.where((((v // P) & 1) == 0) & (v + P < M), v + P, v - P)
    a[:, ::2, 0] = np.where(rng.random((N, 4, M)) < 0.4, v, np.where(rng.random((N, 4, M)) < 0.6, mate, a[:, ::2, 0]))
    a[:, 1, 0] = rng.choice(np.array([0, M - 1, M // 2, E]), (N, M))
    a[:, 3, 2:] = rng.integers(0, M, (N, 14, M)); a[:, 5, 2:] = E; a[:, 7, 2:] = rng.integers(0, M, (N, 1, M))
    return pack(f, a, x, w, t)
def setup_inputs_calm(rng):
    f, a, x, w, t = base(rng); q = [int(c) for c in rng.permutation(8)]
    t[:, q[0]] = 240; a[:, q[0], 0] = np.where(a[:, q[0], 0] == E, rng.integers(0, M, (N, M)), a[:, q[0], 0])
    a[:, q[1], 0] = E
    t[:, q[2]] = 0; f[:, q[2]] = 15 * rng.integers(0, 2, (N, 1, M)); x[:, q[2]] = 15 * rng.integers(0, 2, (N, 1, T * P))
    t[1::2, q[2], 2::2] = 239; t[1::2, q[2], 3::2] = 240
    w[:, q[3]] = 0; w[:, q[4]] = 255
    t[:, q[5]] = 240; t[:, q[5], 1] = 0
    f[:, q[6]] = rng.integers(0, 2, (N, 16, M)); x[:, q[6]] = np.where(((np.arange(T * P) // P) & 1) == 1, 0, 14) + rng.integers(0, 2, (N, 16, T * P))
    a[:, q[6], 0] = np.where(a[:, q[6], 0] < M - P, a[:, q[6], 0], rng.integers(0, M - P, (N, M)))
    w[:, q[6]] = rng.integers(225, 256, (N, 16, 1)); t[:, q[6]] = rng.integers(128, 208, (N, 16, 1))
    f[:, q[7]] = np.abs(15 * rng.integers(0, 2, (N, 1, M)) - rng.integers(0, 2, (N, 16, M)))
    x[:, q[7]] = np.abs(15 * rng.integers(0, 2, (N, 1, T * P)) - rng.integers(0, 2, (N, 16, T * P)))
    a[:, q[7], 0] = np.where(a[:, q[7], 0] == E, rng.integers(0, M, (N, M)), a[:, q[7], 0])
    w[:, q[7]] = rng.integers(128, 256, (N, 16, 1)); t[:, q[7]] = rng.integers(0, 241, (N, 16, 1))
    return pack(f, a, x, w, t)
def setup_inputs_spread(rng):
    f, a, x, w, t = base(rng); e = np.array([0.25, 0.5, 1.0, 1.0, 2.0, 4.0])
    f = np.minimum((16 * rng.random((N, 8, 16, M)) ** rng.choice(e, (N, 8, 1, M))).astype(np.int64), 15)
    x = np.minimum((16 * rng.random((N, 8, 16, T * P)) ** rng.choice(e, (N, 8, 1, T * P))).astype(np.int64), 15)
    a = np.where(rng.random((N, 8, 16, M)) < rng.random((N, 8, 1, M)), rng.integers(0, M, (N, 8, 16, M)), E)
    a[:, :, 0] = np.where(rng.random((N, 8, M)) < 0.1, E, rng.integers(0, M, (N, 8, M)))
    a[:, :, 1, :M - P] = rng.integers(0, M, (N, 8, M - P))
    t = rng.choice(np.array([0, 20, 40, 50, 60, 60, 70, 240]), (N, 8, 16, 1)); t = np.where(rng.random((N, 8, 1, 1)) < 0.5, np.minimum(t, 60), t)
    return pack(f, a, x, w, t)
def check_inputs(d):
    bad = []
    for k in ("fr", "nw"):
        z = d[k].astype(np.float32)
        if not np.all((z >= 0) & (z <= 15) & (z == np.floor(z))): bad.append("whole numbers from 0 to 15 in " + k)
    for k, hi in (("hw", 255), ("th", 240)):
        if np.min(d[k]) < 0 or np.max(d[k]) > hi: bad.append("range of " + k)
    a = d["ptr"]; full = (a >= 0) & (a < M)
    if not np.all(full | (a == E)): bad.append("range of ptr")
    if not np.all(full[:, 1::16, :M - P]): bad.append("row 1 of an old state before the last P is empty")
    return bad
def gaps(F, c, x):
    out = np.empty(c.shape, np.int64)
    for a in range(N):
        for g in range(8): out[a, g] = np.add.reduce(np.abs(F[a, g][:, c[a, g]] - x[a, g][:, None, :]), axis=0)
    return out
def reference(fr, ptr, nw, hw, th):
    F = np.full((N, 8, 16, E + 1), 99, np.int32); F[..., :M] = fr.astype(np.float32).astype(np.int32).reshape(N, 8, 16, M)
    A = np.full((N, 8, 16, E + 1), E, np.int64); A[..., :M] = ptr.reshape(N, 8, 16, M)
    X = nw.astype(np.float32).astype(np.int32).reshape(N, 8, 16, T, P)
    w = hw.astype(np.int64).reshape(N, 8, 16, 1); lim = th.astype(np.int64).reshape(N, 8, 16, 1); piece = np.arange(P)
    for t in range(T):
        n0 = M + P * t; n = n0 + piece; x = X[:, :, :, t]
        F[..., n0:n0 + P] = x; A[:, :, 1, n0 - P:n0] = n
        k = np.array(A[:, :, 0, n0 - P:n0]); link = np.full((N, 8, P), E, np.int64); going = np.ones((N, 8, P), bool)
        for h in range(H):
            c = np.take_along_axis(A, k[:, :, None, :], 3)
            ok = (gaps(F, c, x) <= lim) & (c < E); ok[:, :, 0] = False
            hit = np.any(ok, axis=2); to = np.take_along_axis(c, np.argmax(ok, axis=2)[:, :, None, :], 2)[:, :, 0]
            link = np.where(going & hit, to, link); going = going & ~hit
            free = c == E; free[:, :, 0] = False
            wr = going & (k < E) & ((k & (P - 1)) == piece) & np.any(free, axis=2)
            a, g, p = np.nonzero(wr); A[a, g, np.argmax(free, axis=2)[wr], k[wr]] = n[p]
            k = np.where(going, c[:, :, 0], k)
        A[:, :, 0, n0:n0 + P] = np.where(going, k, link)
        if t < T - 1:
            for a in range(N):
                b = (a + 1 + t % (N - 1)) % N
                for g in range(8):
                    ps = np.nonzero(going[a, g])[0][:C]; z = x[a, g][:, ps].astype(np.int64)
                    q = np.add.reduce(w[b, g] * z, axis=0) & (HM - 1)
                    c = A[b, g][1:, q]
                    best = np.argmin(np.add.reduce(np.abs(F[b, g][:, c] - z[:, None, :]), axis=0), axis=0)
                    f = F[b, g][:, c[best, np.arange(len(ps))]]
                    X[a, g][:, t + 1, ps] = (X[a, g][:, t + 1, ps] + f) >> 1
    return {"yp": np.ascontiguousarray(A[..., :E]).reshape(N, 128, E).astype(np.float32), "yx": X.reshape(N, 128, T * P).astype(np.float32).astype(BF)}

@@ -1,0 +1,749 @@
+from concourse.bass import DstId, RemoteDMATransfer
+from concourse.mybir import AluOpType, ActivationFunctionType
+
+ALU = AluOpType
+ACT = ActivationFunctionType
+M, P, NT, E = 1152, 128, 4, 1664
+NF = [2, 2, 2]
+CHH = [512, 512, 256]
+ONVK = {(0, 'dd', 0), (0, 'nk', 0), (0, 'nk', 128), (0, 'ra', 4864), (0, 'ra', 5632), (0, 'xz', 0), (1, 'F', 0), (1, 'dd', 0),
+        (1, 'ra', 0), (1, 'ra', 3584), (1, 'ra', 4608), (1, 'ra', 5120), (1, 'xz', 0), (2, 'F', 0), (2, 'dd', 0), (2, 'ra', 3072),
+        (2, 'ra', 3584), (2, 'ra', 5120), (2, 'ra', 5888), (2, 'xz', 0), (3, 'F', 0), (3, 'a0', 256), (3, 'dd', 0), (3, 'nk', 128),
+        (3, 'ra', 3072), (3, 'ra', 4096), (3, 'ra', 5888), (3, 'xz', 0)}
+DUE = {'c0': -5.5, 'c1': -0.9, 'c2': 6.4, 'cu0': -21.55, 'raw0': -7.95, 'cu1': -3.55, 'raw1': -6.65, 'cu2': -5.4, 'raw2': -0.15,
+       'sl': -5.15, 'nk0': -11.55, 'nk1': 23.9, 'nk2': 13.9, 'wn0': 1.35, 'wn1': -10.85, 'wn2': 6.05, 'ans': -18.3, 't0': -2.6,
+       'd0': -23.1, 'h0': 2.35, 'p0': 5.3, 't1': -3.75, 'd1': -0.15, 'h1': 0.55, 'p1': -1.7, 't2': 4.4, 'd2': 4.75, 'h2': -1.55,
+       'q': 4.75, 'p2': 5.65, 'co': -3.8, 'ask': 6.75}
+CYC, GATH, SCAT, PEC, SYNC, HOP, BW, LOOK = 1.04, 1.62, 4.0, 0.52, 90.0, 2500.0, 150.0, 40.0
+SAME_WAR = False
+
+F32, BF, I32, U16, F16 = "float32", "bfloat16", "int32", "uint16", "float16"
+SCRATCH = {}
+
+
+def _decl(names, cols, dtype, where="sbuf"):
+    for nm in names.split():
+        SCRATCH[nm] = (where, [128, cols], dtype)
+
+
+_decl("A", 1800, F32)
+_decl("P32", 1672, I32)
+_decl("F FB0 FB1 FB2", 1680, BF)
+_decl("FX", 1280, BF)
+_decl("X dd da", 512, BF)
+_decl("XQ0 XQ1 XQ2 ones esc", 128, BF)
+_decl("CQ0 CQ1 CQ2 CO0 CO1 CO2", 128, F32)
+_decl("hwi thi pi pj", 4, I32)
+_decl("col s1 s2", 32, F32)
+_decl("NV", 640, F32)
+_decl("J", 240, F32)
+_decl("J16 DM MP RB RS R1V tA tB cnt v1 v2 w1 w2 ks", 128, F32)
+_decl("Id Idn BO BOa BOb BOn BOx0 BOx1 BOx2 T1 T2 TM TM3 TMa TMb T3a T3b TH KC pv2 msk", 128, BF)
+_decl("W1 Wp Wn Ww", 144, BF)
+_decl("G8 G8n", 8, BF)
+_decl("I16 BO16 c16", 128, F16)
+_decl("E0w W16", 144, F16)
+_decl("SW", 240, F16)
+_decl("PC DUM nq tq", 24, F32)
+_decl("KI L0", 24, I32)
+_decl("KL L0u SL", 24, U16)
+_decl("QI QA b1 b2", 8, I32)
+_decl("QL POS", 8, U16)
+_decl("CU", 384, U16)
+_decl("raw mx", 6144, BF)
+_decl("nk cc rr", 384, F32)
+_decl("a0 m0 sg mm em", 384, BF)
+_decl("fc", 384, F16)
+_decl("SP", 256, F32)
+_decl("ZI", 256, I32)
+_decl("cqu", 32, U16)
+_decl("INV BL", 2, U16)
+_decl("xo xz", 32, BF)
+_decl("cq16", 32, F16)
+_decl("RR", 16, F16)
+_decl("di", 32, I32)
+_decl("B0 B1 B2 B3 B4 B5 B6 B7", 512, F32, "psum")
+
+SEMAPHORES = ["sV", "sS", "sP", "sG", "ls", "dptr", "dp0", "dfr", "dnw", "dhw", "dth", "dyx", "dy0", "dy1", "dy2",
+              "aXQ0", "aXQ1", "aXQ2", "aCQ0", "aCQ1", "aCQ2", "aFB0", "aFB1", "aFB2",
+              "hX0", "hX1", "hX2", "hC0", "hC1", "hC2", "hB"]
+ESEM = {"V": "sV", "S": "sS", "P": "sP", "G": "sG"}
+WIDTH = {F32: 4, I32: 4, BF: 2, U16: 2, F16: 2}
+_ORDER = {}
+
+
+def R(name, a, b, step=1, p=128):
+    return (name, a, b, step, p)
+
+
+def ncol(r):
+    return (r[2] - r[1] + r[3] - 1) // r[3]
+
+
+def mask_of(engs):
+    m = 0
+    for e in engs:
+        m |= 1 << e
+    return m
+
+
+def pow2(n):
+    k = 1
+    while 2 * k <= n:
+        k *= 2
+    return k
+
+
+def deal(topo, src, dsts):
+    chip = topo.cores_of(src)
+    off = [j for j, d in enumerate(dsts) if d not in chip]
+    on = [j for j, d in enumerate(dsts) if d in chip]
+    res, used = {}, []
+    for part in (off, on):
+        taken = list(used)
+        for k, j in enumerate(part):
+            en = [e for e in topo.engines(src, dsts[j]) if e not in taken]
+            n = pow2(len(en) // len(part))
+            res[j] = en[k * n:(k + 1) * n]
+            used += res[j]
+    return [res[j] for j in range(len(dsts))]
+
+
+def plan(T, topo, r):
+    cores, n = T.cores, len(T.cores)
+    me = cores[r]
+    up = [cores[(r + 1 + t) % n] for t in range(3)]
+    dn = [cores[(r - 1 - t) % n] for t in range(3)]
+    can = [c for c in topo.cores_of(me) if c not in cores and all(topo.may_write(c, d) for d in up + dn)]
+    near = [c for c in can if topo.die(c) == topo.die(me)]
+    far = [c for c in can if topo.die(c) != topo.die(me)]
+    h1 = (near + far)[0]
+    hb = [c for c in far + near if c != h1][0]
+    calls, h1calls = {}, []
+    calls["bulk"] = [(R("F", 0, M), hb, R("FX", 0, M), "hB")]
+    hbcalls = [("hB", [(R("FX", 0, 1280), dn[t], R("FB%d" % t, 0, 1280), "aFB%d" % t)]) for t in range(3)]
+    for s in range(3):
+        src, mid = R("X", 128 * s, 128 * s + 128), R("XQ%d" % s, 0, 128)
+        want = [(up[s], mid, "aXQ%d" % s)]
+        if s > 0:
+            want += [(dn[t], R("FB%d" % t, M + 128 * s, M + 128 * s + 128), "aFB%d" % t) for t in range(s, 3)]
+        mine = [(src, d, o, sem) for d, o, sem in want if topo.may_write(me, d)]
+        via = [(mid, d, o, sem) for d, o, sem in want if not topo.may_write(me, d)]
+        if via:
+            mine.append((src, h1, mid, "hX%d" % s))
+            h1calls.append(("hX%d" % s, via))
+        if s == 0:
+            mine.append((src, hb, R("FX", M, 1280), "hB"))
+        calls["x%d" % s] = mine
+        src, mid = R("CO%d" % s, 0, 128), R("CQ%d" % s, 0, 128)
+        if topo.may_write(me, dn[s]):
+            calls["c%d" % s] = [(src, dn[s], mid, "aCQ%d" % s)]
+        else:
+            calls["c%d" % s] = [(src, h1, mid, "hC%d" % s)]
+            h1calls.append(("hC%d" % s, [(mid, dn[s], mid, "aCQ%d" % s)]))
+    return me, calls, h1, h1calls, hb, hbcalls
+
+
+def arrivals(T, topo, core):
+    tot = {}
+    for r in range(len(T.cores)):
+        me, calls, h1, h1calls, hb, hbcalls = plan(T, topo, r)
+        every = [(me, c) for c in calls.values()] + [(h1, c) for w, c in h1calls] + [(hb, c) for w, c in hbcalls]
+        for src, c in every:
+            for tr, en in zip(c, deal(topo, src, [x[1] for x in c])):
+                if tr[1] == core:
+                    tot[tr[3]] = tot.get(tr[3], 0) + len(en)
+    return tot
+
+
+def ap_of(T, r):
+    if r[3] == 1:
+        return T[r[0]][0:r[4], r[1]:r[2]]
+    return T[r[0]][0:r[4], r[1]:r[2]:r[3]]
+
+
+def remote_call(g, T, topo, src, c):
+    en = deal(topo, src, [x[1] for x in c])
+    if len(c) == 1:
+        rid, pid = topo.addr(c[0][1], src)
+        g.remote_dma(ap_of(T, c[0][2]), ap_of(T, c[0][0]), T.sem[c[0][3]], T.sem["ls"], pid, rid, mask_of(en[0]))
+    else:
+        trs = []
+        for x, e in zip(c, en):
+            rid, pid = topo.addr(x[1], src)
+            trs.append(RemoteDMATransfer(dst_ids=[DstId(rid=rid, pnc=pid)], dma_engine_mask=mask_of(e),
+                                         remote_sem=T.sem[x[3]], src=ap_of(T, x[0]), dst=ap_of(T, x[2])))
+        g.remote_dma_fused(trs, local_sem=T.sem["ls"])
+    return sum(len(e) for e in en)
+
+
+def build(g, T, topo, rank):
+    ops = []
+    due, step, nls, cn = [(0, "c0")], [0], [0], {}
+    me, calls, h1, h1calls, hb, hbcalls = plan(T, topo, rank)
+    arr = arrivals(T, topo, me)
+
+    def ap(x):
+        if x[0] == "ind":
+            return ap_of(T, x[1]).indirect(ap_of(T, x[2]))
+        return ap_of(T, x)
+
+    def sc(x):
+        return ap(x) if isinstance(x, tuple) else x
+
+    def regs(*xs):
+        out = []
+        for x in xs:
+            if isinstance(x, tuple):
+                out += [x[1], x[2]] if x[0] == "ind" else [x]
+        return out
+
+    def add(eng, emit, rd, out, cost, sem=None, lat=0.0, after=None):
+        wr = []
+        if out is not None:
+            if out[0] == "ind":
+                wr, rd = [out[1]], rd + [out[2]]
+            else:
+                wr = [out]
+        ops.append({"e": eng, "f": emit, "r": rd, "w": wr, "c": cost, "sem": sem, "lat": lat, "after": after, "d": due[0]})
+        return len(ops) - 1
+
+    def at(d):
+        due[0] = (step[0], d)
+
+    def vcost(out, ins, two=False):
+        if out[0] == "ind":
+            return 50 + SCAT * 16 * ncol(out[2])
+        if ins[0][0] == "ind":
+            return 50 + GATH * ncol(out)
+        k = 1.0
+        if two:
+            k = 1.0 if any(SCRATCH[x[0]][0] == "psum" for x in ins) else 2.0
+        elif all(WIDTH[SCRATCH[x[0]][2]] == 2 for x in ins + [out]):
+            k = 0.5
+        return CYC * max(64, k * ncol(out))
+
+    def ind(w, o):
+        return ("ind", w, o)
+
+    def cp(out, i):
+        add("V", lambda: g.vector.tensor_copy(ap(out), ap(i)), regs(i), out, vcost(out, [i]))
+
+    def tt(out, a, b, op):
+        add("V", lambda: g.vector.tensor_tensor(ap(out), ap(a), ap(b), op), regs(a, b), out, vcost(out, [a, b], True))
+
+    def ts(out, a, s1, op0, s2=None, op1=None):
+        if op1 is None:
+            f = lambda: g.vector.tensor_scalar(ap(out), ap(a), sc(s1), None, op0)
+        else:
+            f = lambda: g.vector.tensor_scalar(ap(out), ap(a), sc(s1), sc(s2), op0, op1)
+        add("V", f, regs(a, s1, s2), out, vcost(out, [a]))
+
+    def scan(out, d0, d1, init, op0, op1):
+        add("V", lambda: g.vector.tensor_tensor_scan(ap(out), ap(d0), ap(d1), init, op0, op1), regs(d0, d1), out,
+            vcost(out, [d0, d1]))
+
+    def fill(out, val):
+        add("V", lambda: g.vector.memset(ap(out), val), [], out, vcost(out, [out]))
+
+    def act(out, i, func, bias=0.0, scale=1.0):
+        c = 65 + GATH * ncol(out) if i[0] == "ind" else CYC * max(64, ncol(out))
+        if func == ACT.Copy and scale == 1.0:
+            f = lambda: g.scalar.activation(ap(out), ap(i), func)
+        else:
+            f = lambda: g.scalar.activation(ap(out), ap(i), func, bias=sc(bias), scale=sc(scale))
+        add("S", f, regs(i, bias, scale), out, c)
+
+    def take(out, i):
+        cp(out, i)
+        v = ops.pop()
+        act(out, i, ACT.Copy)
+        ops[-1]["key"] = (step[0], out[0][:2], out[1] % 128 if out[0] == "F" else out[1])
+        ops[-1]["alt"] = {"S": (ops[-1]["f"], ops[-1]["c"]), "V": (v["f"], v["c"])}
+
+    def mm(out, l, r, start, stop):
+        add("P", lambda: g.tensor.matmul(ap(out), ap(l), ap(r), start, stop), regs(l, r), out,
+            PEC * max(min(64, ncol(l)), ncol(r)))
+
+    def group(terms):
+        for j, (o, l, r) in enumerate(terms):
+            mm(o, l, r, j == 0, j == len(terms) - 1)
+
+    def iota(out, pat, base, cm):
+        if SCRATCH[out[0]][2] == I32:
+            f = lambda: g.iota(ap(out), pat, base, cm)
+        else:
+            f = lambda: g.iota(ap(out), pat, base, cm, allow_small_or_imprecise_dtypes=True)
+        add("G", f, [], out, 160 + 2 * CYC * ncol(out))
+
+    def load(q, out, src, sem, nbytes):
+        qq = g.sync if q == "Y" else g.scalar
+        add(q, lambda: qq.dma_start(ap(out), src), [], out, 60, sem=(sem, 16), lat=2000 + nbytes / BW)
+
+    def store(q, dst, i, sem, nbytes):
+        qq = g.sync if q == "Y" else g.scalar
+        add(q, lambda: qq.dma_start(dst, ap(i)), [i], None, 60, sem=(sem, 16), lat=2000 + nbytes / BW)
+
+    def send(key):
+        c = calls[key]
+
+        def f():
+            nls[0] += remote_call(g, T, topo, me, c)
+            return None
+        return add("G", f, [c[0][0]], None, 400)
+
+    def recv(out, sem, after, lat):
+        add("N", None, [], out, 0, sem=(sem, arr[sem]), lat=lat, after=after)
+
+    def C(name):
+        if name not in cn:
+            cn[name] = len(cn)
+        return R("col", cn[name], cn[name] + 1)
+
+    def Z(name):
+        return R(name, 0, SCRATCH[name][1][1])
+
+    def Wsl(name, i):
+        return R(name, 15 - i, 143 - i)
+
+    def H(name, h, n=1):
+        return R(name, 128 * h, 128 * (h + n))
+
+    def KL(name, h):
+        return R(name, 8 * h, 8 * h + 8)
+
+    def compact(bank, wide, src):
+        group([(R(bank, 0, 8), Wsl(wide, b), R(src, b, 128, 16)) for b in range(16)])
+
+    load("Y", R("P32", 1024, M), T.ptr[:, 1024:M], "dp0", 128 * 512)
+    load("Y", R("P32", 0, 1024), T.ptr[:, 0:1024], "dptr", 128 * 4096)
+    load("S", R("F", 0, M), T.fr[:], "dfr", 128 * M * 2)
+    load("Y", Z("X"), T.nw[:], "dnw", 128 * 1024)
+    load("Y", R("thi", 0, 1), T.th[:], "dth", 8192)
+    load("Y", R("hwi", 0, 1), T.hw[:], "dhw", 8192)
+    iota(R("pi", 0, 1), [[0, 1]], 0, 1)
+    iota(Z("J"), [[1, 240]], 0, 0)
+    iota(Z("J16"), [[16, 8], [0, 16]], 0, 0)
+    iota(Z("NV"), [[1, 640]], M, 0)
+    iota(Z("tq"), [[0, 3], [16, 8]], 0, 0)
+    cp(C("p"), R("pi", 0, 1))
+    ts(R("pj", 0, 1), R("pi", 0, 1), 15, ALU.bitwise_and)
+    cp(C("i"), R("pj", 0, 1))
+    tt(C("g16"), C("p"), C("i"), ALU.subtract)
+    ts(C("g15"), C("g16"), 15.0, ALU.add)
+    ts(C("r0"), C("i"), 0.0, ALU.is_equal)
+    ts(C("r1"), C("i"), 1.0, ALU.is_equal)
+    ts(C("nr1"), C("i"), 1.0, ALU.not_equal)
+    ts(Z("W1"), R("J", 0, 144), C("g15"), ALU.is_equal)
+    ts(Z("E0w"), Z("W1"), C("r0"), ALU.mult)
+    fill(R("F", M, 1680), 99.0)
+    ts(C("lo"), C("i"), 2.0, ALU.is_ge, float(E), ALU.mult)
+    ts(C("hi"), C("i"), 1.0, ALU.is_ge, float(E), ALU.mult)
+    ts(R("A", M, E), R("NV", 128, 640), C("lo"), ALU.max, C("hi"), ALU.min)
+    ts(R("A", E, E + 1), C("r0"), float(E - 1), ALU.add)
+    fill(R("A", E + 1, 1800), 0.0)
+    ts(Z("R1V"), R("NV", 0, 128), C("r1"), ALU.mult)
+    ts(Z("c16"), R("P32", 1024, M), 1.0, ALU.mult)
+    cp(R("A", 0, 1024), R("P32", 0, 1024))
+    ts(Z("tB"), R("P32", 1024, M), C("nr1"), ALU.mult)
+    tt(R("P32", 1024, M), Z("tB"), Z("R1V"), ALU.max)
+    cp(R("A", 1024, M), R("P32", 1024, M))
+    fill(R("P32", M, E), 0)
+    ts(R("P32", E, E + 1), C("r0"), float(E - 1), ALU.add)
+    J128 = R("J", 0, 128)
+    at("c1")
+    ts(Z("Id"), J128, C("p"), ALU.is_equal)
+    ts(Z("BO"), Z("J16"), C("g16"), ALU.is_equal)
+    ts(Z("T1"), J128, C("p"), ALU.is_gt)
+    tt(Z("T2"), Z("T1"), Z("Id"), ALU.subtract)
+    tt(Z("TM"), Z("T2"), Z("BO"), ALU.mult)
+    tt(Z("TM3"), Z("TM"), Wsl("W1", 0), ALU.add)
+    for o, i, s in (("Wn", "W1", -1.0), ("Wp", "W1", 2.0), ("Idn", "Id", -1.0), ("BOa", "BO", 2048.0),
+                    ("BOb", "BO", 4096.0), ("BOn", "BO", -2048.0), ("TMa", "TM", 2048.0), ("TMb", "TM", 4096.0),
+                    ("T3a", "TM3", 2048.0), ("T3b", "TM3", 4096.0)):
+        act(Z(o), Z(i), ACT.Copy, scale=s)
+    act(Z("pv2"), J128, ACT.Copy, scale=2.0)
+    tt(Z("tA"), J128, Z("J16"), ALU.subtract)
+    ts(Z("DM"), Z("tA"), C("i"), ALU.is_equal)
+    ts(Z("RS"), Z("tA"), 0.0, ALU.not_equal)
+    ts(Z("RB"), Z("tA"), 0.0, ALU.is_equal, float(2 ** 26), ALU.mult)
+    for n in sorted(set(NF)):
+        ts(Z("msk"), Z("tA"), float(15 - n), ALU.is_le, -1.0, ALU.mult)
+        tt(Z("BOx%d" % NF.index(n)), Z("msk"), Z("BO"), ALU.mult)
+    at("c2")
+    ts(Z("v1"), J128, 129.0, ALU.add)
+    tt(Z("MP"), Z("v1"), Z("DM"), ALU.mult)
+    cp(Z("I16"), Z("Id"))
+    cp(Z("BO16"), Z("BO"))
+    cp(Z("W16"), Z("W1"))
+    ts(C("i112"), C("i"), 112.0, ALU.add)
+    ts(Z("SW"), Z("J"), C("i112"), ALU.is_equal)
+    act(Z("G8"), R("BO", 0, 128, 16), ACT.Copy, scale=65536.0)
+    act(Z("G8n"), R("BO", 0, 128, 16), ACT.Copy, scale=-32768.0)
+    ts(C("kc0"), C("r0"), float(2 ** 15), ALU.mult, C("i"), ALU.add)
+    ts(Z("KC"), Z("Id"), C("kc0"), ALU.mult, 2048.0, ALU.mult)
+    ts(C("ma0"), C("p"), 16.0, ALU.is_lt)
+    ts(C("ma1"), C("p"), 16.0, ALU.is_ge)
+    fill(Z("ones"), 1.0)
+    fill(Z("SP"), 0.0)
+    fill(Z("ZI"), 0)
+    for t in range(3):
+        fill(R("FB%d" % t, M + 128 * (t + 1), 1680), 99.0)
+    at("c1")
+    ts(Z("PC"), Z("tq"), C("i"), ALU.add)
+    ts(Z("DUM"), Z("PC"), float(E + 1), ALU.add)
+    ts(C("emb"), C("r0"), -8192.0, ALU.mult, float(1 - E), ALU.add)
+    ts(C("pb0"), C("i"), -0.5, ALU.mult, 0.5, ALU.add)
+    ts(C("pb1"), C("pb0"), -8.0, ALU.add)
+    ts(C("pbx"), C("r0"), -7.0, ALU.mult, -16.0, ALU.add)
+    tt(C("pb2"), C("pbx"), C("pb0"), ALU.add)
+    cp(C("th"), R("thi", 0, 1))
+    cp(C("w"), R("hwi", 0, 1))
+    ts(C("hb"), C("r0"), -1024.0, ALU.mult, 0.5, ALU.add)
+    tt(C("thb"), C("th"), C("hb"), ALU.add)
+    ts(Z("TH"), Z("Id"), C("th"), ALU.mult, -2048.0, ALU.mult)
+    ts(Z("Ww"), Z("W1"), C("w"), ALU.mult)
+    at("c0")
+    send("bulk")
+    sx = {0: send("x0")}
+    sq = {}
+    AW, AS, FW = R("A", 0, E + 1), R("A", 0, E + 129), R("F", 0, E + 1)
+    D = [R("B1", 0, 128), R("B2", 0, 128), R("B5", 0, 128)]
+
+    def ra(h, i):
+        return R("raw", 2048 * h + i, 2048 * (h + 1), 16)
+
+    def mo(h, i, n=1):
+        return R("mx", 2048 * h + 128 * i, 2048 * h + 128 * (i + n))
+
+    compact("B4", "E0w", "c16")
+    cp(KL("KL", 0), R("B4", 0, 8))
+    for t in range(NT):
+        n0 = M + 128 * t
+        step[0] = t
+        x = H("X", t)
+        for h in range(3):
+            at("cu%d" % h)
+            first = ind(AW if t else R("P32", 0, E + 1), KL("KL", h))
+            if t and not h:
+                cp(H("cc", 0), first)
+                first = H("cc", 0)
+            cp(H("CU", h), first)
+            if h < 2:
+                cp(Z("c16"), first)
+                compact("B4", "E0w", "c16")
+                cp(KL("KL", h + 1), R("B4", 0, 8))
+            at("raw%d" % h)
+            ch = CHH[h]
+            for c in range(2048 // ch):
+                take(R("raw", 2048 * h + ch * c, 2048 * h + ch * (c + 1)),
+                     ind(FW, R("CU", 128 * h + ch // 16 * c, 128 * h + ch // 16 * (c + 1))))
+        at("sl")
+        cp(Z("KI"), Z("KL"))
+        ts(Z("L0"), Z("KI"), 127, ALU.bitwise_and)
+        cp(Z("L0u"), Z("L0"))
+        tt(Z("nq"), Z("L0"), Z("PC"), ALU.not_equal)
+        tt(Z("tq"), Z("nq"), Z("DUM"), ALU.mult)
+        tt(Z("nq"), Z("tq"), Z("KI"), ALU.max)
+        cp(Z("SL"), Z("nq"))
+        for h in range(3):
+            at("nk%d" % h)
+            take(H("nk", h), ind(H("NV", t), KL("L0u", h)))
+        for h in range(3):
+            at("wn%d" % h)
+            for i in range(1, 16 - NF[h]):
+                mm(D[h], Wsl("Wn", i), ra(h, i), i == 1, False)
+        if t > 0:
+            s = t - 1
+            at("ans")
+            fb = "FB%d" % s
+            FBW = R(fb, 0, E + 1)
+            hops = len([1 for w, c in h1calls if w == "hC%d" % s]) + 1
+            recv(R(fb, 0, M + 128 * t), "aFB%d" % s, sx[s], 2 * HOP)
+            recv(Z("CQ%d" % s), "aCQ%d" % s, sq[s], hops * HOP)
+            cp(Z("cqu"), ind(Z("CQ%d" % s), Z("INV")))
+            for c in range(2):
+                take(R("dd", 256 * c, 256 * c + 256), ind(FBW, R("cqu", 16 * c, 16 * c + 16)))
+            for c in range(2):
+                tt(R("da", 256 * c, 256 * c + 256), R("dd", 256 * c, 256 * c + 256), R("B7", 256 * c, 256 * c + 256), ALU.max)
+            cp(Z("cq16"), ind(Z("CQ%d" % s), Z("INV")))
+            key = R("B6", 128, 256, 1, 32)
+            group([(key, R("ones", 0, 32), Z("KC")), (key, Z("cq16"), Z("I16"))]
+                  + [(R("B6", 128 + i, 256, 16, 32), R("dd", i, 512, 16), Z("G8n")) for i in range(1, 16)]
+                  + [(R("B6", 128 + i, 256, 16, 32), R("da", i, 512, 16), Z("G8")) for i in range(1, 16)])
+            scan(R("ks", 0, 128, 1, 32), R("RB", 0, 128, 1, 32), key, 0.0, ALU.add, ALU.min)
+            cp(R("b1", 0, 8, 1, 32), R("ks", 15, 128, 16, 32))
+            ts(R("b2", 0, 8, 1, 32), R("b1", 0, 8, 1, 32), 2047, ALU.bitwise_and)
+            for a in range(2):
+                ma = C("ma%d" % a)
+                ts(R("RR", a, 16, 2, 32), R("b2", 0, 8, 1, 32), R("col", ma[1], ma[2], 1, 32), ALU.mult)
+            group([(R("B6", 0, 2), R("SW", 112 - 16 * k, 240 - 16 * k, 1, 32), R("RR", 2 * k, 2 * k + 2, 1, 32)) for k in range(8)])
+            cp(Z("BL"), R("B6", 0, 2))
+            tt(Z("di"), ind(FBW, Z("BL")), Z("xo"), ALU.subtract)
+            ts(R("ZI", 0, 32), Z("di"), 1, ALU.arith_shift_right)
+            tt(x, ind(Z("ZI"), Z("POS")), x, ALU.add)
+            if t < 3:
+                sx[t] = send("x%d" % t)
+            else:
+                store("Y", T.yx[:], Z("X"), "dyx", 128 * 1024)
+        xt = R("B0", 0, 128)
+        group([(xt, Z("Id"), x)])
+        for h in range(3):
+            at("t%d" % h)
+            take(H("a0", h), ind(x, KL("L0u", h)))
+            tt(H("m0", h), H("a0", h), xt, ALU.max)
+            U = H("B3", h)
+            group([(U, Z("TH"), Z("ones")), (U, Z("BOn"), x), (U, Z("BOn"), H("a0", h)), (U, Z("BOb"), H("m0", h))])
+            tt(U, H("nk", h), U, ALU.max)
+            at("d%d" % h)
+            brows, frows = list(range(1, 16 - NF[h])), list(range(16 - NF[h], 16))
+            mm(D[h], Z("BOx%d" % NF.index(NF[h])), x, False, False)
+            for f0 in range(0, len(frows), 4):
+                rows = frows[f0:f0 + 4]
+                for j, i in enumerate(rows):
+                    group([(H("B4", j), Z("Id"), ra(h, i)), (H("B4", j), Z("Idn"), x)])
+                act(mo(h, rows[0], len(rows)), H("B4", 0, len(rows)), ACT.Abs)
+            for i in brows:
+                tt(mo(h, i), ra(h, i), xt, ALU.max)
+            for i in brows + frows:
+                mm(D[h], Wsl("Wp" if i in brows else "W1", i), mo(h, i), False, i == 15)
+            act(H("sg", h), D[h], ACT.Sign, bias=C("thb"), scale=-1.0)
+        if t < 3:
+            at("q")
+            take(R("F", n0, n0 + 128), x)
+            hops = len([1 for w, c in h1calls if w == "hX%d" % t]) + 1
+            recv(Z("XQ%d" % t), "aXQ%d" % t, sx[t], hops * HOP)
+            compact("B1", "Ww", "XQ%d" % t)
+            cp(Z("QI"), R("B1", 0, 8))
+            ts(Z("QA"), Z("QI"), 1023, ALU.bitwise_and)
+            cp(Z("QL"), Z("QA"))
+        for h in range(3):
+            at("h%d" % h)
+            if h or not t:
+                take(H("cc", h), ind(AW, KL("KL", h)))
+            tt(H("mm", h), H("cc", h), H("B3", h), ALU.is_equal)
+            act(H("em", h), H("cc", h), ACT.Relu, bias=C("emb"))
+            Y = R("B6", 0, 128)
+            old = [(Z("BOa"), H("sg", j)) for j in range(h)] + [(Z("BOb"), H("mm", j)) for j in range(h)]
+            group([(Y, l, r) for l, r in [(Z("Id"), Z("pv2"))] + old
+                   + [(Z("BOa"), H("sg", h)), (Z("TMb"), H("em", h)), (Z("BOb"), H("mm", h))]])
+            act(H("rr", h), Y, ACT.Relu, bias=float(E - n0 - 2048 - 16384 * (h + 1)), scale=-0.5)
+            tt(ind(AS, KL("SL", h)), H("cc", h), H("rr", h), ALU.subtract)
+            at("p%d" % h)
+            Pp = H("B7", h)
+            ta, tb = ("TMa", "TMb") if h < 2 else ("T3a", "T3b")
+            group([(Pp, l, r) for l, r in old + [(Z(ta), H("sg", h)), (Z(tb), H("mm", h))]])
+            act(Pp, Pp, ACT.Relu, bias=C("pb%d" % h), scale=-1.0 / 4096)
+            tt(H("fc", h), H("cc", h), Pp, ALU.mult)
+        if t < 3:
+            at("co")
+            take(Z("CO%d" % t), ind(R("A", 0, 1024), Z("QL")))
+            sq[t] = send("c%d" % t)
+            at("p2")
+            group([(R("B0", 0, 128), Z("BO16"), H("fc", h)) for h in range(3)])
+        else:
+            store("Y", T.yp[:, 0:768], R("A", 0, 768), "dy0", 128 * 768 * 8)
+            store("S", T.yp[:, 768:n0], R("A", 768, n0), "dy1", 128 * 768 * 8)
+        group([(R("B6", 0, 128), Wsl("W16", 0), H("fc", h)) for h in range(3)])
+        tt(R("A", n0, n0 + 128), R("A", n0, n0 + 128), R("B6", 0, 128), ALU.add)
+        if t == 3:
+            store("Y", T.yp[:, n0:E], R("A", n0, E), "dy2", 128 * 512)
+            break
+        tt(Z("w1"), Z("DM"), R("B0", 0, 128), ALU.mult)
+        scan(Z("w2"), Z("RS"), Z("w1"), 0.0, ALU.mult, ALU.add)
+        cp(KL("KL", 0), R("w2", 15, 128, 16))
+        at("ask")
+        Zp = R("B2", 0, 128)
+        group([(Zp, Z("BOa"), H("sg", j)) for j in range(3)] + [(Zp, Z("BOb"), H("mm", j)) for j in range(3)])
+        act(Z("esc"), Zp, ACT.Relu, bias=-23.0, scale=-1.0 / 4096)
+        scan(Z("cnt"), Z("ones"), Z("esc"), 98304.0, ALU.mult, ALU.add)
+        tt(R("B2", 128, 256), Z("cnt"), Zp, ALU.add)
+        tt(Z("v1"), Z("MP"), R("B2", 128, 256), ALU.min)
+        scan(Z("v2"), Z("RS"), Z("v1"), 0.0, ALU.mult, ALU.add)
+        ts(Z("POS"), R("v2", 15, 128, 16), -1.0, ALU.add)
+        cp(ind(Z("SP"), Z("POS")), J128)
+        tt(Z("s1"), R("SP", 0, 32), R("DM", 0, 32), ALU.mult)
+        scan(Z("s2"), R("RS", 0, 32), Z("s1"), 0.0, ALU.mult, ALU.add)
+        cp(Z("INV"), R("s2", 15, 32, 16))
+        take(Z("xz"), ind(x, Z("INV")))
+        for i in range(16):
+            group([(R("B7", i, 512, 16), Z("Id"), Z("xz"))])
+        take(Z("xo"), ind(H("X", t + 1), Z("INV")))
+    return ops, nls
+
+
+def hazards(ops):
+    hist, preds = {}, []
+    for j, o in enumerate(ops):
+        pr = {}
+        for wr, rs in ((False, o["r"]), (True, o["w"])):
+            for r in rs:
+                bank = SCRATCH[r[0]][0] == "psum"
+                for (a, b, i, w2) in hist.get(r[0], []):
+                    if i == j:
+                        continue
+                    hit = a < r[2] and r[1] < b
+                    if bank and ops[i]["e"] != o["e"]:
+                        pr[i] = True
+                    elif (hit and (wr or w2)) or (bank and o["e"] == "P"):
+                        pr[i] = pr.get(i, False) or (hit and w2)
+        for wr, rs in ((False, o["r"]), (True, o["w"])):
+            for r in rs:
+                lst = hist.setdefault(r[0], [])
+                if SCRATCH[r[0]][0] == "psum":
+                    if lst and ops[lst[-1][2]]["e"] != o["e"]:
+                        e0 = ops[lst[-1][2]]["e"]
+                        k = len(lst)
+                        while k > 0 and ops[lst[k - 1][2]]["e"] == e0:
+                            k -= 1
+                        lst[:] = lst[k:]
+                    elif lst and o["e"] == "P":
+                        lst.pop()
+                elif wr and r[3] == 1 and r[4] == 128:
+                    lst[:] = [z for z in lst if not (r[1] <= z[0] and z[1] <= r[2])]
+                lst.append((r[1], r[2], j, wr))
+        preds.append(pr)
+    return preds
+
+
+def kind(o):
+    return (o["w"] or o["r"])[0][0] + (o["r"][0][0] if o["e"] == "P" else "")
+
+
+def schedule(ops, preds):
+    n = len(ops)
+    dep = [list(p.keys()) + ([o["after"]] if o["after"] is not None else []) for p, o in zip(preds, ops)]
+    succ = [[] for _ in range(n)]
+    for j in range(n):
+        for i in dep[j]:
+            succ[i].append(j)
+    prio = [-16000.0 * o["d"][0] - 1000.0 * DUE[o["d"][1]] - 0.01 * j for j, o in enumerate(ops)]
+    eng = ["V" if o.get("key") in ONVK else o["e"] for o in ops]
+    left = [len(d) for d in dep]
+    ready, start = [0.0] * n, [0.0] * n
+    free, order, pool, last = {}, [], {}, 0.0
+    for j in range(n):
+        if left[j] == 0:
+            pool.setdefault(eng[j], []).append(j)
+    while len(order) < n:
+        best = None
+        for e, lst in pool.items():
+            if not lst:
+                continue
+            f = 0.0 if e == "N" else free.get(e, 0.0)
+            t0 = max(f, min(ready[j] for j in lst)) + LOOK
+            j = max([k for k in lst if ready[k] <= t0], key=lambda k: prio[k])
+            t0 = max(f, ready[j])
+            if best is None or t0 < best[0]:
+                best = (t0, j, e)
+        t0, j, e = best
+        pool[e].remove(j)
+        order.append(j)
+        start[j] = t0
+        free[e] = t0 + (ops[j]["alt"][e][1] if "alt" in ops[j] else ops[j]["c"])
+        end = free[e] + ops[j]["lat"]
+        last = max(last, end)
+        for k in succ[j]:
+            ready[k] = max(ready[k], end + (0.0 if (e == eng[k] == "P" or eng[k] == "N") else SYNC))
+            left[k] -= 1
+            if left[k] == 0:
+                pool.setdefault(eng[k], []).append(k)
+    return order, eng, start, last
+
+
+def emit(g, T, ops, preds, order, nls):
+    queue = {"V": g.vector, "S": g.scalar, "P": g.tensor, "G": g, "Y": g.sync}
+    pos, cnt = {}, {}
+    at = {j: k for k, j in enumerate(order)}
+    for j in order:
+        e = ops[j]["e"]
+        cnt[e] = cnt.get(e, 0) + 1
+        pos[j] = cnt[e]
+    known, clock, waits, target = {}, {}, {}, set()
+    for j in order:
+        o = ops[j]
+        e = o["e"]
+        if e == "N":
+            clock[j] = {}
+            continue
+        kn = known.setdefault(e, {})
+        need = {}
+        for i, raw in preds[j].items():
+            p = ops[i]
+            if p["sem"] is not None:
+                key, val = p["sem"][0], 1
+            elif p["e"] == "G" and not p["w"]:
+                continue
+            else:
+                if p["e"] == e and (e == "P" or not (raw or SAME_WAR)):
+                    continue
+                key, val = p["e"], pos[i]
+            if key not in need or val > need[key][0]:
+                need[key] = (val, i)
+        ws = []
+        for key, (val, i) in sorted(need.items(), key=lambda z: -at[z[1][1]]):
+            if kn.get(key, 0) >= val:
+                continue
+            ws.append(i)
+            target.add(i)
+            kn[key] = val
+            for k2, v2 in clock[i].items():
+                kn[k2] = max(kn.get(k2, 0), v2)
+        waits[j] = ws
+        clock[j] = dict(kn)
+    count, total = {}, {}
+    for j in order:
+        o = ops[j]
+        if o["sem"] is not None:
+            total[o["sem"][0]] = o["sem"][1]
+        elif j in target:
+            s = ESEM[o["e"]]
+            total[s] = total.get(s, 0) + 1
+            count[j] = total[s]
+    for j in order:
+        o = ops[j]
+        if o["e"] == "N":
+            continue
+        q = queue[o["e"]]
+        for i in waits[j]:
+            p = ops[i]
+            if p["sem"] is not None:
+                q.wait_ge(T.sem[p["sem"][0]], p["sem"][1])
+            else:
+                q.wait_ge(T.sem[ESEM[p["e"]]], count[i])
+        ins = o["f"]()
+        if o["sem"] is not None:
+            ins.then_inc(T.sem[o["sem"][0]], o["sem"][1])
+        elif j in target:
+            ins.then_inc(T.sem[ESEM[o["e"]]], 1)
+    g.wait_ge(T.sem["ls"], nls[0])
+    for s, v in total.items():
+        g.wait_ge(T.sem[s], v)
+
+
+def rank_program(g, core, T, topo):
+    rank = T.rank_of(core)
+    if rank is None:
+        for r in range(len(T.cores)):
+            if core not in topo.cores_of(T.cores[r]):
+                continue
+            me, calls, h1, h1calls, hb, hbcalls = plan(T, topo, r)
+            mine = h1calls if core == h1 else hbcalls if core == hb else []
+            if mine:
+                arr, seen, n = arrivals(T, topo, core), [], 0
+                for w, c in mine:
+                    if w not in seen:
+                        g.wait_ge(T.sem[w], arr[w])
+                        seen.append(w)
+                    n += remote_call(g, T, topo, core, c)
+                g.wait_ge(T.sem["ls"], n)
+        return
+    ops, nls = build(g, T, topo, rank)
+    preds = hazards(ops)
+    if "o" not in _ORDER:
+        _ORDER["o"] = schedule(ops, preds)
+    order, eng = _ORDER["o"][:2]
+    for o, e in zip(ops, eng):
+        if "alt" in o:
+            o["e"], o["f"] = e, o["alt"][e][0]
+    emit(g, T, ops, preds, order, nls)

@@ -4,18 +4,15 @@ from concourse.mybir import AluOpType, ActivationFunctionType
 ALU = AluOpType
 ACT = ActivationFunctionType
 M, P, NT, E = 1152, 128, 4, 1664
-NF = [2, 2, 2]
-CHH = [512, 512, 256]
-ONVK = {(0, 'dd', 0), (0, 'nk', 0), (0, 'nk', 128), (0, 'ra', 4864), (0, 'ra', 5632), (0, 'xz', 0), (1, 'F', 0), (1, 'dd', 0),
-        (1, 'ra', 0), (1, 'ra', 3584), (1, 'ra', 4608), (1, 'ra', 5120), (1, 'xz', 0), (2, 'F', 0), (2, 'dd', 0), (2, 'ra', 3072),
-        (2, 'ra', 3584), (2, 'ra', 5120), (2, 'ra', 5888), (2, 'xz', 0), (3, 'F', 0), (3, 'a0', 256), (3, 'dd', 0), (3, 'nk', 128),
-        (3, 'ra', 3072), (3, 'ra', 4096), (3, 'ra', 5888), (3, 'xz', 0)}
-DUE = {'c0': -5.5, 'c1': -0.9, 'c2': 6.4, 'cu0': -21.55, 'raw0': -7.95, 'cu1': -3.55, 'raw1': -6.65, 'cu2': -5.4, 'raw2': -0.15,
-       'sl': -5.15, 'nk0': -11.55, 'nk1': 23.9, 'nk2': 13.9, 'wn0': 1.35, 'wn1': -10.85, 'wn2': 6.05, 'ans': -18.3, 't0': -2.6,
-       'd0': -23.1, 'h0': 2.35, 'p0': 5.3, 't1': -3.75, 'd1': -0.15, 'h1': 0.55, 'p1': -1.7, 't2': 4.4, 'd2': 4.75, 'h2': -1.55,
-       'q': 4.75, 'p2': 5.65, 'co': -3.8, 'ask': 6.75}
-CYC, GATH, SCAT, PEC, SYNC, HOP, BW, LOOK = 1.04, 1.62, 4.0, 0.52, 90.0, 2500.0, 150.0, 40.0
-SAME_WAR = False
+XW = 160
+NF = [7, 6, 7]
+CHH = [256, 256, 256]
+FIG = {"cyc": 1.04, "gath": 1.62, "scat": 4.0, "pe": 0.52, "sync": 90.0, "hop": 2500.0, "dma": 2000.0, "bw": 200.0, "send": 400.0}
+LOOK, HOLD, PEN, SLACK, AHEAD, DEPTH = 40.0, 2.0, 3000.0, 1000.0, 8, 4
+BOOST = {'p0': 1500, 'p1': 1750, 'p2': 2250, 'link': 5500, 'cu0': 4500, 't1': 250, 'd1': 500, 'h0': -250, 'c': 250, 'sl': -250,
+         'q': 500, 'wn0': -2000, 'ask': -500, 'co': -2500, 'wn1': -750, 'cu1': 250, 'cu2': -1000, 'wn2': 500, 'd0': -250,
+         't0': 250, 't2': -250}
+SAME_WAR = True
 
 F32, BF, I32, U16, F16 = "float32", "bfloat16", "int32", "uint16", "float16"
 SCRATCH = {}
@@ -27,44 +24,43 @@ def _decl(names, cols, dtype, where="sbuf"):
 
 
 _decl("A", 1800, F32)
-_decl("P32", 1672, I32)
+_decl("P32", M, I32)
 _decl("F FB0 FB1 FB2", 1680, BF)
 _decl("FX", 1280, BF)
-_decl("X dd da", 512, BF)
-_decl("XQ0 XQ1 XQ2 ones esc", 128, BF)
-_decl("CQ0 CQ1 CQ2 CO0 CO1 CO2", 128, F32)
+_decl("X", 4 * XW, BF)
+_decl("dd da", 512, BF)
+_decl("XQ0 XQ1 XQ2", 128, BF)
+_decl("ones esc cnt junk J", XW, BF)
+_decl("CQ0 CQ1 CQ2", XW, F32)
+_decl("CO0 CO1 CO2 R1V tB c1", 128, F32)
 _decl("hwi thi pi pj", 4, I32)
-_decl("col s1 s2", 32, F32)
+_decl("col RB ks", 32, F32)
 _decl("NV", 640, F32)
-_decl("J", 240, F32)
-_decl("J16 DM MP RB RS R1V tA tB cnt v1 v2 w1 w2 ks", 128, F32)
-_decl("Id Idn BO BOa BOb BOn BOx0 BOx1 BOx2 T1 T2 TM TM3 TMa TMb T3a T3b TH KC pv2 msk", 128, BF)
+_decl("J16 Id Idn IdB IdA0 IdA1 IdA2 IdA3 CUd BO BOn BO2 BOx0 BOx1 BOx2 Q T3 T3n pv", 128, BF)
+_decl("THd", 256, BF)
 _decl("W1 Wp Wn Ww", 144, BF)
-_decl("G8 G8n", 8, BF)
-_decl("I16 BO16 c16", 128, F16)
+_decl("I32h c16", 128, F16)
 _decl("E0w W16", 144, F16)
-_decl("SW", 240, F16)
+_decl("KC", 32, F16)
 _decl("PC DUM nq tq", 24, F32)
 _decl("KI L0", 24, I32)
 _decl("KL L0u SL", 24, U16)
 _decl("QI QA b1 b2", 8, I32)
-_decl("QL POS", 8, U16)
+_decl("QL INV BL", 8, U16)
+_decl("acc", 8, F32)
 _decl("CU", 384, U16)
 _decl("raw mx", 6144, BF)
-_decl("nk cc rr", 384, F32)
-_decl("a0 m0 sg mm em", 384, BF)
+_decl("cc rr", 384, F32)
+_decl("a0 m0 mm em", 384, BF)
+_decl("sg", 768, BF)
 _decl("fc", 384, F16)
-_decl("SP", 256, F32)
-_decl("ZI", 256, I32)
 _decl("cqu", 32, U16)
-_decl("INV BL", 2, U16)
-_decl("xo xz", 32, BF)
-_decl("cq16", 32, F16)
-_decl("RR", 16, F16)
+_decl("xo xz JM", 32, BF)
 _decl("di", 32, I32)
 _decl("B0 B1 B2 B3 B4 B5 B6 B7", 512, F32, "psum")
 
-SEMAPHORES = ["sV", "sS", "sP", "sG", "ls", "dptr", "dp0", "dfr", "dnw", "dhw", "dth", "dyx", "dy0", "dy1", "dy2",
+SEMAPHORES = ["sV", "sS", "sP", "sG", "ls", "dp0", "dp1", "dp2", "dfr", "dn0", "dn1", "dn2", "dn3", "dhw", "dth",
+              "dx0", "dx1", "dx2", "dx3", "dy0", "dy1", "dy2",
               "aXQ0", "aXQ1", "aXQ2", "aCQ0", "aCQ1", "aCQ2", "aFB0", "aFB1", "aFB2",
               "hX0", "hX1", "hX2", "hC0", "hC1", "hC2", "hB"]
 ESEM = {"V": "sV", "S": "sS", "P": "sP", "G": "sG"}
@@ -72,8 +68,8 @@ WIDTH = {F32: 4, I32: 4, BF: 2, U16: 2, F16: 2}
 _ORDER = {}
 
 
-def R(name, a, b, step=1, p=128):
-    return (name, a, b, step, p)
+def R(name, a, b, step=1):
+    return (name, a, b, step)
 
 
 def ncol(r):
@@ -123,7 +119,7 @@ def plan(T, topo, r):
     calls["bulk"] = [(R("F", 0, M), hb, R("FX", 0, M), "hB")]
     hbcalls = [("hB", [(R("FX", 0, 1280), dn[t], R("FB%d" % t, 0, 1280), "aFB%d" % t)]) for t in range(3)]
     for s in range(3):
-        src, mid = R("X", 128 * s, 128 * s + 128), R("XQ%d" % s, 0, 128)
+        src, mid = R("X", XW * s, XW * s + 128), R("XQ%d" % s, 0, 128)
         want = [(up[s], mid, "aXQ%d" % s)]
         if s > 0:
             want += [(dn[t], R("FB%d" % t, M + 128 * s, M + 128 * s + 128), "aFB%d" % t) for t in range(s, 3)]
@@ -158,8 +154,8 @@ def arrivals(T, topo, core):
 
 def ap_of(T, r):
     if r[3] == 1:
-        return T[r[0]][0:r[4], r[1]:r[2]]
-    return T[r[0]][0:r[4], r[1]:r[2]:r[3]]
+        return T[r[0]][:, r[1]:r[2]]
+    return T[r[0]][:, r[1]:r[2]:r[3]]
 
 
 def remote_call(g, T, topo, src, c):
@@ -177,9 +173,13 @@ def remote_call(g, T, topo, src, c):
     return sum(len(e) for e in en)
 
 
+def price(c, fig):
+    return c[0] + c[1] * fig[c[2]]
+
+
 def build(g, T, topo, rank):
     ops = []
-    due, step, nls, cn = [(0, "c0")], [0], [0], {}
+    tag, nls, cn, groups, loaded = [(0, "c")], [0], {}, [0], [0]
     me, calls, h1, h1calls, hb, hbcalls = plan(T, topo, rank)
     arr = arrivals(T, topo, me)
 
@@ -198,30 +198,31 @@ def build(g, T, topo, rank):
                 out += [x[1], x[2]] if x[0] == "ind" else [x]
         return out
 
-    def add(eng, emit, rd, out, cost, sem=None, lat=0.0, after=None):
-        wr = []
+    def add(eng, emit, rd, out, cost, sem=None, lat=(0, 0, "hop"), after=[], more=(), grp=None):
+        wr = list(more)
         if out is not None:
             if out[0] == "ind":
-                wr, rd = [out[1]], rd + [out[2]]
+                wr, rd = wr + [out[1]], rd + [out[2]]
             else:
-                wr = [out]
-        ops.append({"e": eng, "f": emit, "r": rd, "w": wr, "c": cost, "sem": sem, "lat": lat, "after": after, "d": due[0]})
+                wr = wr + [out]
+        ops.append({"e": eng, "alt": {eng: (emit, cost)}, "r": rd, "w": wr, "sem": sem, "lat": lat, "after": after,
+                    "d": tag[0], "grp": grp, "stop": False})
         return len(ops) - 1
 
-    def at(d):
-        due[0] = (step[0], d)
+    def at(t, d):
+        tag[0] = (t, d)
 
     def vcost(out, ins, two=False):
         if out[0] == "ind":
-            return 50 + SCAT * 16 * ncol(out[2])
+            return (50, 16 * ncol(out[2]), "scat")
         if ins[0][0] == "ind":
-            return 50 + GATH * ncol(out)
+            return (50, ncol(out), "gath")
         k = 1.0
         if two:
             k = 1.0 if any(SCRATCH[x[0]][0] == "psum" for x in ins) else 2.0
         elif all(WIDTH[SCRATCH[x[0]][2]] == 2 for x in ins + [out]):
             k = 0.5
-        return CYC * max(64, k * ncol(out))
+        return (0, max(64, k * ncol(out)), "cyc")
 
     def ind(w, o):
         return ("ind", w, o)
@@ -246,43 +247,66 @@ def build(g, T, topo, rank):
     def fill(out, val):
         add("V", lambda: g.vector.memset(ap(out), val), [], out, vcost(out, [out]))
 
-    def act(out, i, func, bias=0.0, scale=1.0):
-        c = 65 + GATH * ncol(out) if i[0] == "ind" else CYC * max(64, ncol(out))
-        if func == ACT.Copy and scale == 1.0:
+    def act(out, i, func, bias=0.0, scale=1.0, acc=None):
+        c = (65, ncol(out), "gath") if i[0] == "ind" else (20 if acc else 0, max(64, ncol(out)), "cyc")
+        if acc:
+            f = lambda: g.scalar.activation(ap(out), ap(i), func, bias=sc(bias), scale=sc(scale), accum_out=ap(acc))
+        elif func == ACT.Copy and scale == 1.0:
             f = lambda: g.scalar.activation(ap(out), ap(i), func)
         else:
             f = lambda: g.scalar.activation(ap(out), ap(i), func, bias=sc(bias), scale=sc(scale))
-        add("S", f, regs(i, bias, scale), out, c)
+        add("S", f, regs(i, bias, scale), out, c, more=[acc] if acc else [])
+
+    def either():
+        s = ops.pop()
+        ops[-1]["alt"].update(s["alt"])
 
     def take(out, i):
         cp(out, i)
-        v = ops.pop()
         act(out, i, ACT.Copy)
-        ops[-1]["key"] = (step[0], out[0][:2], out[1] % 128 if out[0] == "F" else out[1])
-        ops[-1]["alt"] = {"S": (ops[-1]["f"], ops[-1]["c"]), "V": (v["f"], v["c"])}
+        either()
 
-    def mm(out, l, r, start, stop):
-        add("P", lambda: g.tensor.matmul(ap(out), ap(l), ap(r), start, stop), regs(l, r), out,
-            PEC * max(min(64, ncol(l)), ncol(r)))
+    def scaled(out, i, s):
+        ts(out, i, s, ALU.mult)
+        act(out, i, ACT.Copy, scale=s)
+        either()
+
+    def mm(gid, out, l, r):
+        first = gid == groups[0]
+        if first:
+            groups[0] += 1
+        j = len(ops)
+        add("P", lambda: g.tensor.matmul(ap(out), ap(l), ap(r), first, ops[j]["stop"]), regs(l, r), out,
+            (0, max(min(64, ncol(l)), ncol(r)), "pe"), grp=gid)
 
     def group(terms):
-        for j, (o, l, r) in enumerate(terms):
-            mm(o, l, r, j == 0, j == len(terms) - 1)
+        gid = groups[0]
+        for o, l, r in terms:
+            mm(gid, o, l, r)
+        return gid
 
-    def iota(out, pat, base, cm):
+    def iota(out, pat, base, cm=0):
         if SCRATCH[out[0]][2] == I32:
             f = lambda: g.iota(ap(out), pat, base, cm)
         else:
             f = lambda: g.iota(ap(out), pat, base, cm, allow_small_or_imprecise_dtypes=True)
-        add("G", f, [], out, 160 + 2 * CYC * ncol(out))
+        add("G", f, [], out, (160, 2 * ncol(out), "cyc"))
 
-    def load(q, out, src, sem, nbytes):
+    def gfill(out, val):
+        iota(out, [[0, ncol(out)]], val)
+
+    def keep(out, i, pat, op, val, base, cm):
+        add("G", lambda: g.affine_select(ap(out), ap(i), pat, op, val, base, cm), [i], out, (200, 2 * ncol(out), "cyc"))
+
+    def load(q, out, src, sem):
         qq = g.sync if q == "Y" else g.scalar
-        add(q, lambda: qq.dma_start(ap(out), src), [], out, 60, sem=(sem, 16), lat=2000 + nbytes / BW)
+        loaded[0] += 128 * ncol(out) * WIDTH[SCRATCH[out[0]][2]]
+        add(q, lambda: qq.dma_start(ap(out), src), [], out, (60, 0, "cyc"), sem=(sem, 16),
+            lat=(loaded[0] / FIG["bw"], 1, "dma"))
 
     def store(q, dst, i, sem, nbytes):
         qq = g.sync if q == "Y" else g.scalar
-        add(q, lambda: qq.dma_start(dst, ap(i)), [i], None, 60, sem=(sem, 16), lat=2000 + nbytes / BW)
+        add(q, lambda: qq.dma_start(dst, ap(i)), [i], None, (60, 0, "cyc"), sem=(sem, 16), lat=(nbytes / FIG["bw"], 1, "dma"))
 
     def send(key):
         c = calls[key]
@@ -290,10 +314,10 @@ def build(g, T, topo, rank):
         def f():
             nls[0] += remote_call(g, T, topo, me, c)
             return None
-        return add("G", f, [c[0][0]], None, 400)
+        return add("G", f, [c[0][0]], None, (0, 1, "send"))
 
-    def recv(out, sem, after, lat):
-        add("N", None, [], out, 0, sem=(sem, arr[sem]), lat=lat, after=after)
+    def recv(out, sem, after, hops):
+        add("N", None, [], out, (0, 0, "cyc"), sem=(sem, arr[sem]), lat=(0, hops, "hop"), after=after)
 
     def C(name):
         if name not in cn:
@@ -312,103 +336,98 @@ def build(g, T, topo, rank):
     def KL(name, h):
         return R(name, 8 * h, 8 * h + 8)
 
+    def Xt(t, n=128):
+        return R("X", XW * t, XW * t + n)
+
+    def G8(name):
+        return R(name, 0, 128, 16)
+
     def compact(bank, wide, src):
         group([(R(bank, 0, 8), Wsl(wide, b), R(src, b, 128, 16)) for b in range(16)])
 
-    load("Y", R("P32", 1024, M), T.ptr[:, 1024:M], "dp0", 128 * 512)
-    load("Y", R("P32", 0, 1024), T.ptr[:, 0:1024], "dptr", 128 * 4096)
-    load("S", R("F", 0, M), T.fr[:], "dfr", 128 * M * 2)
-    load("Y", Z("X"), T.nw[:], "dnw", 128 * 1024)
-    load("Y", R("thi", 0, 1), T.th[:], "dth", 8192)
-    load("Y", R("hwi", 0, 1), T.hw[:], "dhw", 8192)
+    load("Y", R("P32", 1024, M), T.ptr[:, 1024:M], "dp0")
+    load("S", R("P32", 0, 512), T.ptr[:, 0:512], "dp1")
+    load("Y", R("P32", 512, 1024), T.ptr[:, 512:1024], "dp2")
+    load("S", R("F", 0, M), T.fr[:], "dfr")
+    load("Y", Xt(0), T.nw[:, 0:128], "dn0")
+    load("Y", R("thi", 0, 1), T.th[:], "dth")
+    load("Y", R("hwi", 0, 1), T.hw[:], "dhw")
+    for t in range(1, NT):
+        load("Y", Xt(t), T.nw[:, 128 * t:128 * t + 128], "dn%d" % t)
+    store("Y", T.yx[:, 0:128], Xt(0), "dx0", 0)
+    J128, one = R("J", 0, 128), R("ones", 0, 128)
     iota(R("pi", 0, 1), [[0, 1]], 0, 1)
-    iota(Z("J"), [[1, 240]], 0, 0)
-    iota(Z("J16"), [[16, 8], [0, 16]], 0, 0)
-    iota(Z("NV"), [[1, 640]], M, 0)
-    iota(Z("tq"), [[0, 3], [16, 8]], 0, 0)
+    iota(Z("J"), [[1, XW]], 0)
+    iota(Z("J16"), [[16, 8], [0, 16]], 0)
+    iota(Z("JM"), [[0, 2], [1, 16]], 0)
+    iota(Z("NV"), [[1, 640]], M)
+    iota(Z("tq"), [[0, 3], [16, 8]], 0)
+    gfill(R("F", M, 1680), 99)
+    for t in range(NT):
+        gfill(R("X", XW * t + 128, XW * t + XW), 0)
+    for t in range(3):
+        gfill(R("FB%d" % t, M + 128 * (t + 1), 1680), 99)
+        gfill(R("CQ%d" % t, 128, XW), 0)
     cp(C("p"), R("pi", 0, 1))
     ts(R("pj", 0, 1), R("pi", 0, 1), 15, ALU.bitwise_and)
     cp(C("i"), R("pj", 0, 1))
     tt(C("g16"), C("p"), C("i"), ALU.subtract)
-    ts(C("g15"), C("g16"), 15.0, ALU.add)
     ts(C("r0"), C("i"), 0.0, ALU.is_equal)
     ts(C("r1"), C("i"), 1.0, ALU.is_equal)
     ts(C("nr1"), C("i"), 1.0, ALU.not_equal)
-    ts(Z("W1"), R("J", 0, 144), C("g15"), ALU.is_equal)
+    ts(Z("W1"), R("J", 0, 144), C("g16"), ALU.subtract, 15.0, ALU.is_equal)
     ts(Z("E0w"), Z("W1"), C("r0"), ALU.mult)
-    fill(R("F", M, 1680), 99.0)
     ts(C("lo"), C("i"), 2.0, ALU.is_ge, float(E), ALU.mult)
     ts(C("hi"), C("i"), 1.0, ALU.is_ge, float(E), ALU.mult)
     ts(R("A", M, E), R("NV", 128, 640), C("lo"), ALU.max, C("hi"), ALU.min)
-    ts(R("A", E, E + 1), C("r0"), float(E - 1), ALU.add)
-    fill(R("A", E + 1, 1800), 0.0)
+    fill(R("A", E, 1800), float(E))
     ts(Z("R1V"), R("NV", 0, 128), C("r1"), ALU.mult)
-    ts(Z("c16"), R("P32", 1024, M), 1.0, ALU.mult)
-    cp(R("A", 0, 1024), R("P32", 0, 1024))
+    cp(Z("c16"), R("P32", 1024, M))
+    cp(R("A", 0, 512), R("P32", 0, 512))
+    cp(R("A", 512, 1024), R("P32", 512, 1024))
     ts(Z("tB"), R("P32", 1024, M), C("nr1"), ALU.mult)
-    tt(R("P32", 1024, M), Z("tB"), Z("R1V"), ALU.max)
-    cp(R("A", 1024, M), R("P32", 1024, M))
-    fill(R("P32", M, E), 0)
-    ts(R("P32", E, E + 1), C("r0"), float(E - 1), ALU.add)
-    J128 = R("J", 0, 128)
-    at("c1")
+    tt(R("A", 1024, M), Z("tB"), Z("R1V"), ALU.max)
     ts(Z("Id"), J128, C("p"), ALU.is_equal)
     ts(Z("BO"), Z("J16"), C("g16"), ALU.is_equal)
-    ts(Z("T1"), J128, C("p"), ALU.is_gt)
-    tt(Z("T2"), Z("T1"), Z("Id"), ALU.subtract)
-    tt(Z("TM"), Z("T2"), Z("BO"), ALU.mult)
-    tt(Z("TM3"), Z("TM"), Wsl("W1", 0), ALU.add)
-    for o, i, s in (("Wn", "W1", -1.0), ("Wp", "W1", 2.0), ("Idn", "Id", -1.0), ("BOa", "BO", 2048.0),
-                    ("BOb", "BO", 4096.0), ("BOn", "BO", -2048.0), ("TMa", "TM", 2048.0), ("TMb", "TM", 4096.0),
-                    ("T3a", "TM3", 2048.0), ("T3b", "TM3", 4096.0)):
-        act(Z(o), Z(i), ACT.Copy, scale=s)
-    act(Z("pv2"), J128, ACT.Copy, scale=2.0)
-    tt(Z("tA"), J128, Z("J16"), ALU.subtract)
-    ts(Z("DM"), Z("tA"), C("i"), ALU.is_equal)
-    ts(Z("RS"), Z("tA"), 0.0, ALU.not_equal)
-    ts(Z("RB"), Z("tA"), 0.0, ALU.is_equal, float(2 ** 26), ALU.mult)
+    for o, i, s in (("BOn", "BO", -1.0), ("BO2", "BO", 2.0), ("Idn", "Id", -1.0), ("IdB", "Id", -1024.0),
+                    ("Wp", "W1", 2048.0), ("Wn", "W1", -1024.0)):
+        scaled(Z(o), Z(i), s)
+    for t in range(NT):
+        scaled(Z("IdA%d" % t), Z("Id"), -64.0 * (NT - t))
+    scaled(Z("pv"), J128, 1.0 / 2048)
+    keep(Z("T3"), Z("BO"), [[1, 128]], ALU.is_gt, 0.0, 0, -1)
+    keep(Z("T3"), Z("T3"), [[1, 128]], ALU.not_equal, -1.0, 0, -1)
+    cp(G8("T3"), G8("BO"))
+    scaled(Z("T3n"), Z("T3"), -1.0)
+    keep(Z("Q"), Z("BOn"), [[-1, 128]], ALU.is_gt, 0.0, 0, 1)
+    keep(Z("Q"), Z("Q"), [[-1, 128]], ALU.not_equal, -2.0, 0, 1)
     for n in sorted(set(NF)):
-        ts(Z("msk"), Z("tA"), float(15 - n), ALU.is_le, -1.0, ALU.mult)
-        tt(Z("BOx%d" % NF.index(n)), Z("msk"), Z("BO"), ALU.mult)
-    at("c2")
-    ts(Z("v1"), J128, 129.0, ALU.add)
-    tt(Z("MP"), Z("v1"), Z("DM"), ALU.mult)
-    cp(Z("I16"), Z("Id"))
-    cp(Z("BO16"), Z("BO"))
+        keep(Z("BOx%d" % NF.index(n)), Z("BOn"), [[0, 8], [-1, 16]], ALU.is_ge, 0.0, 15 - n, 0)
+    ts(Z("RB"), Z("JM"), 0.0, ALU.is_equal, float(2 ** 23), ALU.mult)
+    ts(Z("KC"), R("J", 0, 32), 1.0 / 32, ALU.mult, C("i"), ALU.add)
+    ts(R("KC", 0, 32, 16), R("J", 0, 2), 0.0, ALU.mult, 60000.0, ALU.add)
+    ts(Z("I32h"), Z("Id"), 32.0, ALU.mult)
     cp(Z("W16"), Z("W1"))
-    ts(C("i112"), C("i"), 112.0, ALU.add)
-    ts(Z("SW"), Z("J"), C("i112"), ALU.is_equal)
-    act(Z("G8"), R("BO", 0, 128, 16), ACT.Copy, scale=65536.0)
-    act(Z("G8n"), R("BO", 0, 128, 16), ACT.Copy, scale=-32768.0)
-    ts(C("kc0"), C("r0"), float(2 ** 15), ALU.mult, C("i"), ALU.add)
-    ts(Z("KC"), Z("Id"), C("kc0"), ALU.mult, 2048.0, ALU.mult)
-    ts(C("ma0"), C("p"), 16.0, ALU.is_lt)
-    ts(C("ma1"), C("p"), 16.0, ALU.is_ge)
     fill(Z("ones"), 1.0)
-    fill(Z("SP"), 0.0)
-    fill(Z("ZI"), 0)
-    for t in range(3):
-        fill(R("FB%d" % t, M + 128 * (t + 1), 1680), 99.0)
-    at("c1")
+    fill(R("esc", 128, XW), 1.0)
     ts(Z("PC"), Z("tq"), C("i"), ALU.add)
-    ts(Z("DUM"), Z("PC"), float(E + 1), ALU.add)
+    ts(Z("DUM"), Z("PC"), float(E + 2), ALU.add)
     ts(C("emb"), C("r0"), -8192.0, ALU.mult, float(1 - E), ALU.add)
-    ts(C("pb0"), C("i"), -0.5, ALU.mult, 0.5, ALU.add)
-    ts(C("pb1"), C("pb0"), -8.0, ALU.add)
-    ts(C("pbx"), C("r0"), -7.0, ALU.mult, -16.0, ALU.add)
-    tt(C("pb2"), C("pbx"), C("pb0"), ALU.add)
+    ts(C("cu"), C("r0"), 8192.0, ALU.mult, 640.0, ALU.add)
+    ts(Z("CUd"), Z("Id"), C("cu"), ALU.mult)
+    for a in range(2):
+        ts(C("s%d" % a), C("i"), 16 * a + 0.5, ALU.add)
     cp(C("th"), R("thi", 0, 1))
     cp(C("w"), R("hwi", 0, 1))
-    ts(C("hb"), C("r0"), -1024.0, ALU.mult, 0.5, ALU.add)
-    tt(C("thb"), C("th"), C("hb"), ALU.add)
-    ts(Z("TH"), Z("Id"), C("th"), ALU.mult, -2048.0, ALU.mult)
+    for a in range(2):
+        ts(H("THd", a), Z("Idn"), C("th"), ALU.mult)
     ts(Z("Ww"), Z("W1"), C("w"), ALU.mult)
-    at("c0")
-    send("bulk")
+    bulk = send("bulk")
     sx = {0: send("x0")}
     sq = {}
-    AW, AS, FW = R("A", 0, E + 1), R("A", 0, E + 129), R("F", 0, E + 1)
-    D = [R("B1", 0, 128), R("B2", 0, 128), R("B5", 0, 128)]
+    AW, AS, FW = R("A", 0, E + 1), R("A", 0, E + 130), R("F", 0, E + 1)
+    bank = ["B1", "B2", "B3"]
+    stage = [0]
 
     def ra(h, i):
         return R("raw", 2048 * h + i, 2048 * (h + 1), 16)
@@ -416,249 +435,280 @@ def build(g, T, topo, rank):
     def mo(h, i, n=1):
         return R("mx", 2048 * h + 128 * i, 2048 * h + 128 * (i + n))
 
-    compact("B4", "E0w", "c16")
-    cp(KL("KL", 0), R("B4", 0, 8))
+    compact("B7", "E0w", "c16")
+    cp(KL("KL", 0), R("B7", 0, 8))
     for t in range(NT):
         n0 = M + 128 * t
-        step[0] = t
-        x = H("X", t)
+        x, IdA = Xt(t), Z("IdA%d" % t)
         for h in range(3):
-            at("cu%d" % h)
-            first = ind(AW if t else R("P32", 0, E + 1), KL("KL", h))
-            if t and not h:
-                cp(H("cc", 0), first)
-                first = H("cc", 0)
-            cp(H("CU", h), first)
+            at(t, "cu%d" % h)
             if h < 2:
+                first = H("cc", 0) if h == 0 else Z("c1")
+                take(first, ind(AW, KL("KL", h)))
+                cp(H("CU", h), first)
                 cp(Z("c16"), first)
-                compact("B4", "E0w", "c16")
-                cp(KL("KL", h + 1), R("B4", 0, 8))
-            at("raw%d" % h)
+                compact("B7", "E0w", "c16")
+                cp(KL("KL", h + 1), R("B7", 0, 8))
+            else:
+                cp(H("CU", h), ind(AW, KL("KL", h)))
+            at(t, "raw%d" % h)
             ch = CHH[h]
             for c in range(2048 // ch):
                 take(R("raw", 2048 * h + ch * c, 2048 * h + ch * (c + 1)),
                      ind(FW, R("CU", 128 * h + ch // 16 * c, 128 * h + ch // 16 * (c + 1))))
-        at("sl")
-        cp(Z("KI"), Z("KL"))
+        at(t, "sl")
+        ts(Z("KI"), Z("KL"), 1.0 + 1.0 / 3200, ALU.mult)
         ts(Z("L0"), Z("KI"), 127, ALU.bitwise_and)
         cp(Z("L0u"), Z("L0"))
         tt(Z("nq"), Z("L0"), Z("PC"), ALU.not_equal)
         tt(Z("tq"), Z("nq"), Z("DUM"), ALU.mult)
         tt(Z("nq"), Z("tq"), Z("KI"), ALU.max)
         cp(Z("SL"), Z("nq"))
+        dg = []
         for h in range(3):
-            at("nk%d" % h)
-            take(H("nk", h), ind(H("NV", t), KL("L0u", h)))
-        for h in range(3):
-            at("wn%d" % h)
-            for i in range(1, 16 - NF[h]):
-                mm(D[h], Wsl("Wn", i), ra(h, i), i == 1, False)
+            at(t, "wn%d" % h)
+            dg.append(group([(R(bank[h], 0, 256), one, Z("THd"))]
+                            + [(R(bank[h], i, 128, 16), ra(h, i), G8("BOn")) for i in range(1, 16 - NF[h])]))
         if t > 0:
             s = t - 1
-            at("ans")
+            at(t, "ans")
             fb = "FB%d" % s
             FBW = R(fb, 0, E + 1)
             hops = len([1 for w, c in h1calls if w == "hC%d" % s]) + 1
-            recv(R(fb, 0, M + 128 * t), "aFB%d" % s, sx[s], 2 * HOP)
-            recv(Z("CQ%d" % s), "aCQ%d" % s, sq[s], hops * HOP)
-            cp(Z("cqu"), ind(Z("CQ%d" % s), Z("INV")))
-            for c in range(2):
-                take(R("dd", 256 * c, 256 * c + 256), ind(FBW, R("cqu", 16 * c, 16 * c + 16)))
-            for c in range(2):
-                tt(R("da", 256 * c, 256 * c + 256), R("dd", 256 * c, 256 * c + 256), R("B7", 256 * c, 256 * c + 256), ALU.max)
-            cp(Z("cq16"), ind(Z("CQ%d" % s), Z("INV")))
-            key = R("B6", 128, 256, 1, 32)
-            group([(key, R("ones", 0, 32), Z("KC")), (key, Z("cq16"), Z("I16"))]
-                  + [(R("B6", 128 + i, 256, 16, 32), R("dd", i, 512, 16), Z("G8n")) for i in range(1, 16)]
-                  + [(R("B6", 128 + i, 256, 16, 32), R("da", i, 512, 16), Z("G8")) for i in range(1, 16)])
-            scan(R("ks", 0, 128, 1, 32), R("RB", 0, 128, 1, 32), key, 0.0, ALU.add, ALU.min)
-            cp(R("b1", 0, 8, 1, 32), R("ks", 15, 128, 16, 32))
-            ts(R("b2", 0, 8, 1, 32), R("b1", 0, 8, 1, 32), 2047, ALU.bitwise_and)
+            recv(R(fb, 0, M + 128 * t), "aFB%d" % s, [sx[s]] if s else [sx[s], bulk], 2 if s else 6)
+            recv(R("CQ%d" % s, 0, 128), "aCQ%d" % s, [sq[s]], hops)
             for a in range(2):
-                ma = C("ma%d" % a)
-                ts(R("RR", a, 16, 2, 32), R("b2", 0, 8, 1, 32), R("col", ma[1], ma[2], 1, 32), ALU.mult)
-            group([(R("B6", 0, 2), R("SW", 112 - 16 * k, 240 - 16 * k, 1, 32), R("RR", 2 * k, 2 * k + 2, 1, 32)) for k in range(8)])
-            cp(Z("BL"), R("B6", 0, 2))
-            tt(Z("di"), ind(FBW, Z("BL")), Z("xo"), ALU.subtract)
-            ts(R("ZI", 0, 32), Z("di"), 1, ALU.arith_shift_right)
-            tt(x, ind(Z("ZI"), Z("POS")), x, ALU.add)
+                cp(R("cqu", a, 32, 2), ind(Z("CQ%d" % s), R("INV", 2 * a, 2 * a + 1)))
+            for c in range(2):
+                scaled(R("dd", 256 * c, 256 * c + 256), ind(FBW, R("cqu", 16 * c, 16 * c + 16)), 0.5)
+            for c in range(2):
+                tt(R("da", 256 * c, 256 * c + 256), R("dd", 256 * c, 256 * c + 256), R("B0", 256 * c, 256 * c + 256), ALU.max)
+            key = R("B5", 0, 32)
+            group([(key, Z("I32h"), Z("KC"))]
+                  + [(key, Wsl("Wn", b), R("dd", 32 * b, 32 * b + 32)) for b in range(16)]
+                  + [(key, Wsl("Wp", b), R("da", 32 * b, 32 * b + 32)) for b in range(16)])
+            scan(Z("ks"), Z("RB"), key, 0.0, ALU.add, ALU.min)
+            cp(R("b1", 0, 2), R("ks", 15, 32, 16))
+            ts(R("b2", 0, 2), R("b1", 0, 2), 511, ALU.bitwise_and)
+            cp(R("BL", 0, 2), R("b2", 0, 2))
+            tt(Z("di"), ind(Z("dd"), R("BL", 0, 2)), Z("xo"), ALU.add)
+            cp(ind(Xt(t, XW), R("INV", 0, 2)), Z("di"))
             if t < 3:
                 sx[t] = send("x%d" % t)
-            else:
-                store("Y", T.yx[:], Z("X"), "dyx", 128 * 1024)
+            store("Y", T.yx[:, 128 * t:128 * t + 128], x, "dx%d" % t, 0)
         xt = R("B0", 0, 128)
         group([(xt, Z("Id"), x)])
         for h in range(3):
-            at("t%d" % h)
+            at(t, "t%d" % h)
+            D, DT = R(bank[h], 0, 128), R(bank[h], 128, 256)
             take(H("a0", h), ind(x, KL("L0u", h)))
             tt(H("m0", h), H("a0", h), xt, ALU.max)
-            U = H("B3", h)
-            group([(U, Z("TH"), Z("ones")), (U, Z("BOn"), x), (U, Z("BOn"), H("a0", h)), (U, Z("BOb"), H("m0", h))])
-            tt(U, H("nk", h), U, ALU.max)
-            at("d%d" % h)
+            for l, r in ((x, "BOn"), (H("a0", h), "BOn"), (H("m0", h), "BO2")):
+                mm(dg[h], DT, l, Z(r))
+            at(t, "d%d" % h)
             brows, frows = list(range(1, 16 - NF[h])), list(range(16 - NF[h], 16))
-            mm(D[h], Z("BOx%d" % NF.index(NF[h])), x, False, False)
-            for f0 in range(0, len(frows), 4):
-                rows = frows[f0:f0 + 4]
+            mm(dg[h], D, x, Z("BOx%d" % NF.index(NF[h])))
+            nch = (len(frows) + 3) // 4
+            for c in range(nch):
+                rows = frows[len(frows) * c // nch:len(frows) * (c + 1) // nch]
+                st = "B%d" % (4 + stage[0] % 2)
+                stage[0] += 1
                 for j, i in enumerate(rows):
-                    group([(H("B4", j), Z("Id"), ra(h, i)), (H("B4", j), Z("Idn"), x)])
-                act(mo(h, rows[0], len(rows)), H("B4", 0, len(rows)), ACT.Abs)
+                    group([(H(st, j), Z("Id"), ra(h, i)), (H(st, j), Z("Idn"), x)])
+                act(mo(h, rows[0], len(rows)), H(st, 0, len(rows)), ACT.Abs)
             for i in brows:
                 tt(mo(h, i), ra(h, i), xt, ALU.max)
             for i in brows + frows:
-                mm(D[h], Wsl("Wp" if i in brows else "W1", i), mo(h, i), False, i == 15)
-            act(H("sg", h), D[h], ACT.Sign, bias=C("thb"), scale=-1.0)
+                mm(dg[h], R(bank[h], i, 128, 16), mo(h, i), G8("BO2" if i in brows else "BO"))
+            act(H("sg", 2 * h, 2), R(bank[h], 0, 256), ACT.Sign, bias=0.5, scale=-1.0)
         if t < 3:
-            at("q")
+            at(t, "q")
             take(R("F", n0, n0 + 128), x)
             hops = len([1 for w, c in h1calls if w == "hX%d" % t]) + 1
-            recv(Z("XQ%d" % t), "aXQ%d" % t, sx[t], hops * HOP)
-            compact("B1", "Ww", "XQ%d" % t)
-            cp(Z("QI"), R("B1", 0, 8))
+            recv(Z("XQ%d" % t), "aXQ%d" % t, [sx[t]], hops)
+            compact("B7", "Ww", "XQ%d" % t)
+            cp(Z("QI"), R("B7", 0, 8))
             ts(Z("QA"), Z("QI"), 1023, ALU.bitwise_and)
             cp(Z("QL"), Z("QA"))
         for h in range(3):
-            at("h%d" % h)
-            if h or not t:
+            at(t, "h%d" % h)
+            U = H("B6", h)
+            group([(U, Z("CUd"), one), (U, one, IdA), (U, H("sg", 2 * h), Z("IdB")), (U, H("sg", 2 * h + 1), IdA)])
+            if h:
                 take(H("cc", h), ind(AW, KL("KL", h)))
-            tt(H("mm", h), H("cc", h), H("B3", h), ALU.is_equal)
+            tt(H("mm", h), H("cc", h), U, ALU.is_ge)
+            ts(H("em", h), H("cc", h), C("emb"), ALU.add, 0.0, ALU.max)
             act(H("em", h), H("cc", h), ACT.Relu, bias=C("emb"))
-            Y = R("B6", 0, 128)
-            old = [(Z("BOa"), H("sg", j)) for j in range(h)] + [(Z("BOb"), H("mm", j)) for j in range(h)]
-            group([(Y, l, r) for l, r in [(Z("Id"), Z("pv2"))] + old
-                   + [(Z("BOa"), H("sg", h)), (Z("TMb"), H("em", h)), (Z("BOb"), H("mm", h))]])
-            act(H("rr", h), Y, ACT.Relu, bias=float(E - n0 - 2048 - 16384 * (h + 1)), scale=-0.5)
+            either()
+            Y = H(bank[h], 2)
+            old = [(Z("BO"), H("mm", j)) for j in range(h)] + [(Z("BOn"), H("em", j)) for j in range(h)]
+            group([(Y, l, r) for l, r in [(Z("Id"), Z("pv"))] + old + [(Z("Q"), H("em", h)), (Z("BO"), H("mm", h))]])
+            act(H("rr", h), Y, ACT.Relu, bias=float(E - n0 - 2048), scale=-2048.0)
             tt(ind(AS, KL("SL", h)), H("cc", h), H("rr", h), ALU.subtract)
-            at("p%d" % h)
-            Pp = H("B7", h)
-            ta, tb = ("TMa", "TMb") if h < 2 else ("T3a", "T3b")
-            group([(Pp, l, r) for l, r in old + [(Z(ta), H("sg", h)), (Z(tb), H("mm", h))]])
-            act(Pp, Pp, ACT.Relu, bias=C("pb%d" % h), scale=-1.0 / 4096)
+            at(t, "p%d" % h)
+            Pp = H(bank[h] if h < 2 else "B0", 3)
+            group([(Pp, l, r) for l, r in old + [(Z("T3n"), H("em", h)), (Z("T3"), H("mm", h))]])
+            act(Pp, Pp, ACT.Relu, bias=C("r0") if h == 2 else 0.0, scale=-1.0)
             tt(H("fc", h), H("cc", h), Pp, ALU.mult)
         if t < 3:
-            at("co")
+            at(t, "co")
             take(Z("CO%d" % t), ind(R("A", 0, 1024), Z("QL")))
             sq[t] = send("c%d" % t)
-            at("p2")
-            group([(R("B0", 0, 128), Z("BO16"), H("fc", h)) for h in range(3)])
         else:
-            store("Y", T.yp[:, 0:768], R("A", 0, 768), "dy0", 128 * 768 * 8)
-            store("S", T.yp[:, 768:n0], R("A", 768, n0), "dy1", 128 * 768 * 8)
-        group([(R("B6", 0, 128), Wsl("W16", 0), H("fc", h)) for h in range(3)])
-        tt(R("A", n0, n0 + 128), R("A", n0, n0 + 128), R("B6", 0, 128), ALU.add)
+            store("Y", T.yp[:, 0:768], R("A", 0, 768), "dy0", 128 * n0 * 4)
+            store("S", T.yp[:, 768:n0], R("A", 768, n0), "dy1", 128 * n0 * 4)
+        at(t, "link")
+        group([(H("B4", 0), Wsl("W16", 0), H("fc", h)) for h in range(3)])
+        tt(R("A", n0, n0 + 128), R("A", n0, n0 + 128), H("B4", 0), ALU.add)
         if t == 3:
             store("Y", T.yp[:, n0:E], R("A", n0, E), "dy2", 128 * 512)
             break
-        tt(Z("w1"), Z("DM"), R("B0", 0, 128), ALU.mult)
-        scan(Z("w2"), Z("RS"), Z("w1"), 0.0, ALU.mult, ALU.add)
-        cp(KL("KL", 0), R("w2", 15, 128, 16))
-        at("ask")
-        Zp = R("B2", 0, 128)
-        group([(Zp, Z("BOa"), H("sg", j)) for j in range(3)] + [(Zp, Z("BOb"), H("mm", j)) for j in range(3)])
-        act(Z("esc"), Zp, ACT.Relu, bias=-23.0, scale=-1.0 / 4096)
-        scan(Z("cnt"), Z("ones"), Z("esc"), 98304.0, ALU.mult, ALU.add)
-        tt(R("B2", 128, 256), Z("cnt"), Zp, ALU.add)
-        tt(Z("v1"), Z("MP"), R("B2", 128, 256), ALU.min)
-        scan(Z("v2"), Z("RS"), Z("v1"), 0.0, ALU.mult, ALU.add)
-        ts(Z("POS"), R("v2", 15, 128, 16), -1.0, ALU.add)
-        cp(ind(Z("SP"), Z("POS")), J128)
-        tt(Z("s1"), R("SP", 0, 32), R("DM", 0, 32), ALU.mult)
-        scan(Z("s2"), R("RS", 0, 32), Z("s1"), 0.0, ALU.mult, ALU.add)
-        cp(Z("INV"), R("s2", 15, 32, 16))
-        take(Z("xz"), ind(x, Z("INV")))
+        group([(R("B5", 0, 8), Wsl("W16", b), R("fc", 128 * h + b, 128 * h + 128, 16)) for h in range(3) for b in range(16)])
+        cp(KL("KL", 0), R("B5", 0, 8))
+        at(t, "ask")
+        Zp = H("B6", 3)
+        group([(Zp, Z("BO"), H("mm", j)) for j in range(3)] + [(Zp, Z("BOn"), H("em", j)) for j in range(3)])
+        act(R("esc", 0, 128), Zp, ACT.Relu, bias=1.0, scale=-1.0)
+        scan(Z("cnt"), Z("ones"), Z("esc"), 0.0, ALU.mult, ALU.add)
+        for a in range(2):
+            act(Z("junk"), Z("cnt"), ACT.Sign, bias=C("s%d" % a), scale=-1.0, acc=R("acc", a, a + 1))
+        ts(R("INV", 0, 2), R("acc", 0, 2), 0.5, ALU.mult, XW / 2.0, ALU.add)
+        ts(R("INV", 2, 3), R("acc", 1, 2), 0.5, ALU.mult, XW / 2.0, ALU.add)
+        for a in range(2):
+            scaled(R("xz", a, 32, 2), ind(Xt(t, XW), R("INV", 2 * a, 2 * a + 1)), 0.5)
         for i in range(16):
-            group([(R("B7", i, 512, 16), Z("Id"), Z("xz"))])
-        take(Z("xo"), ind(H("X", t + 1), Z("INV")))
+            group([(R("B0", i, 512, 16), Z("Id"), Z("xz"))])
+        ts(Z("xo"), ind(Xt(t + 1, XW), R("INV", 0, 2)), 0.5, ALU.mult, -0.25, ALU.add)
+        act(Z("xo"), ind(Xt(t + 1, XW), R("INV", 0, 2)), ACT.Identity, bias=-0.25, scale=0.5)
+        either()
     return ops, nls
 
 
 def hazards(ops):
-    hist, preds = {}, []
+    hist, runs, preds = {}, {}, []
     for j, o in enumerate(ops):
         pr = {}
-        for wr, rs in ((False, o["r"]), (True, o["w"])):
-            for r in rs:
-                bank = SCRATCH[r[0]][0] == "psum"
-                for (a, b, i, w2) in hist.get(r[0], []):
-                    if i == j:
-                        continue
-                    hit = a < r[2] and r[1] < b
-                    if bank and ops[i]["e"] != o["e"]:
-                        pr[i] = True
-                    elif (hit and (wr or w2)) or (bank and o["e"] == "P"):
-                        pr[i] = pr.get(i, False) or (hit and w2)
-        for wr, rs in ((False, o["r"]), (True, o["w"])):
-            for r in rs:
-                lst = hist.setdefault(r[0], [])
-                if SCRATCH[r[0]][0] == "psum":
-                    if lst and ops[lst[-1][2]]["e"] != o["e"]:
-                        e0 = ops[lst[-1][2]]["e"]
-                        k = len(lst)
-                        while k > 0 and ops[lst[k - 1][2]]["e"] == e0:
-                            k -= 1
-                        lst[:] = lst[k:]
-                    elif lst and o["e"] == "P":
-                        lst.pop()
-                elif wr and r[3] == 1 and r[4] == 128:
-                    lst[:] = [z for z in lst if not (r[1] <= z[0] and z[1] <= r[2])]
-                lst.append((r[1], r[2], j, wr))
+        both = [(False, r) for r in o["r"]] + [(True, r) for r in o["w"]]
+        for wr, r in both:
+            if SCRATCH[r[0]][0] == "psum":
+                st = runs.setdefault(r[0], {"key": None, "cur": [], "old": [], "by": {}})
+                key = (o["e"], o["grp"])
+                if o["grp"] is not None and o["grp"] in st["by"] and st["key"] != key:
+                    raise ValueError("group cut on " + r[0])
+                if st["key"] != key:
+                    st["key"], st["old"], st["cur"] = key, st["cur"], []
+                    st["by"][o["grp"]] = True
+                for i in st["old"]:
+                    pr[i] = True
+                if o["grp"] is not None and st["cur"] and st["cur"][0] != j:
+                    pr[st["cur"][0]] = True
+                if j not in st["cur"]:
+                    st["cur"].append(j)
+                if o["e"] == "P":
+                    continue
+            for (a, b, i, w2) in hist.get(r[0], []):
+                if i != j and a < r[2] and r[1] < b and (wr or w2):
+                    pr[i] = pr.get(i, False) or w2
+        for wr, r in both:
+            if SCRATCH[r[0]][0] == "psum" and o["e"] == "P":
+                hist[r[0]] = []
+                continue
+            lst = hist.setdefault(r[0], [])
+            if wr and r[3] == 1:
+                lst[:] = [z for z in lst if not (r[1] <= z[0] and z[1] <= r[2])]
+            lst.append((r[1], r[2], j, wr))
         preds.append(pr)
     return preds
 
 
-def kind(o):
-    return (o["w"] or o["r"])[0][0] + (o["r"][0][0] if o["e"] == "P" else "")
-
-
-def schedule(ops, preds):
+def schedule(ops, preds, fig):
     n = len(ops)
-    dep = [list(p.keys()) + ([o["after"]] if o["after"] is not None else []) for p, o in zip(preds, ops)]
+    dep = [list(p.keys()) + o["after"] for p, o in zip(preds, ops)]
     succ = [[] for _ in range(n)]
     for j in range(n):
         for i in dep[j]:
             succ[i].append(j)
-    prio = [-16000.0 * o["d"][0] - 1000.0 * DUE[o["d"][1]] - 0.01 * j for j, o in enumerate(ops)]
-    eng = ["V" if o.get("key") in ONVK else o["e"] for o in ops]
+    cost = [{e: price(v[1], fig) for e, v in o["alt"].items()} for o in ops]
+    lat = [price(o["lat"], fig) for o in ops]
+
+    def gap(i, k):
+        return 0.0 if (ops[i]["e"] == ops[k]["e"] == "P" or ops[k]["e"] == "N") else fig["sync"]
+    prio = [0.0] * n
+    for j in range(n - 1, -1, -1):
+        prio[j] = min(cost[j].values()) + lat[j] + max([gap(j, k) + prio[k] for k in succ[j]] + [0.0]) - 0.001 * j
     left = [len(d) for d in dep]
-    ready, start = [0.0] * n, [0.0] * n
-    free, order, pool, last = {}, [], {}, 0.0
-    for j in range(n):
-        if left[j] == 0:
-            pool.setdefault(eng[j], []).append(j)
-    while len(order) < n:
-        best = None
-        for e, lst in pool.items():
-            if not lst:
-                continue
-            f = 0.0 if e == "N" else free.get(e, 0.0)
-            t0 = max(f, min(ready[j] for j in lst)) + LOOK
-            j = max([k for k in lst if ready[k] <= t0], key=lambda k: prio[k])
-            t0 = max(f, ready[j])
-            if best is None or t0 < best[0]:
-                best = (t0, j, e)
-        t0, j, e = best
-        pool[e].remove(j)
+    prio = [p + BOOST.get(o["d"][1], 0.0) for p, o in zip(prio, ops)]
+    ready, start, eng, end = [0.0] * n, [0.0] * n, [None] * n, [None] * n
+    now, order, pool = {e: 0.0 for e in "VSPGY"}, [], {e: [] for e in "VSPGY"}
+    todo = {e: sorted([j for j in range(n) if list(cost[j]) == [e]], key=lambda j: -prio[j]) for e in now}
+    held = {e: 0.0 for e in now}
+
+    def place(j, e, t0):
         order.append(j)
-        start[j] = t0
-        free[e] = t0 + (ops[j]["alt"][e][1] if "alt" in ops[j] else ops[j]["c"])
-        end = free[e] + ops[j]["lat"]
-        last = max(last, end)
+        start[j], eng[j], end[j] = t0, e, t0 + cost[j][e] + lat[j]
         for k in succ[j]:
-            ready[k] = max(ready[k], end + (0.0 if (e == eng[k] == "P" or eng[k] == "N") else SYNC))
+            ready[k] = max(ready[k], end[j] + gap(j, k))
             left[k] -= 1
             if left[k] == 0:
-                pool.setdefault(eng[k], []).append(k)
-    return order, eng, start, last
+                offer(k)
+
+    def offer(j):
+        if ops[j]["e"] == "N":
+            place(j, "N", ready[j])
+        else:
+            for e in cost[j]:
+                pool[e].append(j)
+
+    def soon(u, depth, memo):
+        if u not in memo:
+            r = ready[u]
+            if left[u] and depth == 0:
+                r = 1e12
+            elif left[u]:
+                for i in dep[u]:
+                    if end[i] is None:
+                        s = soon(i, depth - 1, memo)
+                        r = max(r, min(max(s, now.get(e, 0.0)) + c for e, c in cost[i].items()) + lat[i] + gap(i, u))
+            memo[u] = r
+        return memo[u]
+    for j in [j for j in range(n) if left[j] == 0]:
+        offer(j)
+    while len(order) < n:
+        e = min(now, key=lambda q: now[q])
+        t0, j = now[e], None
+        can = [k for k in pool[e] if ready[k] <= t0 + LOOK]
+        if can:
+            todo[e] = [u for u in todo[e] if end[u] is None]
+            memo = {}
+            urgent = [(u, soon(u, DEPTH, memo)) for u in todo[e][:AHEAD] if u not in can]
+            for k in sorted(can, key=lambda k: -prio[k] + (PEN if e == "V" and len(cost[k]) > 1 else 0.0)):
+                fin = max(t0, ready[k]) + cost[k][e]
+                if held[e] > 1000 or all(prio[u] < prio[k] + SLACK or HOLD * (r - t0) >= fin - r for u, r in urgent):
+                    j = k
+                    break
+        if j is None:
+            now[e] = t0 + 30.0
+            held[e] += 30.0 if can else 0.0
+            continue
+        for e2 in cost[j]:
+            pool[e2].remove(j)
+        now[e], held[e] = max(t0, ready[j]) + cost[j][e], 0.0
+        place(j, e, max(t0, ready[j]))
+    return order, eng, start, max(end)
 
 
 def emit(g, T, ops, preds, order, nls):
     queue = {"V": g.vector, "S": g.scalar, "P": g.tensor, "G": g, "Y": g.sync}
-    pos, cnt = {}, {}
+    pos, cnt, final = {}, {}, {}
     at = {j: k for k, j in enumerate(order)}
     for j in order:
         e = ops[j]["e"]
         cnt[e] = cnt.get(e, 0) + 1
         pos[j] = cnt[e]
+        if ops[j]["grp"] is not None:
+            final[ops[j]["grp"]] = j
+    for j in final.values():
+        ops[j]["stop"] = True
     known, clock, waits, target = {}, {}, {}, set()
     for j in order:
         o = ops[j]
@@ -711,7 +761,7 @@ def emit(g, T, ops, preds, order, nls):
                 q.wait_ge(T.sem[p["sem"][0]], p["sem"][1])
             else:
                 q.wait_ge(T.sem[ESEM[p["e"]]], count[i])
-        ins = o["f"]()
+        ins = o["alt"][o["e"]][0]()
         if o["sem"] is not None:
             ins.then_inc(T.sem[o["sem"][0]], o["sem"][1])
         elif j in target:
@@ -741,9 +791,8 @@ def rank_program(g, core, T, topo):
     ops, nls = build(g, T, topo, rank)
     preds = hazards(ops)
     if "o" not in _ORDER:
-        _ORDER["o"] = schedule(ops, preds)
+        _ORDER["o"] = schedule(ops, preds, FIG)
     order, eng = _ORDER["o"][:2]
     for o, e in zip(ops, eng):
-        if "alt" in o:
-            o["e"], o["f"] = e, o["alt"][e][0]
+        o["e"] = e
     emit(g, T, ops, preds, order, nls)

@@ -3,15 +3,22 @@ from concourse.mybir import AluOpType, ActivationFunctionType
 
 ALU = AluOpType
 ACT = ActivationFunctionType
-M, P, NT, E = 1152, 128, 4, 1664
+M, P, NT, E, HM = 1152, 128, 4, 1664, 1024
+FO = 272
+FAR = 64
 XW = 160
-NF = [7, 6, 7]
-CHH = [256, 256, 256]
-FIG = {"cyc": 1.04, "gath": 1.62, "scat": 4.0, "pe": 0.52, "sync": 90.0, "hop": 2500.0, "dma": 2000.0, "bw": 200.0, "send": 400.0}
-LOOK, HOLD, PEN, SLACK, AHEAD, DEPTH = 40.0, 2.0, 3000.0, 1000.0, 8, 4
-BOOST = {'p0': 1500, 'p1': 1750, 'p2': 2250, 'link': 5500, 'cu0': 4500, 't1': 250, 'd1': 500, 'h0': -250, 'c': 250, 'sl': -250,
-         'q': 500, 'wn0': -2000, 'ask': -500, 'co': -2500, 'wn1': -750, 'cu1': 250, 'cu2': -1000, 'wn2': 500, 'd0': -250,
-         't0': 250, 't2': -250}
+SETS = [(3, 4), (2, 4), (1, 4), (4, 8), (8, 16)]
+ONV = [3, 3, 2]
+CHH = [1024, 512, 512]
+TSPLIT = [(0, 3)]
+BIG = 2048.0
+FIGS = [{"cyc": c, "gath": c * ga, "scat": c * sc, "pe": c / 2, "sync": sync, "fix": fix, "hop": hop, "dma": 2000.0, "bw": bw,
+         "send": 400.0, "norm": norm}
+        for c, ga, sc, sync, fix, hop, bw, norm in ((0.9, 1.56, 3.8, 130.0, 30.0, 2300.0, 200.0, 75.0),
+                                                    (0.83, 1.3, 3.0, 170.0, 30.0, 2900.0, 150.0, 75.0),
+                                                    (1.15, 1.95, 5.0, 130.0, 30.0, 2000.0, 200.0, 95.0),
+                                                    (1.1, 1.15, 4.5, 120.0, 40.0, 2000.0, 200.0, 82.0))]
+LEAN, SLACK, ROUNDS, SEED, MEAN = 500.0, 5.0, 10000, 1, 0.3
 SAME_WAR = True
 
 F32, BF, I32, U16, F16 = "float32", "bfloat16", "int32", "uint16", "float16"
@@ -24,45 +31,57 @@ def _decl(names, cols, dtype, where="sbuf"):
 
 
 _decl("A", 1800, F32)
-_decl("P32", M, I32)
-_decl("F FB0 FB1 FB2", 1680, BF)
-_decl("FX", 1280, BF)
+_decl("P32", 1672, I32)
+_decl("F FB0 FB1 FB2", FO + 1680, BF)
+_decl("AB0 AB1 AB2 VM", HM, F32)
 _decl("X", 4 * XW, BF)
 _decl("dd da", 512, BF)
-_decl("XQ0 XQ1 XQ2", 128, BF)
-_decl("ones esc cnt junk J", XW, BF)
-_decl("CQ0 CQ1 CQ2", XW, F32)
-_decl("CO0 CO1 CO2 R1V tB c1", 128, F32)
-_decl("hwi thi pi pj", 4, I32)
-_decl("col RB ks", 32, F32)
-_decl("NV", 640, F32)
-_decl("J16 Id Idn IdB IdA0 IdA1 IdA2 IdA3 CUd BO BOn BO2 BOx0 BOx1 BOx2 Q T3 T3n pv", 128, BF)
-_decl("THd", 256, BF)
-_decl("W1 Wp Wn Ww", 144, BF)
-_decl("I32h c16", 128, F16)
-_decl("E0w W16", 144, F16)
+_decl("XQ", 384, BF)
+_decl("ones esc cnt", XW, BF)
+_decl("junk", 4 * XW, BF)
+_decl("J", 256, BF)
+_decl("CO", XW, F32)
+_decl("WQ WK", 384, F32)
+_decl("R1V tB E00", 128, F32)
+_decl("hwi thi", 4, I32)
+_decl("pi", 8, I32)
+_decl("col qb", 32, F32)
+_decl("RB", 64, F32)
+_decl("ks", 96, F32)
+_decl("NV", 512, F32)
+_decl("J16 Id Idn Id2 Id4 CUd BO BOn BO2 BO3 BO3n BOB BOBn BK1 BK2 BOx0 BOx1 BOx2 T3 T3n THd", 128, BF)
+_decl("W1 Wp Wn", 144, BF)
+_decl("I32h LT", 128, F16)
+_decl("E0w", 144, F16)
+_decl("Wd", 240, F16)
 _decl("KC", 32, F16)
-_decl("PC DUM nq tq", 24, F32)
+_decl("RR", 64, F16)
+_decl("G64 MK tq", 64, F32)
+_decl("Wc", 192, BF)
+_decl("J8", 64, BF)
+_decl("PC DUM nq", 24, F32)
 _decl("KI L0", 24, I32)
 _decl("KL L0u SL", 24, U16)
-_decl("QI QA b1 b2", 8, I32)
-_decl("QL INV BL", 8, U16)
-_decl("acc", 8, F32)
+_decl("QI QA b1 b2 qc", 8, I32)
+_decl("QL INV BL QM", 8, U16)
+_decl("acc cs wc kn", 8, F32)
 _decl("CU", 384, U16)
 _decl("raw mx", 6144, BF)
-_decl("cc rr", 384, F32)
-_decl("a0 m0 mm em", 384, BF)
+_decl("cc nv fc", 384, F32)
+_decl("a0 m0 mm sp PV", 384, BF)
 _decl("sg", 768, BF)
-_decl("fc", 384, F16)
+_decl("c16", 384, F16)
 _decl("cqu", 32, U16)
-_decl("xo xz JM", 32, BF)
-_decl("di", 32, I32)
+_decl("xo xz K2 qr eq", 32, BF)
+_decl("KH K1 dm", 64, BF)
+_decl("cq6", 32, F16)
+_decl("di", 64, I32)
 _decl("B0 B1 B2 B3 B4 B5 B6 B7", 512, F32, "psum")
 
 SEMAPHORES = ["sV", "sS", "sP", "sG", "ls", "dp0", "dp1", "dp2", "dfr", "dn0", "dn1", "dn2", "dn3", "dhw", "dth",
-              "dx0", "dx1", "dx2", "dx3", "dy0", "dy1", "dy2",
-              "aXQ0", "aXQ1", "aXQ2", "aCQ0", "aCQ1", "aCQ2", "aFB0", "aFB1", "aFB2",
-              "hX0", "hX1", "hX2", "hC0", "hC1", "hC2", "hB"]
+              "dx0", "dx1", "dx2", "dx3", "dy0", "dy1", "dy2", "dy3", "df0", "df1", "df2",
+              "da0", "da1", "da2", "aAB0", "aAB1", "aAB2", "aWQ0", "aWQ1", "aWQ2", "aFB0", "aFB1", "aFB2", "aFX1", "aFX2",
+              "hX1", "hX2", "hC0", "hC1", "hC2", "hA0", "hA1", "hA2", "lA0", "lA1", "lA2", "hB"]
 ESEM = {"V": "sV", "S": "sS", "P": "sP", "G": "sG"}
 WIDTH = {F32: 4, I32: 4, BF: 2, U16: 2, F16: 2}
 _ORDER = {}
@@ -108,43 +127,51 @@ def deal(topo, src, dsts):
 def plan(T, topo, r):
     cores, n = T.cores, len(T.cores)
     me = cores[r]
-    up = [cores[(r + 1 + t) % n] for t in range(3)]
     dn = [cores[(r - 1 - t) % n] for t in range(3)]
-    can = [c for c in topo.cores_of(me) if c not in cores and all(topo.may_write(c, d) for d in up + dn)]
+    can = [c for c in topo.cores_of(me) if c not in cores and all(topo.may_write(c, d) for d in dn)]
     near = [c for c in can if topo.die(c) == topo.die(me)]
     far = [c for c in can if topo.die(c) != topo.die(me)]
-    h1 = (near + far)[0]
-    hb = [c for c in far + near if c != h1][0]
-    calls, h1calls = {}, []
-    calls["bulk"] = [(R("F", 0, M), hb, R("FX", 0, M), "hB")]
-    hbcalls = [("hB", [(R("FX", 0, 1280), dn[t], R("FB%d" % t, 0, 1280), "aFB%d" % t)]) for t in range(3)]
+    hs = (near + far)[:pow2(len(can))]
+    h1, calls, hands = hs[0], {}, {h: [] for h in hs}
+    h1calls = hands[h1]
+    wf, wa = (FO + M + 128) // len(hs), HM // len(hs)
+    calls["bulk"] = [(R("F", wf * k, wf * k + wf), h, R("FB0", wf * k, wf * k + wf), "hB") for k, h in enumerate(hs)]
+
+    def frames(t):
+        for src, h, mid, sem in calls["bulk"]:
+            hands[h].append((sem, [(mid, dn[t], R("FB%d" % t, mid[1], mid[2]), "aFB%d" % t)]))
+    frames(0)
     for s in range(3):
-        src, mid = R("X", XW * s, XW * s + 128), R("XQ%d" % s, 0, 128)
-        want = [(up[s], mid, "aXQ%d" % s)]
-        if s > 0:
-            want += [(dn[t], R("FB%d" % t, M + 128 * s, M + 128 * s + 128), "aFB%d" % t) for t in range(s, 3)]
-        mine = [(src, d, o, sem) for d, o, sem in want if topo.may_write(me, d)]
-        via = [(mid, d, o, sem) for d, o, sem in want if not topo.may_write(me, d)]
-        if via:
-            mine.append((src, h1, mid, "hX%d" % s))
-            h1calls.append(("hX%d" % s, via))
+        calls["a%d" % s] = [(R("A", wa * k, wa * k + wa), h, R("AB%d" % s, wa * k, wa * k + wa), "hA%d" % s)
+                            for k, h in enumerate(hs)]
+        for src, h, mid, sem in calls["a%d" % s]:
+            hands[h].append((sem, [(mid, dn[s], mid, "aAB%d" % s)]))
+        src, mid, new = R("X", XW * s, XW * s + 128), R("XQ", 128 * s, 128 * s + 128), FO + M + 128 * s
         if s == 0:
-            mine.append((src, hb, R("FX", M, 1280), "hB"))
-        calls["x%d" % s] = mine
-        src, mid = R("CO%d" % s, 0, 128), R("CQ%d" % s, 0, 128)
+            frames(1)
+            frames(2)
+        else:
+            want = [(dn[t], R("FB%d" % t, new, new + 128), "aFX%d" % t) for t in range(s, 3)]
+            mine = [(src, d, o, sem) for d, o, sem in want if topo.may_write(me, d)]
+            via = [(mid, d, o, sem) for d, o, sem in want if not topo.may_write(me, d)]
+            if via:
+                mine.append((src, h1, mid, "hX%d" % s))
+                h1calls.append(("hX%d" % s, via))
+            calls["x%d" % s] = mine
+        src, mid = R("WK", 128 * s, 128 * s + 128), R("WQ", 128 * s, 128 * s + 128)
         if topo.may_write(me, dn[s]):
-            calls["c%d" % s] = [(src, dn[s], mid, "aCQ%d" % s)]
+            calls["c%d" % s] = [(src, dn[s], mid, "aWQ%d" % s)]
         else:
             calls["c%d" % s] = [(src, h1, mid, "hC%d" % s)]
-            h1calls.append(("hC%d" % s, [(mid, dn[s], mid, "aCQ%d" % s)]))
-    return me, calls, h1, h1calls, hb, hbcalls
+            h1calls.append(("hC%d" % s, [(mid, dn[s], mid, "aWQ%d" % s)]))
+    return me, calls, hands
 
 
 def arrivals(T, topo, core):
     tot = {}
     for r in range(len(T.cores)):
-        me, calls, h1, h1calls, hb, hbcalls = plan(T, topo, r)
-        every = [(me, c) for c in calls.values()] + [(h1, c) for w, c in h1calls] + [(hb, c) for w, c in hbcalls]
+        me, calls, hands = plan(T, topo, r)
+        every = [(me, c) for c in calls.values()] + [(h, c) for h in hands for w, c in hands[h]]
         for src, c in every:
             for tr, en in zip(c, deal(topo, src, [x[1] for x in c])):
                 if tr[1] == core:
@@ -158,18 +185,18 @@ def ap_of(T, r):
     return T[r[0]][:, r[1]:r[2]:r[3]]
 
 
-def remote_call(g, T, topo, src, c):
+def remote_call(g, T, topo, src, c, left="ls"):
     en = deal(topo, src, [x[1] for x in c])
     if len(c) == 1:
         rid, pid = topo.addr(c[0][1], src)
-        g.remote_dma(ap_of(T, c[0][2]), ap_of(T, c[0][0]), T.sem[c[0][3]], T.sem["ls"], pid, rid, mask_of(en[0]))
+        g.remote_dma(ap_of(T, c[0][2]), ap_of(T, c[0][0]), T.sem[c[0][3]], T.sem[left], pid, rid, mask_of(en[0]))
     else:
         trs = []
         for x, e in zip(c, en):
             rid, pid = topo.addr(x[1], src)
             trs.append(RemoteDMATransfer(dst_ids=[DstId(rid=rid, pnc=pid)], dma_engine_mask=mask_of(e),
                                          remote_sem=T.sem[x[3]], src=ap_of(T, x[0]), dst=ap_of(T, x[2])))
-        g.remote_dma_fused(trs, local_sem=T.sem["ls"])
+        g.remote_dma_fused(trs, local_sem=T.sem[left])
     return sum(len(e) for e in en)
 
 
@@ -180,7 +207,7 @@ def price(c, fig):
 def build(g, T, topo, rank):
     ops = []
     tag, nls, cn, groups, loaded = [(0, "c")], [0], {}, [0], [0]
-    me, calls, h1, h1calls, hb, hbcalls = plan(T, topo, rank)
+    me, calls, hands = plan(T, topo, rank)
     arr = arrivals(T, topo, me)
 
     def ap(x):
@@ -271,18 +298,31 @@ def build(g, T, topo, rank):
         act(out, i, ACT.Copy, scale=s)
         either()
 
-    def mm(gid, out, l, r):
+    def lin(out, i, s, b):
+        ts(out, i, s, ALU.mult, b, ALU.add)
+        act(out, i, ACT.Identity, bias=b, scale=s)
+        either()
+
+    def mm(gid, terms, every=0):
         first = gid == groups[0]
         if first:
             groups[0] += 1
         j = len(ops)
-        add("P", lambda: g.tensor.matmul(ap(out), ap(l), ap(r), first, ops[j]["stop"]), regs(l, r), out,
-            (0, max(min(64, ncol(l)), ncol(r)), "pe"), grp=gid)
+
+        def f():
+            for k, (o, l, r) in enumerate(terms):
+                ins = g.tensor.matmul(ap(o), ap(l), ap(r), k % every == 0 if every else first and k == 0,
+                                      k % every == every - 1 if every else ops[j]["stop"] and k == len(terms) - 1)
+            return ins
+        add("P", f, [x for o, l, r in terms for x in (l, r)], None,
+            (0, sum(max(min(64, ncol(l)), ncol(r)) * WIDTH[SCRATCH[l[0]][2]] ** 2 // 4 for o, l, r in terms), "pe"),
+            grp=gid, more=[o for o, l, r in terms])
 
     def group(terms):
         gid = groups[0]
-        for o, l, r in terms:
-            mm(gid, o, l, r)
+        for x in terms:
+            if x:
+                mm(gid, x if isinstance(x, list) else [x])
         return gid
 
     def iota(out, pat, base, cm=0):
@@ -302,19 +342,29 @@ def build(g, T, topo, rank):
         qq = g.sync if q == "Y" else g.scalar
         loaded[0] += 128 * ncol(out) * WIDTH[SCRATCH[out[0]][2]]
         add(q, lambda: qq.dma_start(ap(out), src), [], out, (60, 0, "cyc"), sem=(sem, 16),
-            lat=(loaded[0] / FIG["bw"], 1, "dma"))
+            lat=(loaded[0], 1, "dma"))
 
     def store(q, dst, i, sem, nbytes):
         qq = g.sync if q == "Y" else g.scalar
-        add(q, lambda: qq.dma_start(dst, ap(i)), [i], None, (60, 0, "cyc"), sem=(sem, 16), lat=(nbytes / FIG["bw"], 1, "dma"))
+        add(q, lambda: qq.dma_start(dst, ap(i)), [i], None, (60, 0, "cyc"), sem=(sem, 16), lat=(nbytes, 1, "dma"))
 
-    def send(key):
+    def move(out, i, sem, rows=slice(0, 128)):
+        add("Y", lambda: g.sync.dma_start(T[out[0]][rows, out[1]:out[2]], T[i[0]][rows, i[1]:i[2]]), [i], out, (60, 0, "cyc"),
+            sem=(sem, 16), lat=(0, 1, "dma"))
+
+    def send(key, left=None):
         c = calls[key]
 
         def f():
-            nls[0] += remote_call(g, T, topo, me, c)
+            if left:
+                remote_call(g, T, topo, me, c, left)
+            else:
+                nls[0] += remote_call(g, T, topo, me, c)
             return None
-        return add("G", f, [c[0][0]], None, (0, 1, "send"))
+        if left:
+            return add("G", f, [x[0] for x in c], None, (0, 1, "send"), lat=(0, 1.5, "dma"),
+                       sem=(left, sum(len(e) for e in deal(topo, me, [x[1] for x in c]))))
+        return add("G", f, [x[0] for x in c], None, (0, 5 if key == "bulk" else 1, "send"))
 
     def recv(out, sem, after, hops):
         add("N", None, [], out, (0, 0, "cyc"), sem=(sem, arr[sem]), lat=(0, hops, "hop"), after=after)
@@ -342,13 +392,14 @@ def build(g, T, topo, rank):
     def G8(name):
         return R(name, 0, 128, 16)
 
-    def compact(bank, wide, src):
-        group([(R(bank, 0, 8), Wsl(wide, b), R(src, b, 128, 16)) for b in range(16)])
+    def compact(bank, wide, src, h=0):
+        group([[(R(bank, 0, 8), Wsl(wide, b), R(src, 128 * h + b, 128 * h + 128, 16)) for b in range(16)]])
 
     load("Y", R("P32", 1024, M), T.ptr[:, 1024:M], "dp0")
     load("S", R("P32", 0, 512), T.ptr[:, 0:512], "dp1")
     load("Y", R("P32", 512, 1024), T.ptr[:, 512:1024], "dp2")
-    load("S", R("F", 0, M), T.fr[:], "dfr")
+    load("S", R("F", FO, FO + M), T.fr[:], "dfr")
+    load("Y", R("F", FO + M, FO + M + 128), T.nw[:, 0:128], "df0")
     load("Y", Xt(0), T.nw[:, 0:128], "dn0")
     load("Y", R("thi", 0, 1), T.th[:], "dth")
     load("Y", R("hwi", 0, 1), T.hw[:], "dhw")
@@ -356,101 +407,123 @@ def build(g, T, topo, rank):
         load("Y", Xt(t), T.nw[:, 128 * t:128 * t + 128], "dn%d" % t)
     store("Y", T.yx[:, 0:128], Xt(0), "dx0", 0)
     J128, one = R("J", 0, 128), R("ones", 0, 128)
+    fill(Z("ones"), 1.0)
     iota(R("pi", 0, 1), [[0, 1]], 0, 1)
-    iota(Z("J"), [[1, XW]], 0)
+    iota(Z("J"), [[1, 256]], 0)
     iota(Z("J16"), [[16, 8], [0, 16]], 0)
-    iota(Z("JM"), [[0, 2], [1, 16]], 0)
-    iota(Z("NV"), [[1, 640]], M)
-    iota(Z("tq"), [[0, 3], [16, 8]], 0)
-    gfill(R("F", M, 1680), 99)
+    iota(Z("KH"), [[0, 4], [512, 16]], 0)
+    iota(R("NV", 0, 128), [[1, 128]], M)
+    iota(R("NV", 128, 512), [[1, 384]], M + 128)
+    iota(Z("tq"), [[0, 8], [16, 8]], 0)
+    iota(Z("J8"), [[16, 8], [0, 8]], 0)
+    fill(R("P32", M, 1672), E)
+    gfill(R("F", FO + M + 128, FO + 1680), FAR)
     for t in range(NT):
         gfill(R("X", XW * t + 128, XW * t + XW), 0)
     for t in range(3):
-        gfill(R("FB%d" % t, M + 128 * (t + 1), 1680), 99)
-        gfill(R("CQ%d" % t, 128, XW), 0)
+        gfill(R("FB%d" % t, FO + M + 128 * (t + 1), FO + 1680), FAR)
+    gfill(R("CO", 128, XW), 0)
+    iota(Z("VM"), [[0, HM // 128], [1, 128]], M)
     cp(C("p"), R("pi", 0, 1))
-    ts(R("pj", 0, 1), R("pi", 0, 1), 15, ALU.bitwise_and)
-    cp(C("i"), R("pj", 0, 1))
+    ts(R("pi", 4, 5), R("pi", 0, 1), 15, ALU.bitwise_and)
+    cp(C("i"), R("pi", 4, 5))
     tt(C("g16"), C("p"), C("i"), ALU.subtract)
     ts(C("r0"), C("i"), 0.0, ALU.is_equal)
     ts(C("r1"), C("i"), 1.0, ALU.is_equal)
-    ts(C("nr1"), C("i"), 1.0, ALU.not_equal)
+    lin(C("nr1"), C("r1"), -1.0, 1.0)
     ts(Z("W1"), R("J", 0, 144), C("g16"), ALU.subtract, 15.0, ALU.is_equal)
     ts(Z("E0w"), Z("W1"), C("r0"), ALU.mult)
-    ts(C("lo"), C("i"), 2.0, ALU.is_ge, float(E), ALU.mult)
-    ts(C("hi"), C("i"), 1.0, ALU.is_ge, float(E), ALU.mult)
-    ts(R("A", M, E), R("NV", 128, 640), C("lo"), ALU.max, C("hi"), ALU.min)
-    fill(R("A", E, 1800), float(E))
-    ts(Z("R1V"), R("NV", 0, 128), C("r1"), ALU.mult)
-    cp(Z("c16"), R("P32", 1024, M))
-    cp(R("A", 0, 512), R("P32", 0, 512))
-    cp(R("A", 512, 1024), R("P32", 512, 1024))
+    lin(C("hi"), C("r0"), -float(E), float(E))
+    lin(C("lo"), C("r1"), -float(E), C("hi"))
+    lin(R("A", M, E - 128), R("NV", 128, 512), C("r1"), C("lo"))
+    scaled(R("A", E - 128, E), one, C("hi"))
+    gfill(R("A", E, 1800), E)
+    scaled(Z("R1V"), R("NV", 0, 128), C("r1"))
+    cp(H("c16", 2), R("P32", 1024, M))
     ts(Z("tB"), R("P32", 1024, M), C("nr1"), ALU.mult)
-    tt(R("A", 1024, M), Z("tB"), Z("R1V"), ALU.max)
+    tt(R("P32", 1024, M), Z("tB"), Z("R1V"), ALU.max)
+    for a, b in ((0, 256), (256, 512), (512, 768), (768, 1024), (1024, M)):
+        cp(R("A", a, b), R("P32", a, b))
     ts(Z("Id"), J128, C("p"), ALU.is_equal)
     ts(Z("BO"), Z("J16"), C("g16"), ALU.is_equal)
-    for o, i, s in (("BOn", "BO", -1.0), ("BO2", "BO", 2.0), ("Idn", "Id", -1.0), ("IdB", "Id", -1024.0),
-                    ("Wp", "W1", 2048.0), ("Wn", "W1", -1024.0)):
+    for o, i, s in (("BOn", "BO", -1.0), ("BO2", "BO", 2.0), ("BOB", "BO", BIG), ("BOBn", "BO", -BIG), ("Idn", "Id", -1.0),
+                    ("Id2", "Id", BIG), ("Id4", "Id", 2 * BIG), ("Wp", "W1", 16384.0), ("Wn", "W1", -16384.0)):
         scaled(Z(o), Z(i), s)
-    for t in range(NT):
-        scaled(Z("IdA%d" % t), Z("Id"), -64.0 * (NT - t))
-    scaled(Z("pv"), J128, 1.0 / 2048)
-    keep(Z("T3"), Z("BO"), [[1, 128]], ALU.is_gt, 0.0, 0, -1)
-    keep(Z("T3"), Z("T3"), [[1, 128]], ALU.not_equal, -1.0, 0, -1)
-    cp(G8("T3"), G8("BO"))
+    keep(Z("T3"), Z("BOB"), [[1, 128]], ALU.is_gt, 0.0, 0, -1)
+    keep(Z("T3"), Z("T3"), [[1, 128]], ALU.not_equal, -BIG, 0, -1)
+    take(G8("T3"), G8("BOB"))
     scaled(Z("T3n"), Z("T3"), -1.0)
-    keep(Z("Q"), Z("BOn"), [[-1, 128]], ALU.is_gt, 0.0, 0, 1)
-    keep(Z("Q"), Z("Q"), [[-1, 128]], ALU.not_equal, -2.0, 0, 1)
-    for n in sorted(set(NF)):
-        keep(Z("BOx%d" % NF.index(n)), Z("BOn"), [[0, 8], [-1, 16]], ALU.is_ge, 0.0, 15 - n, 0)
-    ts(Z("RB"), Z("JM"), 0.0, ALU.is_equal, float(2 ** 23), ALU.mult)
+    gfill(H("PV", 0), 0)
+    scaled(H("PV", 1), J128, 1.0 / BIG)
+    scaled(H("PV", 2), one, C("r0"))
+    fill(Z("LT"), 0.0)
+    ts(Z("Wd"), R("J", 0, 240), C("i"), ALU.subtract, 112.0, ALU.is_equal)
+    ts(Z("G64"), Z("J8"), C("g16"), ALU.is_equal)
+    ts(Z("MK"), Z("tq"), C("g16"), ALU.is_equal)
+    lin(R("wc", 0, 1), C("i"), -BIG, 47 * BIG)
+    lin(R("wc", 4, 7), R("J", 0, 3), -16 * BIG, R("wc", 0, 1))
+    for j in range(3):
+        scaled(R("Wc", 64 * j, 64 * j + 64), Z("G64"), R("wc", 4 + j, 5 + j))
+    lin(R("cs", 0, 4), R("J", 0, 4), 1.0 / 16, 1 + M / BIG)
+    scaled(R("cs", 4, 8), R("cs", 0, 4), C("r0"))
+    for n in sorted(set(ONV)):
+        o = "BOx%d" % ONV.index(n)
+        keep(Z(o), Z("BOn"), [[0, 32], [1, 4]], ALU.is_ge, 0.0, min(n, 3) - 4, 0)
+        for a, step in SETS[3:n]:
+            cp(R(o, a, 128, step), R("BOn", a, 128, step))
+    for j in (1, 2):
+        keep(Z("BK%d" % j), Z("BOB"), [[0, 8], [1, 16]], ALU.is_ge, 0.0, -j, 0)
+        scaled(C("n%d" % j), C("r0"), 128.0 * j)
+    ts(C("r3"), C("i"), 3.0, ALU.is_lt)
+    scaled(Z("BO3"), Z("BO"), C("r3"))
+    scaled(Z("BO3n"), Z("BOn"), C("r3"))
+    iota(Z("K1"), [[-1, 2], [0, 32]], 1)
+    gfill(R("ks", 0, 32), 2 ** 24 - 1)
+    scaled(Z("E00"), Z("Id"), C("r0"))
+    ts(Z("RB"), Z("KH"), 512.0, ALU.is_equal, float(2 ** 25), ALU.mult)
+    gfill(Z("K2"), 8192 * 16 * FAR // int(2 * BIG))
     ts(Z("KC"), R("J", 0, 32), 1.0 / 32, ALU.mult, C("i"), ALU.add)
-    ts(R("KC", 0, 32, 16), R("J", 0, 2), 0.0, ALU.mult, 60000.0, ALU.add)
     ts(Z("I32h"), Z("Id"), 32.0, ALU.mult)
-    cp(Z("W16"), Z("W1"))
-    fill(Z("ones"), 1.0)
-    fill(R("esc", 128, XW), 1.0)
-    ts(Z("PC"), Z("tq"), C("i"), ALU.add)
-    ts(Z("DUM"), Z("PC"), float(E + 2), ALU.add)
-    ts(C("emb"), C("r0"), -8192.0, ALU.mult, float(1 - E), ALU.add)
-    ts(C("cu"), C("r0"), 8192.0, ALU.mult, 640.0, ALU.add)
-    ts(Z("CUd"), Z("Id"), C("cu"), ALU.mult)
+    gfill(R("esc", 128, XW), 1)
+    lin(Z("PC"), R("tq", 0, 24), 1.0, C("i"))
+    lin(Z("DUM"), Z("PC"), 1.0, float(E + 2))
+    lin(C("cu"), C("r0"), -10240.0 - E, float(E))
+    scaled(Z("CUd"), Z("Id"), C("cu"))
     for a in range(2):
-        ts(C("s%d" % a), C("i"), 16 * a + 0.5, ALU.add)
+        lin(C("s%d" % a), C("i"), 1.0, 16 * a + 0.5)
+        lin(C("s%d" % (2 + a)), C("i"), 2.0, a + 0.5)
     cp(C("th"), R("thi", 0, 1))
     cp(C("w"), R("hwi", 0, 1))
-    for a in range(2):
-        ts(H("THd", a), Z("Idn"), C("th"), ALU.mult)
-    ts(Z("Ww"), Z("W1"), C("w"), ALU.mult)
-    bulk = send("bulk")
-    sx = {0: send("x0")}
-    sq = {}
-    AW, AS, FW = R("A", 0, E + 1), R("A", 0, E + 130), R("F", 0, E + 1)
+    scaled(Z("THd"), Z("Idn"), C("th"))
+    scaled(R("F", 0, 144), Z("W1"), C("w"))
+    scaled(R("F", 144, FO), Z("BO2"), C("w"))
+    sx = {0: send("bulk")}
+    sq, sa = {}, {}
+    AW, AS, FW = R("A", 0, E + 1), R("A", 0, E + 130), R("F", FO, FO + E + 1)
     bank = ["B1", "B2", "B3"]
     stage = [0]
 
     def ra(h, i):
         return R("raw", 2048 * h + i, 2048 * (h + 1), 16)
 
-    def mo(h, i, n=1):
-        return R("mx", 2048 * h + 128 * i, 2048 * h + 128 * (i + n))
-
-    compact("B7", "E0w", "c16")
+    compact("B7", "E0w", "c16", 2)
     cp(KL("KL", 0), R("B7", 0, 8))
     for t in range(NT):
         n0 = M + 128 * t
-        x, IdA = Xt(t), Z("IdA%d" % t)
+        x = Xt(t)
+        if t < 3:
+            at(t, "snap")
+            sa[t] = send("a%d" % t, "lA%d" % t)
         for h in range(3):
             at(t, "cu%d" % h)
+            cp(H("CU", h), ind(AW if t else R("P32", 0, E + 1), KL("KL", h)))
             if h < 2:
-                first = H("cc", 0) if h == 0 else Z("c1")
-                take(first, ind(AW, KL("KL", h)))
-                cp(H("CU", h), first)
-                cp(Z("c16"), first)
-                compact("B7", "E0w", "c16")
+                cp(H("c16", h), H("CU", h))
+                compact("B7", "E0w", "c16", h)
                 cp(KL("KL", h + 1), R("B7", 0, 8))
-            else:
-                cp(H("CU", h), ind(AW, KL("KL", h)))
+            if h == 2:
+                at(t, "sp")
+                ts(Z("sp"), Z("CU"), n0 - 0.5, ALU.is_ge, R("cs", 4 + t, 5 + t), ALU.max)
             at(t, "raw%d" % h)
             ch = CHH[h]
             for c in range(2048 // ch):
@@ -461,126 +534,176 @@ def build(g, T, topo, rank):
         ts(Z("L0"), Z("KI"), 127, ALU.bitwise_and)
         cp(Z("L0u"), Z("L0"))
         tt(Z("nq"), Z("L0"), Z("PC"), ALU.not_equal)
-        tt(Z("tq"), Z("nq"), Z("DUM"), ALU.mult)
-        tt(Z("nq"), Z("tq"), Z("KI"), ALU.max)
+        tt(R("tq", 0, 24), Z("nq"), Z("DUM"), ALU.mult)
+        tt(Z("nq"), R("tq", 0, 24), Z("KI"), ALU.max)
         cp(Z("SL"), Z("nq"))
         dg = []
         for h in range(3):
             at(t, "wn%d" % h)
-            dg.append(group([(R(bank[h], 0, 256), one, Z("THd"))]
-                            + [(R(bank[h], i, 128, 16), ra(h, i), G8("BOn")) for i in range(1, 16 - NF[h])]))
+            sums = [(R(bank[h], i, 128, 16), ra(h, i), G8("BOn")) for a, step in SETS[:ONV[h]] for i in range(a, 16, step)]
+            dg.append(group([(R(bank[h], 0, 128), one, Z("THd")), sums[:4], sums[4:]]))
         if t > 0:
             s = t - 1
             at(t, "ans")
-            fb = "FB%d" % s
-            FBW = R(fb, 0, E + 1)
-            hops = len([1 for w, c in h1calls if w == "hC%d" % s]) + 1
-            recv(R(fb, 0, M + 128 * t), "aFB%d" % s, [sx[s]] if s else [sx[s], bulk], 2 if s else 6)
-            recv(R("CQ%d" % s, 0, 128), "aCQ%d" % s, [sq[s]], hops)
-            for a in range(2):
-                cp(R("cqu", a, 32, 2), ind(Z("CQ%d" % s), R("INV", 2 * a, 2 * a + 1)))
-            for c in range(2):
-                scaled(R("dd", 256 * c, 256 * c + 256), ind(FBW, R("cqu", 16 * c, 16 * c + 16)), 0.5)
-            for c in range(2):
-                tt(R("da", 256 * c, 256 * c + 256), R("dd", 256 * c, 256 * c + 256), R("B0", 256 * c, 256 * c + 256), ALU.max)
-            key = R("B5", 0, 32)
-            group([(key, Z("I32h"), Z("KC"))]
-                  + [(key, Wsl("Wn", b), R("dd", 32 * b, 32 * b + 32)) for b in range(16)]
-                  + [(key, Wsl("Wp", b), R("da", 32 * b, 32 * b + 32)) for b in range(16)])
-            scan(Z("ks"), Z("RB"), key, 0.0, ALU.add, ALU.min)
-            cp(R("b1", 0, 2), R("ks", 15, 32, 16))
-            ts(R("b2", 0, 2), R("b1", 0, 2), 511, ALU.bitwise_and)
-            cp(R("BL", 0, 2), R("b2", 0, 2))
-            tt(Z("di"), ind(Z("dd"), R("BL", 0, 2)), Z("xo"), ALU.add)
-            cp(ind(Xt(t, XW), R("INV", 0, 2)), Z("di"))
+            hops = 2 if calls["c%d" % s][0][1] in hands else 1
+            recv(H("WQ", s), "aWQ%d" % s, [sq[s]], hops)
+            tt(Z("eq"), ind(H("WQ", s), R("QM", 0, 2)), Z("qb"), ALU.is_equal)
+            group([(R("B6", 384, 448), Z("Id"), Z("K1")),
+                   [(R("B6", 384, 416), Z("BO3n"), Z("eq")), (R("B6", 416, 448), Z("BO3"), Z("eq"))]])
+            tt(Z("dm"), Z("di"), R("B6", 384, 448), ALU.mult)
+            tt(ind(Xt(t, XW), R("INV", 2, 4)), R("dm", 0, 32), R("dm", 32, 64), ALU.add)
             if t < 3:
                 sx[t] = send("x%d" % t)
             store("Y", T.yx[:, 128 * t:128 * t + 128], x, "dx%d" % t, 0)
-        xt = R("B0", 0, 128)
-        group([(xt, Z("Id"), x)])
+        mm(groups[0], [(R("B0", j, 512, 4), Z("Id"), x) for j in range(4)], 1)
+        for h0, n in TSPLIT if t else [(1, 2)]:
+            at(t, "t%d" % h0)
+            take(H("a0", h0, n), ind(x, R("L0u", 8 * h0, 8 * (h0 + n))))
+            st = "B%d" % (4 + stage[0] % 2)
+            stage[0] += 1
+            mm(groups[0], [y for j in range(n) for y in ((H(st, j), Z("Idn"), x), (H(st, j), Z("Id"), H("a0", h0 + j)))], 2)
+            act(H("m0", h0, n), H(st, 0, n), ACT.Abs)
+            mm(groups[0], [y for h in range(h0, h0 + n) for y in ((H("B7", h), one, Z("THd")), (H("B7", h), H("m0", h), Z("BO")))], 2)
+            act(H("sg", 3 + h0, n), H("B7", h0, n), ACT.Sign, bias=0.5, scale=-1.0)
         for h in range(3):
-            at(t, "t%d" % h)
-            D, DT = R(bank[h], 0, 128), R(bank[h], 128, 256)
-            take(H("a0", h), ind(x, KL("L0u", h)))
-            tt(H("m0", h), H("a0", h), xt, ALU.max)
-            for l, r in ((x, "BOn"), (H("a0", h), "BOn"), (H("m0", h), "BO2")):
-                mm(dg[h], DT, l, Z(r))
+            D = R(bank[h], 0, 128)
             at(t, "d%d" % h)
-            brows, frows = list(range(1, 16 - NF[h])), list(range(16 - NF[h], 16))
-            mm(dg[h], D, x, Z("BOx%d" % NF.index(NF[h])))
-            nch = (len(frows) + 3) // 4
+            mm(dg[h], [(D, x, Z("BOx%d" % ONV.index(ONV[h])))])
+            rows = [i for a, step in SETS[ONV[h]:] for i in range(a, 16, step)]
+            nch, o = (len(rows) + 3) // 4, 2048 * h
             for c in range(nch):
-                rows = frows[len(frows) * c // nch:len(frows) * (c + 1) // nch]
+                some = rows[len(rows) * c // nch:len(rows) * (c + 1) // nch]
                 st = "B%d" % (4 + stage[0] % 2)
                 stage[0] += 1
-                for j, i in enumerate(rows):
-                    group([(H(st, j), Z("Id"), ra(h, i)), (H(st, j), Z("Idn"), x)])
-                act(mo(h, rows[0], len(rows)), H(st, 0, len(rows)), ACT.Abs)
-            for i in brows:
-                tt(mo(h, i), ra(h, i), xt, ALU.max)
-            for i in brows + frows:
-                mm(dg[h], R(bank[h], i, 128, 16), mo(h, i), G8("BO2" if i in brows else "BO"))
-            act(H("sg", 2 * h, 2), R(bank[h], 0, 256), ACT.Sign, bias=0.5, scale=-1.0)
+                mm(groups[0], [y for j, i in enumerate(some) for y in ((H(st, j), Z("Id"), ra(h, i)), (H(st, j), Z("Idn"), x))], 2)
+                act(R("mx", o, o + 128 * len(some)), H(st, 0, len(some)), ACT.Abs)
+                mm(dg[h], [(R(bank[h], i, 128, 16), R("mx", o + 128 * j, o + 128 * j + 128), G8("BO")) for j, i in enumerate(some)])
+                o += 128 * len(some)
+            for a, step in SETS[:ONV[h]]:
+                n = 16 // step
+                tt(R("mx", o, o + 128 * n), R("raw", 2048 * h + a, 2048 * (h + 1), step), R("B0", 0, 512, step // 4), ALU.max)
+                mm(dg[h], [(R(bank[h], a + step * j, 128, 16), R("mx", o + j, o + 128 * n, n), G8("BO2")) for j in range(n)])
+                o += 128 * n
+            at(t, "s%d" % h)
+            act(H("sg", h), D, ACT.Sign, bias=0.5, scale=-1.0)
         if t < 3:
             at(t, "q")
-            take(R("F", n0, n0 + 128), x)
-            hops = len([1 for w, c in h1calls if w == "hX%d" % t]) + 1
-            recv(Z("XQ%d" % t), "aXQ%d" % t, [sx[t]], hops)
-            compact("B7", "Ww", "XQ%d" % t)
+            if t:
+                move(R("F", FO + n0, FO + n0 + 128), x, "df%d" % t)
+            fb, ab = "FB%d" % t, "AB%d" % t
+            recv(R(fb, 0, FO + M + 128), "aFB%d" % t, [sx[0]], 3)
+            if t:
+                recv(R(fb, FO + M + 128, FO + n0 + 128), "aFX%d" % t, [sx[t]], 2)
+            recv(Z(ab), "aAB%d" % t, [sa[t]], 2)
+            move(Z(ab), Z("VM"), "da%d" % t, slice(0, 128, 16))
+            group([[(R("B7", 0, 8), Wsl(fb, b), R("X", XW * t + b, XW * t + 128, 16)) for b in range(a, a + 4)]
+                   for a in range(0, 16, 4)])
             cp(Z("QI"), R("B7", 0, 8))
-            ts(Z("QA"), Z("QI"), 1023, ALU.bitwise_and)
+            ts(Z("QA"), Z("QI"), HM - 1, ALU.bitwise_and)
             cp(Z("QL"), Z("QA"))
+            at(t, "co")
+            if t:
+                lin(H("CO", 0), ind(Z(ab), Z("QL")), 1.0, C("n%d" % t))
+            else:
+                take(H("CO", 0), ind(Z(ab), Z("QL")))
         for h in range(3):
             at(t, "h%d" % h)
             U = H("B6", h)
-            group([(U, Z("CUd"), one), (U, one, IdA), (U, H("sg", 2 * h), Z("IdB")), (U, H("sg", 2 * h + 1), IdA)])
+            fresh = [(U, Z("Id2"), H("sp", h)), (U, H("sg", 3 + h), Z("Id2"))] if t + h else []
+            group([(U, Z("CUd"), one)] + fresh + [(U, H("sg", h), Z("Id4"))])
+            cc = H("cc", h) if h else H("c16", 0)
             if h:
-                take(H("cc", h), ind(AW, KL("KL", h)))
-            tt(H("mm", h), H("cc", h), U, ALU.is_ge)
-            ts(H("em", h), H("cc", h), C("emb"), ALU.add, 0.0, ALU.max)
-            act(H("em", h), H("cc", h), ACT.Relu, bias=C("emb"))
-            either()
-            Y = H(bank[h], 2)
-            old = [(Z("BO"), H("mm", j)) for j in range(h)] + [(Z("BOn"), H("em", j)) for j in range(h)]
-            group([(Y, l, r) for l, r in [(Z("Id"), Z("pv"))] + old + [(Z("Q"), H("em", h)), (Z("BO"), H("mm", h))]])
-            act(H("rr", h), Y, ACT.Relu, bias=float(E - n0 - 2048), scale=-2048.0)
-            tt(ind(AS, KL("SL", h)), H("cc", h), H("rr", h), ALU.subtract)
+                take(cc, ind(AW, KL("KL", h)))
+            tt(H("mm", h), cc, U, ALU.is_lt)
+            Wr, Fs = H(bank[h], 1), H(bank[max(h - 1, 0)], 2)
+            group([[(Wr, Z("Id2"), H("PV", 1)), (Wr, Z("T3"), H("sp", h))]] + [(Wr, Z("BOB"), H("mm", j)) for j in range(h + 1)])
+            if h:
+                act(H("nv", h), Wr, ACT.Relu, bias=float(E), scale=-1.0)
+            else:
+                tt(H("nv", h), cc, Wr, ALU.min)
             at(t, "p%d" % h)
-            Pp = H(bank[h] if h < 2 else "B0", 3)
-            group([(Pp, l, r) for l, r in old + [(Z("T3n"), H("em", h)), (Z("T3"), H("mm", h))]])
-            act(Pp, Pp, ACT.Relu, bias=C("r0") if h == 2 else 0.0, scale=-1.0)
-            tt(H("fc", h), H("cc", h), Pp, ALU.mult)
-        if t < 3:
-            at(t, "co")
-            take(Z("CO%d" % t), ind(R("A", 0, 1024), Z("QL")))
-            sq[t] = send("c%d" % t)
-        else:
-            store("Y", T.yp[:, 0:768], R("A", 0, 768), "dy0", 128 * n0 * 4)
-            store("S", T.yp[:, 768:n0], R("A", 768, n0), "dy1", 128 * n0 * 4)
+            group([(Fs, Z("Id2"), H("PV", 2))] * (h // 2) + [(Fs, Z("BOBn"), H("mm", j)) for j in range(h)]
+                  + [(Fs, Z("T3n"), H("mm", h))])
+            tt(H("fc", h), cc, Fs, ALU.min)
+            if h == 2 and t < 3:
+                at(t, "wk")
+                WK = H("B0", 0)
+                group([(WK, Z("E00"), R("A", n0 - 128, n0))] + [(WK, Wsl("E0w", j + 1), H("c16", j)) for j in range(2)]
+                      + [(WK, Z(l), H("mm", j)) for j, l in enumerate(("BOB", "BK1", "BK2"))])
+                take(H("WK", t), WK)
+                sq[t] = send("c%d" % t)
+            at(t, "w%d" % h)
+            if h:
+                tt(ind(AS, KL("SL", h)), cc, H("nv", h), ALU.subtract)
+            else:
+                cp(ind(AS, KL("SL", h)), H("nv", h))
+        if t == 3:
+            half = (n0 - 128) // 2
+            store("Y", T.yp[:, 0:half], R("A", 0, half), "dy0", 128 * (n0 - 128) * 4)
+            store("S", T.yp[:, half:n0 - 128], R("A", half, n0 - 128), "dy1", 128 * (n0 - 128) * 4)
         at(t, "link")
-        group([(H("B4", 0), Wsl("W16", 0), H("fc", h)) for h in range(3)])
+        LK = R("B1", 384, 448)
+        group([(LK, H("mm", j), R("Wc", 64 * j, 64 * j + 64)) for j in range(3)] + [(LK, H("fc", j), Z("G64")) for j in range(3)])
+        if t < 3:
+            tt(Z("RR"), Z("MK"), LK, ALU.mult)
+            group([[(R("B2", 384, 392), R("Wd", 112 - 16 * a, 240 - 16 * a), R("RR", 8 * a, 8 * a + 8)) for a in range(8)]])
+            cp(KL("KL", 0), R("B2", 384, 392))
+        at(t, "lw")
+        ts(G8("LT"), R("B1", 384, 448, 8), 1.0 / 32, ALU.mult)
+        group([(H("B4", 0), Z("LT"), Z("I32h"))])
         tt(R("A", n0, n0 + 128), R("A", n0, n0 + 128), H("B4", 0), ALU.add)
+        if t == 2:
+            store("Y", T.yp[:, n0:n0 + 128], R("A", n0, n0 + 128), "dy3", 128 * 512)
         if t == 3:
             store("Y", T.yp[:, n0:E], R("A", n0, E), "dy2", 128 * 512)
             break
-        group([(R("B5", 0, 8), Wsl("W16", b), R("fc", 128 * h + b, 128 * h + 128, 16)) for h in range(3) for b in range(16)])
-        cp(KL("KL", 0), R("B5", 0, 8))
         at(t, "ask")
-        Zp = H("B6", 3)
-        group([(Zp, Z("BO"), H("mm", j)) for j in range(3)] + [(Zp, Z("BOn"), H("em", j)) for j in range(3)])
+        Zp = H("B5", 3)
+        group([(Zp, Z("BO"), H("mm", j)) for j in range(3)])
+        ts(R("esc", 0, 128), Zp, 0.5, ALU.is_lt)
         act(R("esc", 0, 128), Zp, ACT.Relu, bias=1.0, scale=-1.0)
-        scan(Z("cnt"), Z("ones"), Z("esc"), 0.0, ALU.mult, ALU.add)
-        for a in range(2):
-            act(Z("junk"), Z("cnt"), ACT.Sign, bias=C("s%d" % a), scale=-1.0, acc=R("acc", a, a + 1))
-        ts(R("INV", 0, 2), R("acc", 0, 2), 0.5, ALU.mult, XW / 2.0, ALU.add)
-        ts(R("INV", 2, 3), R("acc", 1, 2), 0.5, ALU.mult, XW / 2.0, ALU.add)
-        for a in range(2):
-            scaled(R("xz", a, 32, 2), ind(Xt(t, XW), R("INV", 2 * a, 2 * a + 1)), 0.5)
-        for i in range(16):
-            group([(R("B0", i, 512, 16), Z("Id"), Z("xz"))])
-        ts(Z("xo"), ind(Xt(t + 1, XW), R("INV", 0, 2)), 0.5, ALU.mult, -0.25, ALU.add)
-        act(Z("xo"), ind(Xt(t + 1, XW), R("INV", 0, 2)), ACT.Identity, bias=-0.25, scale=0.5)
         either()
+        scan(Z("cnt"), Z("ones"), Z("esc"), 0.0, ALU.mult, ALU.add)
+        for k in range(2):
+            at(t, "ask%d" % k)
+            for a in range(2 * k, 2 * k + 2):
+                act(R("junk", XW * a, XW * a + XW), Z("cnt"), ACT.Sign, bias=C("s%d" % a), scale=-1.0, acc=R("acc", a, a + 1))
+            ts(R("INV", 2 * k, 2 * k + 2), R("acc", 2 * k, 2 * k + 2), 0.5, ALU.mult, XW / 2.0, ALU.add)
+        at(t, "xz")
+        scaled(Z("xz"), ind(Xt(t, XW), R("INV", 0, 2)), 0.5)
+        dif = group([(Z("B0"), H("PV", 0), R("F", FO, FO + 512)), [(R("B0", i, 512, 16), Z("Idn"), Z("xz")) for i in range(16)]])
+        lin(Z("xo"), ind(Xt(t + 1, XW), R("INV", 2, 4)), 0.5, -0.25)
+        at(t, "qs")
+        QS = R("B3", 384, 416)
+        hashed = [(R("B3", 384 + 16 * a, 400 + 16 * a), R("FB%d" % t, 144, FO), R("xz", a, 32, 2)) for a in range(2)]
+        mm(groups[0], hashed, 1)
+        lin(Z("qr"), QS, 1.0, 128.0 * HM + HM / 2 + 0.5)
+        group([[(QS, Z("Idn"), Z("qr"))] + hashed])
+        lin(Z("qb"), QS, 1.0, 129.0 * HM)
+        at(t, "near")
+        FBW = R("FB%d" % t, FO, FO + E + 1)
+        cp(Z("cqu"), ind(Z("CO"), R("INV", 0, 2)))
+        at(t, "qm")
+        cp(Z("cq6"), Z("cqu"))
+        group([[(R("B3", 448, 450), Wsl("E0w", b), R("cq6", 2 * b, 2 * b + 2)) for b in range(a, a + 4)] for a in range(0, 16, 4)])
+        ts(R("QM", 0, 2), R("B3", 448, 450), -float(n0), ALU.add)
+        at(t, "near")
+        for c in range(2):
+            scaled(R("dd", 256 * c, 256 * c + 256), ind(FBW, R("cqu", 16 * c, 16 * c + 16)), 0.5)
+            mm(dif, [(R("B0", 256 * c, 256 * c + 256), Z("Id"), R("dd", 256 * c, 256 * c + 256))])
+        act(Z("da"), Z("B0"), ACT.Abs)
+        key, hole = R("B4", 0, 32), R("B4", 32, 64)
+        sums = [(Wsl("Wn", b), R("dd", 32 * b, 32 * b + 32)) for b in range(16)]
+        gaps = [(Wsl("Wp", b), R("da", 32 * b, 32 * b + 32)) for b in range(16)]
+        group([[(R("B4", 0, 64), Z("Id"), Z("KH")), (hole, Z("Id4"), Z("K2")), (key, Z("I32h"), Z("KC"))]]
+              + [[(hole, l, r) for l, r in part] for part in (sums[:8], sums[8:])] + [[(key, l, r) for l, r in gaps]])
+        scan(R("ks", 32, 96), Z("RB"), R("B4", 0, 64), 0.0, ALU.add, ALU.min)
+        tt(R("ks", 79, 96, 16), R("ks", 79, 96, 16), R("B4", 0, 32, 16), ALU.add)
+        tt(R("b1", 0, 4), R("ks", 47, 96, 16), R("ks", 15, 64, 16), ALU.min)
+        ts(R("b2", 0, 4), R("b1", 0, 4), 511, ALU.bitwise_and)
+        cp(R("BL", 0, 4), R("b2", 0, 4))
+        for a in range(2):
+            tt(R("di", 32 * a, 32 * a + 32), ind(Z("dd"), R("BL", 2 * a, 2 * a + 2)), Z("xo"), ALU.add)
     return ops, nls
 
 
@@ -592,7 +715,7 @@ def hazards(ops):
         for wr, r in both:
             if SCRATCH[r[0]][0] == "psum":
                 st = runs.setdefault(r[0], {"key": None, "cur": [], "old": [], "by": {}})
-                key = (o["e"], o["grp"])
+                key = (o["e"] if len(o["alt"]) == 1 else j, o["grp"])
                 if o["grp"] is not None and o["grp"] in st["by"] and st["key"] != key:
                     raise ValueError("group cut on " + r[0])
                 if st["key"] != key:
@@ -606,8 +729,9 @@ def hazards(ops):
                     st["cur"].append(j)
                 if o["e"] == "P":
                     continue
-            for (a, b, i, w2) in hist.get(r[0], []):
-                if i != j and a < r[2] and r[1] < b and (wr or w2):
+            for (a, b, i, w2, sp) in hist.get(r[0], []):
+                apart = sp == r[3] and (a - r[1]) % sp != 0
+                if i != j and a < r[2] and r[1] < b and (wr or w2) and not apart:
                     pr[i] = pr.get(i, False) or w2
         for wr, r in both:
             if SCRATCH[r[0]][0] == "psum" and o["e"] == "P":
@@ -616,85 +740,163 @@ def hazards(ops):
             lst = hist.setdefault(r[0], [])
             if wr and r[3] == 1:
                 lst[:] = [z for z in lst if not (r[1] <= z[0] and z[1] <= r[2])]
-            lst.append((r[1], r[2], j, wr))
+            lst.append((r[1], r[2], j, wr, r[3]))
         preds.append(pr)
     return preds
 
 
-def schedule(ops, preds, fig):
-    n = len(ops)
-    dep = [list(p.keys()) + o["after"] for p, o in zip(preds, ops)]
-    succ = [[] for _ in range(n)]
-    for j in range(n):
-        for i in dep[j]:
-            succ[i].append(j)
-    cost = [{e: price(v[1], fig) for e, v in o["alt"].items()} for o in ops]
-    lat = [price(o["lat"], fig) for o in ops]
+def figures(ops, preds, fig):
+    cost = [{e: price(v[1], fig) + (fig["fix"] if e in "VS" else 0.0) for e, v in o["alt"].items()} for o in ops]
+    lat = [o["lat"][0] / fig["bw"] + o["lat"][1] * fig[o["lat"][2]] for o in ops]
+    pre = [[(i, 0.0 if o["e"] == "N" or ops[i]["e"] == o["e"] == "P" else fig["sync"]) for i in list(p) + o["after"]]
+           for o, p in zip(ops, preds)]
+    return cost, lat, pre
 
-    def gap(i, k):
-        return 0.0 if (ops[i]["e"] == ops[k]["e"] == "P" or ops[k]["e"] == "N") else fig["sync"]
-    prio = [0.0] * n
-    for j in range(n - 1, -1, -1):
-        prio[j] = min(cost[j].values()) + lat[j] + max([gap(j, k) + prio[k] for k in succ[j]] + [0.0]) - 0.001 * j
-    left = [len(d) for d in dep]
-    prio = [p + BOOST.get(o["d"][1], 0.0) for p, o in zip(prio, ops)]
-    ready, start, eng, end = [0.0] * n, [0.0] * n, [None] * n, [None] * n
-    now, order, pool = {e: 0.0 for e in "VSPGY"}, [], {e: [] for e in "VSPGY"}
-    todo = {e: sorted([j for j in range(n) if list(cost[j]) == [e]], key=lambda j: -prio[j]) for e in now}
-    held = {e: 0.0 for e in now}
 
-    def place(j, e, t0):
-        order.append(j)
-        start[j], eng[j], end[j] = t0, e, t0 + cost[j][e] + lat[j]
-        for k in succ[j]:
-            ready[k] = max(ready[k], end[j] + gap(j, k))
-            left[k] -= 1
-            if left[k] == 0:
-                offer(k)
-
-    def offer(j):
-        if ops[j]["e"] == "N":
-            place(j, "N", ready[j])
-        else:
-            for e in cost[j]:
-                pool[e].append(j)
-
-    def soon(u, depth, memo):
-        if u not in memo:
-            r = ready[u]
-            if left[u] and depth == 0:
-                r = 1e12
-            elif left[u]:
-                for i in dep[u]:
-                    if end[i] is None:
-                        s = soon(i, depth - 1, memo)
-                        r = max(r, min(max(s, now.get(e, 0.0)) + c for e, c in cost[i].items()) + lat[i] + gap(i, u))
-            memo[u] = r
-        return memo[u]
-    for j in [j for j in range(n) if left[j] == 0]:
-        offer(j)
-    while len(order) < n:
-        e = min(now, key=lambda q: now[q])
-        t0, j = now[e], None
-        can = [k for k in pool[e] if ready[k] <= t0 + LOOK]
-        if can:
-            todo[e] = [u for u in todo[e] if end[u] is None]
-            memo = {}
-            urgent = [(u, soon(u, DEPTH, memo)) for u in todo[e][:AHEAD] if u not in can]
-            for k in sorted(can, key=lambda k: -prio[k] + (PEN if e == "V" and len(cost[k]) > 1 else 0.0)):
-                fin = max(t0, ready[k]) + cost[k][e]
-                if held[e] > 1000 or all(prio[u] < prio[k] + SLACK or HOLD * (r - t0) >= fin - r for u, r in urgent):
-                    j = k
-                    break
-        if j is None:
-            now[e] = t0 + 30.0
-            held[e] += 30.0 if can else 0.0
+def ordered(key, before):
+    done, out = [False] * len(key), []
+    for j in sorted(range(len(key)), key=lambda j: key[j]):
+        if done[j]:
             continue
-        for e2 in cost[j]:
-            pool[e2].remove(j)
-        now[e], held[e] = max(t0, ready[j]) + cost[j][e], 0.0
-        place(j, e, max(t0, ready[j]))
-    return order, eng, start, max(end)
+        stack = [j]
+        while stack:
+            u = stack[-1]
+            miss = [] if done[u] else [i for i, gap in before[u] if not done[i]]
+            if miss:
+                stack += miss
+            else:
+                if not done[u]:
+                    done[u] = True
+                    out.append(u)
+                stack.pop()
+    return out
+
+
+def lay(seq, before, cost, head, tail, lean):
+    start, end, eng = [0.0] * len(seq), [0.0] * len(seq), [None] * len(seq)
+    lines = {e: [] for e in "VSPGYN"}
+    for j in seq:
+        r = 0.0
+        for i, gap in before[j]:
+            if end[i] + gap > r:
+                r = end[i] + gap
+        r += head[j]
+        best = None
+        for e, c in cost[j].items():
+            line, t = lines[e], r
+            k = m = len(line)
+            while k and line[k - 1][1] > r:
+                k -= 1
+            while k < m and line[k][0] < t + c:
+                t = line[k][1]
+                k += 1
+            key = t + c + (lean[j] if e == "V" else 0.0)
+            if best is None or key < best[0]:
+                best = (key, t, k, e, c)
+        key, t, k, e, c = best
+        if e != "N":
+            lines[e].insert(k, (t, t + c))
+        start[j], eng[j], end[j] = t - head[j], e, t + c + tail[j]
+    return start, end, eng
+
+
+def replay(order, eng, cost, lat, pre, mean=0.0):
+    end, now = [0.0] * len(order), {e: 0.0 for e in "VSPGYN"}
+    for j in order:
+        e = eng[j]
+        r = now[e]
+        for i, gap in pre[j]:
+            if end[i] + gap > r:
+                r = end[i] + gap
+        r += cost[j][e]
+        if e != "N":
+            now[e] = r
+        end[j] = r + lat[j]
+    return max(end) + mean * sum(end) / len(end)
+
+
+def blocked(order, eng, cost, lat, pre):
+    end, now, last, why = [0.0] * len(order), {e: 0.0 for e in "VSPGYN"}, {}, [None] * len(order)
+    for j in order:
+        e = eng[j]
+        r, why[j] = now[e], (last.get(e), True)
+        for i, gap in pre[j]:
+            if end[i] + gap > r:
+                r, why[j] = end[i] + gap, (i, False)
+        r += cost[j][e]
+        if e != "N":
+            now[e], last[e] = r, j
+        end[j] = r + lat[j]
+    j, out = end.index(max(end)), []
+    while j is not None:
+        i, queued = why[j]
+        if queued and i is not None:
+            out.append((i, j))
+        j = i
+    return out
+
+
+def schedule(ops, preds):
+    n = len(ops)
+    sets = [figures(ops, preds, f) for f in FIGS]
+    cost, lat, pre = sets[0]
+    suc, zero, parts, seed = [[] for _ in range(n)], [0.0] * n, {}, [SEED]
+    for j in range(n):
+        parts.setdefault(ops[j]["d"], []).append(j)
+        for i, gap in pre[j]:
+            suc[i].append((j, gap))
+    names = list(parts)
+
+    def pick(seq):
+        seed[0] = (seed[0] * 1103515245 + 12345) % 2 ** 31
+        return seq[(seed[0] >> 8) % len(seq)]
+
+    def judge(key, lean):
+        start, end, eng = lay(ordered(key, pre), pre, cost, zero, lat, lean)
+        order = sorted(range(n), key=lambda j: start[j])
+        return sum(replay(order, eng, *s, MEAN) / f["norm"] for s, f in zip(sets, FIGS)), start, end, order, eng
+    key = [0.0] * n
+    for j in range(n - 1, -1, -1):
+        key[j] = min([key[k] - gap for k, gap in suc[j]] + [0.0]) - min(cost[j].values()) - lat[j]
+    lean, free = [LEAN] * n, [j for j in range(n) if len(cost[j]) > 1]
+    cur = best = judge(key, lean)
+    held = None
+    for r in range(ROUNDS):
+        how, tilt = pick(range(24)), lean
+        if how >= 12:
+            held = held or [blocked(cur[3], cur[4], *s) for s in sets]
+            (i, j), new, d = pick(pick(held)), list(key), pick([10, 100, 300, 1000])
+            if len(cost[i]) > 1 and how % 3:
+                tilt = list(lean)
+                tilt[i] = 5000.0 if cur[4][i] == "V" else -5000.0
+            elif how % 3:
+                new[j] = min(new[i], new[j]) - d
+            else:
+                new[i] = max(new[i], new[j]) + d
+        elif how == 0:
+            new = [-v for v in lay(ordered([-v for v in cur[2]], suc), suc, cost, lat, zero, lean)[1]]
+        elif how > 9:
+            new, tilt, a = key, list(lean), pick(range(len(free)))
+            for j in free[a:a + pick([1, 1, 2])]:
+                tilt[j] = pick([-3000.0, 0.0, LEAN, 3000.0])
+        else:
+            new = list(cur[1] if how == 1 else key)
+            for _ in range(pick([1, 1, 2, 4])):
+                name, d = pick(names), pick([-1, 1]) * pick([100, 200, 400, 800, 1500, 3000])
+                some = [name] if pick([0, 1]) else [k for k in names if k[1] == name[1]]
+                a, b = 0, n
+                if pick(range(5)) < 2:
+                    a = pick(range(len(parts[name])))
+                    b = a + pick([1, 2, 4, 8])
+                for k in some:
+                    for j in parts[k][a:b]:
+                        new[j] += d
+        res = judge(new, tilt)
+        if res[0] <= cur[0] + SLACK * pick(range(100)) / 100 * (1 - r / ROUNDS):
+            cur, key, lean, held = res, new, tilt, None
+            if cur[0] < best[0]:
+                best = cur
+    return best[3], best[4]
 
 
 def emit(g, T, ops, preds, order, nls):
@@ -762,6 +964,8 @@ def emit(g, T, ops, preds, order, nls):
             else:
                 q.wait_ge(T.sem[ESEM[p["e"]]], count[i])
         ins = o["alt"][o["e"]][0]()
+        if ins is None:
+            continue
         if o["sem"] is not None:
             ins.then_inc(T.sem[o["sem"][0]], o["sem"][1])
         elif j in target:
@@ -777,8 +981,7 @@ def rank_program(g, core, T, topo):
         for r in range(len(T.cores)):
             if core not in topo.cores_of(T.cores[r]):
                 continue
-            me, calls, h1, h1calls, hb, hbcalls = plan(T, topo, r)
-            mine = h1calls if core == h1 else hbcalls if core == hb else []
+            mine = plan(T, topo, r)[2].get(core, [])
             if mine:
                 arr, seen, n = arrivals(T, topo, core), [], 0
                 for w, c in mine:
@@ -791,8 +994,8 @@ def rank_program(g, core, T, topo):
     ops, nls = build(g, T, topo, rank)
     preds = hazards(ops)
     if "o" not in _ORDER:
-        _ORDER["o"] = schedule(ops, preds, FIG)
-    order, eng = _ORDER["o"][:2]
+        _ORDER["o"] = schedule(ops, preds)
+    order, eng = _ORDER["o"]
     for o, e in zip(ops, eng):
         o["e"] = e
     emit(g, T, ops, preds, order, nls)

@@ -5,20 +5,23 @@ ALU = AluOpType
 ACT = ActivationFunctionType
 M, P, NT, E, HM = 1152, 128, 4, 1664, 1024
 FO = 272
-FAR = 64
+FAR = 48
 XW = 160
 SETS = [(3, 4), (2, 4), (1, 4), (4, 8), (8, 16)]
-ONV = [3, 3, 2]
-CHH = [1024, 512, 512]
+ONV = [3, 3, 3]
+CHH = [[64, 32, 16, 16], [64, 32, 16, 16], [32, 32, 32, 16, 16]]
 TSPLIT = [(0, 3)]
 BIG = 2048.0
-FIGS = [{"cyc": c, "gath": c * ga, "scat": c * sc, "pe": c / 2, "sync": sync, "fix": fix, "hop": hop, "dma": 2000.0, "bw": bw,
+FIGS = [{"cyc": c, "gath": c * ga, "scat": c * sc, "pe": c * 0.53, "sync": sync, "fix": fix, "hop": hop, "dma": 2000.0, "bw": bw,
          "send": 400.0, "norm": norm}
-        for c, ga, sc, sync, fix, hop, bw, norm in ((0.9, 1.56, 3.8, 130.0, 30.0, 2300.0, 200.0, 75.0),
-                                                    (0.83, 1.3, 3.0, 170.0, 30.0, 2900.0, 150.0, 75.0),
-                                                    (1.15, 1.95, 5.0, 130.0, 30.0, 2000.0, 200.0, 95.0),
-                                                    (1.1, 1.15, 4.5, 120.0, 40.0, 2000.0, 200.0, 82.0))]
-LEAN, SLACK, ROUNDS, SEED, MEAN = 500.0, 5.0, 10000, 1, 0.3
+        for c, ga, sc, sync, fix, hop, bw, norm in ((0.95, 1.56, 3.8, 130.0, 18.0, 2300.0, 200.0, 73.0),
+                                                    (0.86, 1.3, 3.0, 160.0, 20.0, 2900.0, 150.0, 73.0),
+                                                    (1.17, 1.95, 5.0, 130.0, 15.0, 2000.0, 200.0, 94.0),
+                                                    (1.12, 1.15, 4.5, 120.0, 25.0, 2000.0, 200.0, 80.0))]
+LEAN, SLACK, ROUNDS, SEED, MEAN, FAIL, SHORT = 1500.0, 12.0, 1500, 51, 0.2, 400.0, 600.0
+SWAPS = [(30000, 12.0), (20000, 5.0), (20000, 4.0)]
+SFIX = 2.5
+FARS = [0, 0, 0, 1, 2, 4, 8]
 SAME_WAR = True
 
 F32, BF, I32, U16, F16 = "float32", "bfloat16", "int32", "uint16", "float16"
@@ -35,46 +38,46 @@ _decl("P32", 1672, I32)
 _decl("F FB0 FB1 FB2", FO + 1680, BF)
 _decl("AB0 AB1 AB2 VM", HM, F32)
 _decl("X", 4 * XW, BF)
-_decl("dd da", 512, BF)
+_decl("dd", 1024, BF)
 _decl("XQ", 384, BF)
 _decl("ones esc cnt", XW, BF)
-_decl("junk", 4 * XW, BF)
-_decl("J", 256, BF)
+_decl("junk", 2 * XW, BF)
+_decl("J", 144, BF)
 _decl("CO", XW, F32)
 _decl("WQ WK", 384, F32)
-_decl("R1V tB E00", 128, F32)
+_decl("R1V tB", 128, F32)
 _decl("hwi thi", 4, I32)
 _decl("pi", 8, I32)
-_decl("col qb", 32, F32)
-_decl("RB", 64, F32)
+_decl("col qb RB", 32, F32)
 _decl("ks", 96, F32)
 _decl("NV", 512, F32)
-_decl("J16 Id Idn Id2 Id4 CUd BO BOn BO2 BO3 BO3n BOB BOBn BK1 BK2 BOx0 BOx1 BOx2 T3 T3n THd", 128, BF)
-_decl("W1 Wp Wn", 144, BF)
+_decl("J16 Id Idn Id2 Id4 CUd BO BOn BO2 BO3 BO3n BOB BOBn BOH BK1 BK2 BOx0 BOx1 BOx2 T3 T3n THd", 128, BF)
+_decl("W1 Wp", 144, BF)
 _decl("I32h LT", 128, F16)
 _decl("E0w", 144, F16)
-_decl("Wd", 240, F16)
+_decl("Wd", 48, F16)
 _decl("KC", 32, F16)
 _decl("RR", 64, F16)
-_decl("G64 MK tq", 64, F32)
-_decl("Wc", 192, BF)
+_decl("MK tq", 64, F32)
+_decl("G64", 64, F16)
+_decl("Wc", 128, BF)
 _decl("J8", 64, BF)
 _decl("PC DUM nq", 24, F32)
 _decl("KI L0", 24, I32)
 _decl("KL L0u SL", 24, U16)
 _decl("QI QA b1 b2 qc", 8, I32)
 _decl("QL INV BL QM", 8, U16)
-_decl("acc cs wc kn", 8, F32)
+_decl("acc cs", 8, F32)
 _decl("CU", 384, U16)
 _decl("raw mx", 6144, BF)
-_decl("cc nv fc", 384, F32)
+_decl("cc nv", 384, F32)
+_decl("fc", 384, F16)
 _decl("a0 m0 mm sp PV", 384, BF)
 _decl("sg", 768, BF)
-_decl("c16", 384, F16)
+_decl("c16", 448, F16)
 _decl("cqu", 32, U16)
 _decl("xo xz K2 qr eq", 32, BF)
 _decl("KH K1 dm", 64, BF)
-_decl("cq6", 32, F16)
 _decl("di", 64, I32)
 _decl("B0 B1 B2 B3 B4 B5 B6 B7", 512, F32, "psum")
 
@@ -180,6 +183,8 @@ def arrivals(T, topo, core):
 
 
 def ap_of(T, r):
+    if len(r) > 4:
+        return T[r[0]][r[4]:r[4] + 32, r[1]:r[2]]
     if r[3] == 1:
         return T[r[0]][:, r[1]:r[2]]
     return T[r[0]][:, r[1]:r[2]:r[3]]
@@ -392,8 +397,11 @@ def build(g, T, topo, rank):
     def G8(name):
         return R(name, 0, 128, 16)
 
-    def compact(bank, wide, src, h=0):
-        group([[(R(bank, 0, 8), Wsl(wide, b), R(src, 128 * h + b, 128 * h + 128, 16)) for b in range(16)]])
+    def C16(h):
+        return R("c16", 160 * h, 160 * h + 128)
+
+    def compact(h, n=8):
+        group([[(R("B7", 0, n), Wsl("E0w", b), R("c16", 160 * h + b, 160 * h + 16 * n, 16)) for b in range(16)]])
 
     load("Y", R("P32", 1024, M), T.ptr[:, 1024:M], "dp0")
     load("S", R("P32", 0, 512), T.ptr[:, 0:512], "dp1")
@@ -409,9 +417,9 @@ def build(g, T, topo, rank):
     J128, one = R("J", 0, 128), R("ones", 0, 128)
     fill(Z("ones"), 1.0)
     iota(R("pi", 0, 1), [[0, 1]], 0, 1)
-    iota(Z("J"), [[1, 256]], 0)
+    iota(Z("J"), [[1, 144]], 0)
     iota(Z("J16"), [[16, 8], [0, 16]], 0)
-    iota(Z("KH"), [[0, 4], [512, 16]], 0)
+    iota(Z("KH"), [[0, 2], [1024, 16], [0, 2]], 0)
     iota(R("NV", 0, 128), [[1, 128]], M)
     iota(R("NV", 128, 512), [[1, 384]], M + 128)
     iota(Z("tq"), [[0, 8], [16, 8]], 0)
@@ -439,7 +447,7 @@ def build(g, T, topo, rank):
     scaled(R("A", E - 128, E), one, C("hi"))
     gfill(R("A", E, 1800), E)
     scaled(Z("R1V"), R("NV", 0, 128), C("r1"))
-    cp(H("c16", 2), R("P32", 1024, M))
+    cp(C16(2), R("P32", 1024, M))
     ts(Z("tB"), R("P32", 1024, M), C("nr1"), ALU.mult)
     tt(R("P32", 1024, M), Z("tB"), Z("R1V"), ALU.max)
     for a, b in ((0, 256), (256, 512), (512, 768), (768, 1024), (1024, M)):
@@ -447,7 +455,8 @@ def build(g, T, topo, rank):
     ts(Z("Id"), J128, C("p"), ALU.is_equal)
     ts(Z("BO"), Z("J16"), C("g16"), ALU.is_equal)
     for o, i, s in (("BOn", "BO", -1.0), ("BO2", "BO", 2.0), ("BOB", "BO", BIG), ("BOBn", "BO", -BIG), ("Idn", "Id", -1.0),
-                    ("Id2", "Id", BIG), ("Id4", "Id", 2 * BIG), ("Wp", "W1", 16384.0), ("Wn", "W1", -16384.0)):
+                    ("BOH", "BO", -8 * BIG),
+                    ("Id2", "Id", BIG), ("Id4", "Id", 2 * BIG), ("Wp", "W1", 32768.0)):
         scaled(Z(o), Z(i), s)
     keep(Z("T3"), Z("BOB"), [[1, 128]], ALU.is_gt, 0.0, 0, -1)
     keep(Z("T3"), Z("T3"), [[1, 128]], ALU.not_equal, -BIG, 0, -1)
@@ -457,13 +466,12 @@ def build(g, T, topo, rank):
     scaled(H("PV", 1), J128, 1.0 / BIG)
     scaled(H("PV", 2), one, C("r0"))
     fill(Z("LT"), 0.0)
-    ts(Z("Wd"), R("J", 0, 240), C("i"), ALU.subtract, 112.0, ALU.is_equal)
+    ts(Z("Wd"), R("J", 0, 48), C("i"), ALU.subtract, 16.0, ALU.is_equal)
     ts(Z("G64"), Z("J8"), C("g16"), ALU.is_equal)
     ts(Z("MK"), Z("tq"), C("g16"), ALU.is_equal)
-    lin(R("wc", 0, 1), C("i"), -BIG, 47 * BIG)
-    lin(R("wc", 4, 7), R("J", 0, 3), -16 * BIG, R("wc", 0, 1))
-    for j in range(3):
-        scaled(R("Wc", 64 * j, 64 * j + 64), Z("G64"), R("wc", 4 + j, 5 + j))
+    for j in range(2):
+        lin(C("c%d" % j), C("i"), -BIG, (31 - 16 * j) * BIG)
+        ts(R("Wc", 64 * j, 64 * j + 64), Z("G64"), C("c%d" % j), ALU.mult)
     lin(R("cs", 0, 4), R("J", 0, 4), 1.0 / 16, 1 + M / BIG)
     scaled(R("cs", 4, 8), R("cs", 0, 4), C("r0"))
     for n in sorted(set(ONV)):
@@ -477,21 +485,20 @@ def build(g, T, topo, rank):
     ts(C("r3"), C("i"), 3.0, ALU.is_lt)
     scaled(Z("BO3"), Z("BO"), C("r3"))
     scaled(Z("BO3n"), Z("BOn"), C("r3"))
-    iota(Z("K1"), [[-1, 2], [0, 32]], 1)
+    iota(Z("K1"), [[1, 2], [0, 32]], -1)
     gfill(R("ks", 0, 32), 2 ** 24 - 1)
-    scaled(Z("E00"), Z("Id"), C("r0"))
-    ts(Z("RB"), Z("KH"), 512.0, ALU.is_equal, float(2 ** 25), ALU.mult)
-    gfill(Z("K2"), 8192 * 16 * FAR // int(2 * BIG))
-    ts(Z("KC"), R("J", 0, 32), 1.0 / 32, ALU.mult, C("i"), ALU.add)
+    ts(Z("RB"), R("KH", 0, 64, 2), 1024.0, ALU.is_equal, float(2 ** 25), ALU.mult)
+    gfill(Z("K2"), 16384 * 16 * FAR // int(2 * BIG))
+    scaled(C("i2"), C("i"), 2.0)
+    ts(Z("KC"), R("J", 0, 32), 1.0 / 16, ALU.mult, C("i2"), ALU.add)
     ts(Z("I32h"), Z("Id"), 32.0, ALU.mult)
     gfill(R("esc", 128, XW), 1)
     lin(Z("PC"), R("tq", 0, 24), 1.0, C("i"))
     lin(Z("DUM"), Z("PC"), 1.0, float(E + 2))
-    lin(C("cu"), C("r0"), -10240.0 - E, float(E))
+    lin(C("cu"), C("r0"), -3 * BIG - E, BIG + E)
     scaled(Z("CUd"), Z("Id"), C("cu"))
     for a in range(2):
         lin(C("s%d" % a), C("i"), 1.0, 16 * a + 0.5)
-        lin(C("s%d" % (2 + a)), C("i"), 2.0, a + 0.5)
     cp(C("th"), R("thi", 0, 1))
     cp(C("w"), R("hwi", 0, 1))
     scaled(Z("THd"), Z("Idn"), C("th"))
@@ -506,7 +513,7 @@ def build(g, T, topo, rank):
     def ra(h, i):
         return R("raw", 2048 * h + i, 2048 * (h + 1), 16)
 
-    compact("B7", "E0w", "c16", 2)
+    compact(2)
     cp(KL("KL", 0), R("B7", 0, 8))
     for t in range(NT):
         n0 = M + 128 * t
@@ -518,17 +525,19 @@ def build(g, T, topo, rank):
             at(t, "cu%d" % h)
             cp(H("CU", h), ind(AW if t else R("P32", 0, E + 1), KL("KL", h)))
             if h < 2:
-                cp(H("c16", h), H("CU", h))
-                compact("B7", "E0w", "c16", h)
+                cp(C16(h), H("CU", h))
+                compact(h, 10 if t and not h else 8)
                 cp(KL("KL", h + 1), R("B7", 0, 8))
+                if t and not h:
+                    ts(R("QM", 0, 2), R("B7", 8, 10), 128.0 - n0, ALU.add)
             if h == 2:
                 at(t, "sp")
                 ts(Z("sp"), Z("CU"), n0 - 0.5, ALU.is_ge, R("cs", 4 + t, 5 + t), ALU.max)
             at(t, "raw%d" % h)
-            ch = CHH[h]
-            for c in range(2048 // ch):
-                take(R("raw", 2048 * h + ch * c, 2048 * h + ch * (c + 1)),
-                     ind(FW, R("CU", 128 * h + ch // 16 * c, 128 * h + ch // 16 * (c + 1))))
+            a = 128 * h
+            for n in CHH[h]:
+                take(R("raw", 16 * a, 16 * (a + n)), ind(FW, R("CU", a, a + n)))
+                a += n
         at(t, "sl")
         ts(Z("KI"), Z("KL"), 1.0 + 1.0 / 3200, ALU.mult)
         ts(Z("L0"), Z("KI"), 127, ALU.bitwise_and)
@@ -549,9 +558,9 @@ def build(g, T, topo, rank):
             recv(H("WQ", s), "aWQ%d" % s, [sq[s]], hops)
             tt(Z("eq"), ind(H("WQ", s), R("QM", 0, 2)), Z("qb"), ALU.is_equal)
             group([(R("B6", 384, 448), Z("Id"), Z("K1")),
-                   [(R("B6", 384, 416), Z("BO3n"), Z("eq")), (R("B6", 416, 448), Z("BO3"), Z("eq"))]])
+                   [(R("B6", 384, 416), Z("BO3"), Z("eq")), (R("B6", 416, 448), Z("BO3n"), Z("eq"))]])
             tt(Z("dm"), Z("di"), R("B6", 384, 448), ALU.mult)
-            tt(ind(Xt(t, XW), R("INV", 2, 4)), R("dm", 0, 32), R("dm", 32, 64), ALU.add)
+            tt(ind(Xt(t, XW), R("INV", 4, 6)), R("dm", 0, 32), R("dm", 32, 64), ALU.add)
             if t < 3:
                 sx[t] = send("x%d" % t)
             store("Y", T.yx[:, 128 * t:128 * t + 128], x, "dx%d" % t, 0)
@@ -609,9 +618,9 @@ def build(g, T, topo, rank):
         for h in range(3):
             at(t, "h%d" % h)
             U = H("B6", h)
-            fresh = [(U, Z("Id2"), H("sp", h)), (U, H("sg", 3 + h), Z("Id2"))] if t + h else []
-            group([(U, Z("CUd"), one)] + fresh + [(U, H("sg", h), Z("Id4"))])
-            cc = H("cc", h) if h else H("c16", 0)
+            group([(U, Z("CUd"), H("sp", h))] + [(U, H("sg", 3 + h), Z("Id2"))] * (t + h > 0)
+                  + [(U, Z("BOH"), H("mm", j)) for j in range(h)] + [(U, H("sg", h), Z("Id4"))])
+            cc = H("cc", h) if h else C16(0)
             if h:
                 take(cc, ind(AW, KL("KL", h)))
             tt(H("mm", h), cc, U, ALU.is_lt)
@@ -622,14 +631,19 @@ def build(g, T, topo, rank):
             else:
                 tt(H("nv", h), cc, Wr, ALU.min)
             at(t, "p%d" % h)
-            group([(Fs, Z("Id2"), H("PV", 2))] * (h // 2) + [(Fs, Z("BOBn"), H("mm", j)) for j in range(h)]
+            group([(Fs, Z("Id2"), H("PV", 2)), (Fs, Z("BOBn"), H("mm", 0)), (Fs, Z("BOBn"), H("mm", 1))] * (h // 2)
                   + [(Fs, Z("T3n"), H("mm", h))])
             tt(H("fc", h), cc, Fs, ALU.min)
             if h == 2 and t < 3:
                 at(t, "wk")
-                WK = H("B0", 0)
-                group([(WK, Z("E00"), R("A", n0 - 128, n0))] + [(WK, Wsl("E0w", j + 1), H("c16", j)) for j in range(2)]
+                WK, Zp = H("B7", 0), H("B0", 0)
+                group([[(WK, Z("LT"), Z("I32h")) if t else (WK, Wsl("E0w", 0), C16(2))]
+                       + [(WK, Wsl("E0w", j + 1), C16(j)) for j in range(2)]]
                       + [(WK, Z(l), H("mm", j)) for j, l in enumerate(("BOB", "BK1", "BK2"))])
+                group([(Zp, Z("BO"), H("mm", j)) for j in range(3)])
+                ts(R("esc", 0, 128), Zp, 0.5, ALU.is_lt)
+                act(R("esc", 0, 128), Zp, ACT.Relu, bias=1.0, scale=-1.0)
+                either()
                 take(H("WK", t), WK)
                 sq[t] = send("c%d" % t)
             at(t, "w%d" % h)
@@ -643,10 +657,12 @@ def build(g, T, topo, rank):
             store("S", T.yp[:, half:n0 - 128], R("A", half, n0 - 128), "dy1", 128 * (n0 - 128) * 4)
         at(t, "link")
         LK = R("B1", 384, 448)
-        group([(LK, H("mm", j), R("Wc", 64 * j, 64 * j + 64)) for j in range(3)] + [(LK, H("fc", j), Z("G64")) for j in range(3)])
+        group([(LK, H("mm", j), R("Wc", 64 * (j // 2), 64 * (j // 2) + 64)) for j in range(3)]
+              + [(LK, H("fc", j), Z("G64")) for j in range(3)])
         if t < 3:
             tt(Z("RR"), Z("MK"), LK, ALU.mult)
-            group([[(R("B2", 384, 392), R("Wd", 112 - 16 * a, 240 - 16 * a), R("RR", 8 * a, 8 * a + 8)) for a in range(8)]])
+            mm(groups[0], [(R("B2", 384, 392) + (32 * (a // 2),), R("Wd", 16 - 16 * (a % 2), 48 - 16 * (a % 2)),
+                            R("RR", 8 * a, 8 * a + 8)) for a in range(8)], 2)
             cp(KL("KL", 0), R("B2", 384, 392))
         at(t, "lw")
         ts(G8("LT"), R("B1", 384, 448, 8), 1.0 / 32, ALU.mult)
@@ -658,21 +674,16 @@ def build(g, T, topo, rank):
             store("Y", T.yp[:, n0:E], R("A", n0, E), "dy2", 128 * 512)
             break
         at(t, "ask")
-        Zp = H("B5", 3)
-        group([(Zp, Z("BO"), H("mm", j)) for j in range(3)])
-        ts(R("esc", 0, 128), Zp, 0.5, ALU.is_lt)
-        act(R("esc", 0, 128), Zp, ACT.Relu, bias=1.0, scale=-1.0)
-        either()
         scan(Z("cnt"), Z("ones"), Z("esc"), 0.0, ALU.mult, ALU.add)
-        for k in range(2):
-            at(t, "ask%d" % k)
-            for a in range(2 * k, 2 * k + 2):
-                act(R("junk", XW * a, XW * a + XW), Z("cnt"), ACT.Sign, bias=C("s%d" % a), scale=-1.0, acc=R("acc", a, a + 1))
-            ts(R("INV", 2 * k, 2 * k + 2), R("acc", 2 * k, 2 * k + 2), 0.5, ALU.mult, XW / 2.0, ALU.add)
+        for a in range(2):
+            act(R("junk", XW * a, XW * a + XW), Z("cnt"), ACT.Sign, bias=C("s%d" % a), scale=-1.0, acc=R("acc", a, a + 1))
+        ts(R("INV", 0, 3, 2), R("acc", 0, 2), 0.5, ALU.mult, XW / 2.0, ALU.add)
+        ts(R("INV", 4, 6), R("acc", 0, 2), 0.5, ALU.mult, XW / 2.0, ALU.add)
         at(t, "xz")
-        scaled(Z("xz"), ind(Xt(t, XW), R("INV", 0, 2)), 0.5)
-        dif = group([(Z("B0"), H("PV", 0), R("F", FO, FO + 512)), [(R("B0", i, 512, 16), Z("Idn"), Z("xz")) for i in range(16)]])
-        lin(Z("xo"), ind(Xt(t + 1, XW), R("INV", 2, 4)), 0.5, -0.25)
+        for a in range(2):
+            scaled(R("xz", a, 32, 2), ind(Xt(t, XW), R("INV", 2 * a, 2 * a + 1)), 0.5)
+        dif = group([(Z("B0"), H("PV", 0), R("F", FO, FO + 512)), [(R("B0", i, 512, 16), Z("Id"), Z("xz")) for i in range(16)]])
+        lin(Z("xo"), ind(Xt(t + 1, XW), R("INV", 4, 6)), 0.5, -0.25)
         at(t, "qs")
         QS = R("B3", 384, 416)
         hashed = [(R("B3", 384 + 16 * a, 400 + 16 * a), R("FB%d" % t, 144, FO), R("xz", a, 32, 2)) for a in range(2)]
@@ -682,28 +693,26 @@ def build(g, T, topo, rank):
         lin(Z("qb"), QS, 1.0, 129.0 * HM)
         at(t, "near")
         FBW = R("FB%d" % t, FO, FO + E + 1)
-        cp(Z("cqu"), ind(Z("CO"), R("INV", 0, 2)))
+        for a in range(2):
+            cp(R("cqu", a, 32, 2), ind(Z("CO"), R("INV", 2 * a, 2 * a + 1)))
         at(t, "qm")
-        cp(Z("cq6"), Z("cqu"))
-        group([[(R("B3", 448, 450), Wsl("E0w", b), R("cq6", 2 * b, 2 * b + 2)) for b in range(a, a + 4)] for a in range(0, 16, 4)])
-        ts(R("QM", 0, 2), R("B3", 448, 450), -float(n0), ALU.add)
+        cp(R("c16", 128, 160), ind(Z("CO"), R("INV", 4, 6)))
         at(t, "near")
         for c in range(2):
-            scaled(R("dd", 256 * c, 256 * c + 256), ind(FBW, R("cqu", 16 * c, 16 * c + 16)), 0.5)
-            mm(dif, [(R("B0", 256 * c, 256 * c + 256), Z("Id"), R("dd", 256 * c, 256 * c + 256))])
-        act(Z("da"), Z("B0"), ACT.Abs)
-        key, hole = R("B4", 0, 32), R("B4", 32, 64)
-        sums = [(Wsl("Wn", b), R("dd", 32 * b, 32 * b + 32)) for b in range(16)]
-        gaps = [(Wsl("Wp", b), R("da", 32 * b, 32 * b + 32)) for b in range(16)]
-        group([[(R("B4", 0, 64), Z("Id"), Z("KH")), (hole, Z("Id4"), Z("K2")), (key, Z("I32h"), Z("KC"))]]
-              + [[(hole, l, r) for l, r in part] for part in (sums[:8], sums[8:])] + [[(key, l, r) for l, r in gaps]])
-        scan(R("ks", 32, 96), Z("RB"), R("B4", 0, 64), 0.0, ALU.add, ALU.min)
-        tt(R("ks", 79, 96, 16), R("ks", 79, 96, 16), R("B4", 0, 32, 16), ALU.add)
+            scaled(R("dd", 512 * c, 512 * c + 512, 2), ind(FBW, R("cqu", 16 * c, 16 * c + 16)), -0.5)
+            mm(dif, [(R("B0", 256 * c, 256 * c + 256), Z("Id"), R("dd", 512 * c, 512 * c + 512, 2))])
+        act(R("dd", 1, 1024, 2), Z("B0"), ACT.Abs)
+        both, hole, key = R("B4", 0, 64), R("B4", 0, 64, 2), R("B4", 1, 64, 2)
+        group([[(both, Z("Id"), Z("KH")), (hole, Z("Id4"), Z("K2")), (key, Z("I32h"), Z("KC"))],
+               [(both, Wsl("Wp", b), R("dd", 64 * b, 64 * b + 64)) for b in range(16)]])
+        scan(R("ks", 64, 96), Z("RB"), hole, 0.0, ALU.add, ALU.min)
+        scan(R("ks", 32, 64), Z("RB"), key, 0.0, ALU.add, ALU.min)
+        tt(R("ks", 79, 96, 16), R("ks", 79, 96, 16), R("B4", 1, 64, 32), ALU.add)
         tt(R("b1", 0, 4), R("ks", 47, 96, 16), R("ks", 15, 64, 16), ALU.min)
-        ts(R("b2", 0, 4), R("b1", 0, 4), 511, ALU.bitwise_and)
+        ts(R("b2", 0, 4), R("b1", 0, 4), 1023, ALU.bitwise_and)
         cp(R("BL", 0, 4), R("b2", 0, 4))
         for a in range(2):
-            tt(R("di", 32 * a, 32 * a + 32), ind(Z("dd"), R("BL", 2 * a, 2 * a + 2)), Z("xo"), ALU.add)
+            tt(R("di", 32 * a, 32 * a + 32), ind(Z("dd"), R("BL", 2 * a, 2 * a + 2)), Z("xo"), ALU.subtract)
     return ops, nls
 
 
@@ -746,7 +755,7 @@ def hazards(ops):
 
 
 def figures(ops, preds, fig):
-    cost = [{e: price(v[1], fig) + (fig["fix"] if e in "VS" else 0.0) for e, v in o["alt"].items()} for o in ops]
+    cost = [{e: price(v[1], fig) + fig["fix"] * {"V": 1, "S": SFIX}.get(e, 0) for e, v in o["alt"].items()} for o in ops]
     lat = [o["lat"][0] / fig["bw"] + o["lat"][1] * fig[o["lat"][2]] for o in ops]
     pre = [[(i, 0.0 if o["e"] == "N" or ops[i]["e"] == o["e"] == "P" else fig["sync"]) for i in list(p) + o["after"]]
            for o, p in zip(ops, preds)]
@@ -800,40 +809,135 @@ def lay(seq, before, cost, head, tail, lean):
     return start, end, eng
 
 
-def replay(order, eng, cost, lat, pre, mean=0.0):
-    end, now = [0.0] * len(order), {e: 0.0 for e in "VSPGYN"}
-    for j in order:
+def replay(order, eng, cost, lat, pre, a=0, old=None):
+    end, free, why = [list(v) for v in old] if old else [[0.0] * len(order) for _ in range(3)]
+    now, last, k = {e: 0.0 for e in "VSPGYN"}, {}, a - 1
+    while k >= 0 and len(last) < 5:
+        e = eng[order[k]]
+        if e != "N" and e not in last:
+            now[e], last[e] = free[order[k]], order[k]
+        k -= 1
+    for j in order[a:]:
         e = eng[j]
-        r = now[e]
+        r, w = now[e], -1 - last.get(e, j)
         for i, gap in pre[j]:
             if end[i] + gap > r:
-                r = end[i] + gap
-        r += cost[j][e]
-        if e != "N":
-            now[e] = r
-        end[j] = r + lat[j]
-    return max(end) + mean * sum(end) / len(end)
-
-
-def blocked(order, eng, cost, lat, pre):
-    end, now, last, why = [0.0] * len(order), {e: 0.0 for e in "VSPGYN"}, {}, [None] * len(order)
-    for j in order:
-        e = eng[j]
-        r, why[j] = now[e], (last.get(e), True)
-        for i, gap in pre[j]:
-            if end[i] + gap > r:
-                r, why[j] = end[i] + gap, (i, False)
+                r, w = end[i] + gap, i
         r += cost[j][e]
         if e != "N":
             now[e], last[e] = r, j
-        end[j] = r + lat[j]
-    j, out = end.index(max(end)), []
-    while j is not None:
-        i, queued = why[j]
-        if queued and i is not None:
+        free[j], end[j], why[j] = r, r + lat[j], w
+    return end, free, why
+
+
+def worth(runs):
+    return sum((max(r[0]) + MEAN * sum(r[0]) / len(r[0])) / f["norm"] for r, f in zip(runs, FIGS))
+
+
+def blocked(run):
+    j, out = run[0].index(max(run[0])), []
+    while True:
+        i = run[2][j]
+        if i < 0:
+            i = -1 - i
+            if i == j:
+                return out
             out.append((i, j))
         j = i
-    return out
+
+
+def ahead(order, eng, pre, a, b):
+    j = order[b]
+    need, queues, along = {i for i, gap in pre[j]}, set(), []
+    for u in reversed(order[a:b]):
+        if u in need or eng[u] in queues:
+            if eng[u] == eng[j]:
+                return None
+            along.append(u)
+            need.update(i for i, gap in pre[u])
+            if eng[u] != "N":
+                queues.add(eng[u])
+    moved = set(along)
+    return order[:a] + along[::-1] + [j] + [u for u in order[a:b] if u not in moved] + order[b + 1:]
+
+
+def behind(order, eng, pre, a, b):
+    i = order[a]
+    moved, queues, along = {i}, set(), []
+    for u in order[a + 1:b + 1]:
+        if eng[u] in queues or any(p in moved for p, gap in pre[u]):
+            if eng[u] == eng[i]:
+                return None
+            along.append(u)
+            moved.add(u)
+            if eng[u] != "N":
+                queues.add(eng[u])
+    return order[:a] + [u for u in order[a + 1:b + 1] if u not in moved] + [i] + along + order[b + 1:]
+
+
+def polish(order, eng, sets, pick, swaps, slack):
+    cost, lat, pre = sets[0]
+    runs = [replay(order, eng, *s) for s in sets]
+    cur, held = worth(runs), None
+    best = (cur, order, eng)
+    for r in range(swaps):
+        if held is None:
+            held, pos = [blocked(u) for u in runs], {j: k for k, j in enumerate(order)}
+        f = pick(range(len(sets)))
+        (i, j), how, far = pick(held[f]), pick(range(6)), pick(FARS)
+        a, b, on = pos[i], pos[j], eng
+        free = [u for u in (i, j) if len(cost[u]) > 1]
+        if how >= 4 and free:
+            u, on = pick(free), list(eng)
+            on[u] = "S" if eng[u] == "V" else "V"
+            new, a = order, pos[u]
+        elif how % 2:
+            while far and a > 0:
+                a -= 1
+                far -= eng[order[a]] == eng[j]
+            new = ahead(order, eng, pre, a, b)
+        else:
+            while far and b < len(order) - 1:
+                b += 1
+                far -= eng[order[b]] == eng[j]
+            new = behind(order, eng, pre, a, b)
+        if new is None:
+            continue
+        room = slack * pick(range(100)) / 100 * (1 - r / swaps)
+        first = replay(new, on, *sets[f], a, runs[f])
+        if max(first[0]) > max(runs[f][0]) + room * FIGS[f]["norm"] / 2:
+            continue
+        tried = [first if k == f else replay(new, on, *sets[k], a, runs[k]) for k in range(len(sets))]
+        v = worth(tried)
+        if v <= cur + room:
+            cur, order, eng, runs, held = v, new, on, tried, None
+            if v < best[0]:
+                best = (v, order, eng)
+    return best[1], best[2], best[0]
+
+
+def repeat(ops, order, eng, sets):
+    cost, lat, pre = sets[0]
+    free = replay(order, eng, *sets[0])[1]
+    start = [free[j] - cost[j][eng[j]] for j in range(len(ops))]
+    seen, name = {}, []
+    for o in ops:
+        k = o["d"] + tuple(sorted(o["alt"]))
+        seen[k] = seen.get(k, -1) + 1
+        name.append(k[1:] + (seen[k],))
+    edge = [start[j] for j, o in enumerate(ops) if name[j] == ("p2", "V", 0)]
+    s = min(range(1, NT), key=lambda u: edge[u] - edge[u - 1] + (SHORT if u == NT - 1 else 0.0))
+    span = edge[s] - edge[s - 1]
+    model = {name[j]: j for j in range(len(ops)) if edge[s - 1] <= start[j] < edge[s]}
+    key, on = list(start), list(eng)
+    for j, o in enumerate(ops):
+        u = len([b for b in edge if b <= start[j]])
+        if u:
+            key[j] = edge[0] + span * (u - 1) + (start[j] - edge[u - 1]) * (1 if u == NT else span / (edge[u] - edge[u - 1]))
+        i = model.get(name[j])
+        if i is not None and 1 <= o["d"][0] - ops[i]["d"][0] + s < NT and o["d"][1] != "c":
+            key[j], on[j] = start[i] - edge[s - 1] + edge[0] + span * (o["d"][0] - ops[i]["d"][0] + s - 1), eng[i]
+    return ordered(key, pre), on
 
 
 def schedule(ops, preds):
@@ -851,10 +955,15 @@ def schedule(ops, preds):
         seed[0] = (seed[0] * 1103515245 + 12345) % 2 ** 31
         return seq[(seed[0] >> 8) % len(seq)]
 
-    def judge(key, lean):
+    def judge(key, lean, old=None):
         start, end, eng = lay(ordered(key, pre), pre, cost, zero, lat, lean)
+        if old and start == old[1]:
+            return old
+        if old and max(end) > max(old[2]) + FAIL:
+            return [old[0] + 1e9]
         order = sorted(range(n), key=lambda j: start[j])
-        return sum(replay(order, eng, *s, MEAN) / f["norm"] for s, f in zip(sets, FIGS)), start, end, order, eng
+        runs = [replay(order, eng, *s) for s in sets]
+        return worth(runs), start, end, order, eng, runs
     key = [0.0] * n
     for j in range(n - 1, -1, -1):
         key[j] = min([key[k] - gap for k, gap in suc[j]] + [0.0]) - min(cost[j].values()) - lat[j]
@@ -864,7 +973,7 @@ def schedule(ops, preds):
     for r in range(ROUNDS):
         how, tilt = pick(range(24)), lean
         if how >= 12:
-            held = held or [blocked(cur[3], cur[4], *s) for s in sets]
+            held = held or [blocked(u) for u in cur[5]]
             (i, j), new, d = pick(pick(held)), list(key), pick([10, 100, 300, 1000])
             if len(cost[i]) > 1 and how % 3:
                 tilt = list(lean)
@@ -891,12 +1000,16 @@ def schedule(ops, preds):
                 for k in some:
                     for j in parts[k][a:b]:
                         new[j] += d
-        res = judge(new, tilt)
+        res = judge(new, tilt, cur)
         if res[0] <= cur[0] + SLACK * pick(range(100)) / 100 * (1 - r / ROUNDS):
-            cur, key, lean, held = res, new, tilt, None
+            cur, key, lean, held = res, new, tilt, held if res is cur else None
             if cur[0] < best[0]:
                 best = cur
-    return best[3], best[4]
+    found = polish(best[3], best[4], sets, pick, *SWAPS[0])
+    for swaps in SWAPS[1:]:
+        again = polish(*repeat(ops, found[0], found[1], sets), sets, pick, *swaps)
+        found = again if again[2] < found[2] else found
+    return found[:2]
 
 
 def emit(g, T, ops, preds, order, nls):

from concourse.bass import DstId, RemoteDMATransfer
from concourse.mybir import AluOpType, ActivationFunctionType

ALU = AluOpType
ACT = ActivationFunctionType
M, P, NT, E, HM = 1152, 128, 4, 1664, 1024
FO = 272
FAR = 48
XW = 160
SETS = [(3, 4), (2, 4), (1, 4), (4, 8), (8, 16)]
ONV = [3, 3, 3]
CHH = [[64, 32, 16, 16], [64, 32, 16, 16], [32, 32, 32, 16, 16]]
TSPLIT = [(0, 3)]
BIG = 2048.0
FIGS = [{"cyc": c, "gath": c * ga, "scat": c * sc, "pe": c * 0.53, "sync": sync, "fix": fix, "hop": hop, "dma": 2000.0, "bw": bw,
         "send": 400.0, "norm": norm}
        for c, ga, sc, sync, fix, hop, bw, norm in ((0.95, 1.56, 3.8, 130.0, 18.0, 2300.0, 200.0, 73.0),
                                                    (0.86, 1.3, 3.0, 160.0, 20.0, 2900.0, 150.0, 73.0),
                                                    (1.17, 1.95, 5.0, 130.0, 15.0, 2000.0, 200.0, 94.0),
                                                    (1.12, 1.15, 4.5, 120.0, 25.0, 2000.0, 200.0, 80.0))]
LEAN, SLACK, ROUNDS, SEED, MEAN, FAIL, SHORT = 1500.0, 12.0, 1500, 51, 0.2, 400.0, 600.0
SWAPS = [(30000, 12.0), (20000, 5.0), (20000, 4.0)]
SFIX = 2.5
FARS = [0, 0, 0, 1, 2, 4, 8]
SAME_WAR = True

F32, BF, I32, U16, F16 = "float32", "bfloat16", "int32", "uint16", "float16"
SCRATCH = {}


def _decl(names, cols, dtype, where="sbuf"):
    for nm in names.split():
        SCRATCH[nm] = (where, [128, cols], dtype)


_decl("A", 1800, F32)
_decl("P32", 1672, I32)
_decl("F FB0 FB1 FB2", FO + 1680, BF)
_decl("AB0 AB1 AB2 VM", HM, F32)
_decl("X", 4 * XW, BF)
_decl("dd", 1024, BF)
_decl("XQ", 384, BF)
_decl("ones esc cnt", XW, BF)
_decl("junk", 2 * XW, BF)
_decl("J", 144, BF)
_decl("CO", XW, F32)
_decl("WQ WK", 384, F32)
_decl("R1V tB", 128, F32)
_decl("hwi thi", 4, I32)
_decl("pi", 8, I32)
_decl("col qb RB", 32, F32)
_decl("ks", 96, F32)
_decl("NV", 512, F32)
_decl("J16 Id Idn Id2 Id4 CUd BO BOn BO2 BO3 BO3n BOB BOBn BOH BK1 BK2 BOx0 BOx1 BOx2 T3 T3n THd", 128, BF)
_decl("W1 Wp", 144, BF)
_decl("I32h LT", 128, F16)
_decl("E0w", 144, F16)
_decl("Wd", 48, F16)
_decl("KC", 32, F16)
_decl("RR", 64, F16)
_decl("MK tq", 64, F32)
_decl("G64", 64, F16)
_decl("Wc", 128, BF)
_decl("J8", 64, BF)
_decl("PC DUM nq", 24, F32)
_decl("KI L0", 24, I32)
_decl("KL L0u SL", 24, U16)
_decl("QI QA b1 b2 qc", 8, I32)
_decl("QL INV BL QM", 8, U16)
_decl("acc cs", 8, F32)
_decl("CU", 384, U16)
_decl("raw mx", 6144, BF)
_decl("cc nv", 384, F32)
_decl("fc", 384, F16)
_decl("a0 m0 mm sp PV", 384, BF)
_decl("sg", 768, BF)
_decl("c16", 448, F16)
_decl("cqu", 32, U16)
_decl("xo xz K2 qr eq", 32, BF)
_decl("KH K1 dm", 64, BF)
_decl("di", 64, I32)
_decl("B0 B1 B2 B3 B4 B5 B6 B7", 512, F32, "psum")

SEMAPHORES = ["sV", "sS", "sP", "sG", "ls", "dp0", "dp1", "dp2", "dfr", "dn0", "dn1", "dn2", "dn3", "dhw", "dth",
              "dx0", "dx1", "dx2", "dx3", "dy0", "dy1", "dy2", "dy3", "df0", "df1", "df2",
              "da0", "da1", "da2", "aAB0", "aAB1", "aAB2", "aWQ0", "aWQ1", "aWQ2", "aFB0", "aFB1", "aFB2", "aFX1", "aFX2",
              "hX1", "hX2", "hC0", "hC1", "hC2", "hA0", "hA1", "hA2", "lA0", "lA1", "lA2", "hB"]
ESEM = {"V": "sV", "S": "sS", "P": "sP", "G": "sG"}
WIDTH = {F32: 4, I32: 4, BF: 2, U16: 2, F16: 2}
_ORDER = {}


def R(name, a, b, step=1):
    return (name, a, b, step)


def ncol(r):
    return (r[2] - r[1] + r[3] - 1) // r[3]


def mask_of(engs):
    m = 0
    for e in engs:
        m |= 1 << e
    return m


def pow2(n):
    k = 1
    while 2 * k <= n:
        k *= 2
    return k


def deal(topo, src, dsts):
    chip = topo.cores_of(src)
    off = [j for j, d in enumerate(dsts) if d not in chip]
    on = [j for j, d in enumerate(dsts) if d in chip]
    res, used = {}, []
    for part in (off, on):
        taken = list(used)
        for k, j in enumerate(part):
            en = [e for e in topo.engines(src, dsts[j]) if e not in taken]
            n = pow2(len(en) // len(part))
            res[j] = en[k * n:(k + 1) * n]
            used += res[j]
    return [res[j] for j in range(len(dsts))]


def plan(T, topo, r):
    cores, n = T.cores, len(T.cores)
    me = cores[r]
    dn = [cores[(r - 1 - t) % n] for t in range(3)]
    can = [c for c in topo.cores_of(me) if c not in cores and all(topo.may_write(c, d) for d in dn)]
    near = [c for c in can if topo.die(c) == topo.die(me)]
    far = [c for c in can if topo.die(c) != topo.die(me)]
    hs = (near + far)[:pow2(len(can))]
    h1, calls, hands = hs[0], {}, {h: [] for h in hs}
    h1calls = hands[h1]
    wf, wa = (FO + M + 128) // len(hs), HM // len(hs)
    calls["bulk"] = [(R("F", wf * k, wf * k + wf), h, R("FB0", wf * k, wf * k + wf), "hB") for k, h in enumerate(hs)]

    def frames(t):
        for src, h, mid, sem in calls["bulk"]:
            hands[h].append((sem, [(mid, dn[t], R("FB%d" % t, mid[1], mid[2]), "aFB%d" % t)]))
    frames(0)
    for s in range(3):
        calls["a%d" % s] = [(R("A", wa * k, wa * k + wa), h, R("AB%d" % s, wa * k, wa * k + wa), "hA%d" % s)
                            for k, h in enumerate(hs)]
        for src, h, mid, sem in calls["a%d" % s]:
            hands[h].append((sem, [(mid, dn[s], mid, "aAB%d" % s)]))
        src, mid, new = R("X", XW * s, XW * s + 128), R("XQ", 128 * s, 128 * s + 128), FO + M + 128 * s
        if s == 0:
            frames(1)
            frames(2)
        else:
            want = [(dn[t], R("FB%d" % t, new, new + 128), "aFX%d" % t) for t in range(s, 3)]
            mine = [(src, d, o, sem) for d, o, sem in want if topo.may_write(me, d)]
            via = [(mid, d, o, sem) for d, o, sem in want if not topo.may_write(me, d)]
            if via:
                mine.append((src, h1, mid, "hX%d" % s))
                h1calls.append(("hX%d" % s, via))
            calls["x%d" % s] = mine
        src, mid = R("WK", 128 * s, 128 * s + 128), R("WQ", 128 * s, 128 * s + 128)
        if topo.may_write(me, dn[s]):
            calls["c%d" % s] = [(src, dn[s], mid, "aWQ%d" % s)]
        else:
            calls["c%d" % s] = [(src, h1, mid, "hC%d" % s)]
            h1calls.append(("hC%d" % s, [(mid, dn[s], mid, "aWQ%d" % s)]))
    return me, calls, hands


def arrivals(T, topo, core):
    tot = {}
    for r in range(len(T.cores)):
        me, calls, hands = plan(T, topo, r)
        every = [(me, c) for c in calls.values()] + [(h, c) for h in hands for w, c in hands[h]]
        for src, c in every:
            for tr, en in zip(c, deal(topo, src, [x[1] for x in c])):
                if tr[1] == core:
                    tot[tr[3]] = tot.get(tr[3], 0) + len(en)
    return tot


def ap_of(T, r):
    if len(r) > 4:
        return T[r[0]][r[4]:r[4] + 32, r[1]:r[2]]
    if r[3] == 1:
        return T[r[0]][:, r[1]:r[2]]
    return T[r[0]][:, r[1]:r[2]:r[3]]


def remote_call(g, T, topo, src, c, left="ls"):
    en = deal(topo, src, [x[1] for x in c])
    if len(c) == 1:
        rid, pid = topo.addr(c[0][1], src)
        g.remote_dma(ap_of(T, c[0][2]), ap_of(T, c[0][0]), T.sem[c[0][3]], T.sem[left], pid, rid, mask_of(en[0]))
    else:
        trs = []
        for x, e in zip(c, en):
            rid, pid = topo.addr(x[1], src)
            trs.append(RemoteDMATransfer(dst_ids=[DstId(rid=rid, pnc=pid)], dma_engine_mask=mask_of(e),
                                         remote_sem=T.sem[x[3]], src=ap_of(T, x[0]), dst=ap_of(T, x[2])))
        g.remote_dma_fused(trs, local_sem=T.sem[left])
    return sum(len(e) for e in en)


def price(c, fig):
    return c[0] + c[1] * fig[c[2]]


def build(g, T, topo, rank):
    ops = []
    tag, nls, cn, groups, loaded = [(0, "c")], [0], {}, [0], [0]
    me, calls, hands = plan(T, topo, rank)
    arr = arrivals(T, topo, me)

    def ap(x):
        if x[0] == "ind":
            return ap_of(T, x[1]).indirect(ap_of(T, x[2]))
        return ap_of(T, x)

    def sc(x):
        return ap(x) if isinstance(x, tuple) else x

    def regs(*xs):
        out = []
        for x in xs:
            if isinstance(x, tuple):
                out += [x[1], x[2]] if x[0] == "ind" else [x]
        return out

    def add(eng, emit, rd, out, cost, sem=None, lat=(0, 0, "hop"), after=[], more=(), grp=None):
        wr = list(more)
        if out is not None:
            if out[0] == "ind":
                wr, rd = wr + [out[1]], rd + [out[2]]
            else:
                wr = wr + [out]
        ops.append({"e": eng, "alt": {eng: (emit, cost)}, "r": rd, "w": wr, "sem": sem, "lat": lat, "after": after,
                    "d": tag[0], "grp": grp, "stop": False})
        return len(ops) - 1

    def at(t, d):
        tag[0] = (t, d)

    def vcost(out, ins, two=False):
        if out[0] == "ind":
            return (50, 16 * ncol(out[2]), "scat")
        if ins[0][0] == "ind":
            return (50, ncol(out), "gath")
        k = 1.0
        if two:
            k = 1.0 if any(SCRATCH[x[0]][0] == "psum" for x in ins) else 2.0
        elif all(WIDTH[SCRATCH[x[0]][2]] == 2 for x in ins + [out]):
            k = 0.5
        return (0, max(64, k * ncol(out)), "cyc")

    def ind(w, o):
        return ("ind", w, o)

    def cp(out, i):
        add("V", lambda: g.vector.tensor_copy(ap(out), ap(i)), regs(i), out, vcost(out, [i]))

    def tt(out, a, b, op):
        add("V", lambda: g.vector.tensor_tensor(ap(out), ap(a), ap(b), op), regs(a, b), out, vcost(out, [a, b], True))

    def ts(out, a, s1, op0, s2=None, op1=None):
        if op1 is None:
            f = lambda: g.vector.tensor_scalar(ap(out), ap(a), sc(s1), None, op0)
        else:
            f = lambda: g.vector.tensor_scalar(ap(out), ap(a), sc(s1), sc(s2), op0, op1)
        add("V", f, regs(a, s1, s2), out, vcost(out, [a]))

    def scan(out, d0, d1, init, op0, op1):
        add("V", lambda: g.vector.tensor_tensor_scan(ap(out), ap(d0), ap(d1), init, op0, op1), regs(d0, d1), out,
            vcost(out, [d0, d1]))

    def fill(out, val):
        add("V", lambda: g.vector.memset(ap(out), val), [], out, vcost(out, [out]))

    def act(out, i, func, bias=0.0, scale=1.0, acc=None):
        c = (65, ncol(out), "gath") if i[0] == "ind" else (20 if acc else 0, max(64, ncol(out)), "cyc")
        if acc:
            f = lambda: g.scalar.activation(ap(out), ap(i), func, bias=sc(bias), scale=sc(scale), accum_out=ap(acc))
        elif func == ACT.Copy and scale == 1.0:
            f = lambda: g.scalar.activation(ap(out), ap(i), func)
        else:
            f = lambda: g.scalar.activation(ap(out), ap(i), func, bias=sc(bias), scale=sc(scale))
        add("S", f, regs(i, bias, scale), out, c, more=[acc] if acc else [])

    def either():
        s = ops.pop()
        ops[-1]["alt"].update(s["alt"])

    def take(out, i):
        cp(out, i)
        act(out, i, ACT.Copy)
        either()

    def scaled(out, i, s):
        ts(out, i, s, ALU.mult)
        act(out, i, ACT.Copy, scale=s)
        either()

    def lin(out, i, s, b):
        ts(out, i, s, ALU.mult, b, ALU.add)
        act(out, i, ACT.Identity, bias=b, scale=s)
        either()

    def mm(gid, terms, every=0):
        first = gid == groups[0]
        if first:
            groups[0] += 1
        j = len(ops)

        def f():
            for k, (o, l, r) in enumerate(terms):
                ins = g.tensor.matmul(ap(o), ap(l), ap(r), k % every == 0 if every else first and k == 0,
                                      k % every == every - 1 if every else ops[j]["stop"] and k == len(terms) - 1)
            return ins
        add("P", f, [x for o, l, r in terms for x in (l, r)], None,
            (0, sum(max(min(64, ncol(l)), ncol(r)) * WIDTH[SCRATCH[l[0]][2]] ** 2 // 4 for o, l, r in terms), "pe"),
            grp=gid, more=[o for o, l, r in terms])

    def group(terms):
        gid = groups[0]
        for x in terms:
            if x:
                mm(gid, x if isinstance(x, list) else [x])
        return gid

    def iota(out, pat, base, cm=0):
        if SCRATCH[out[0]][2] == I32:
            f = lambda: g.iota(ap(out), pat, base, cm)
        else:
            f = lambda: g.iota(ap(out), pat, base, cm, allow_small_or_imprecise_dtypes=True)
        add("G", f, [], out, (160, 2 * ncol(out), "cyc"))

    def gfill(out, val):
        iota(out, [[0, ncol(out)]], val)

    def keep(out, i, pat, op, val, base, cm):
        add("G", lambda: g.affine_select(ap(out), ap(i), pat, op, val, base, cm), [i], out, (200, 2 * ncol(out), "cyc"))

    def load(q, out, src, sem):
        qq = g.sync if q == "Y" else g.scalar
        loaded[0] += 128 * ncol(out) * WIDTH[SCRATCH[out[0]][2]]
        add(q, lambda: qq.dma_start(ap(out), src), [], out, (60, 0, "cyc"), sem=(sem, 16),
            lat=(loaded[0], 1, "dma"))

    def store(q, dst, i, sem, nbytes):
        qq = g.sync if q == "Y" else g.scalar
        add(q, lambda: qq.dma_start(dst, ap(i)), [i], None, (60, 0, "cyc"), sem=(sem, 16), lat=(nbytes, 1, "dma"))

    def move(out, i, sem, rows=slice(0, 128)):
        add("Y", lambda: g.sync.dma_start(T[out[0]][rows, out[1]:out[2]], T[i[0]][rows, i[1]:i[2]]), [i], out, (60, 0, "cyc"),
            sem=(sem, 16), lat=(0, 1, "dma"))

    def send(key, left=None):
        c = calls[key]

        def f():
            if left:
                remote_call(g, T, topo, me, c, left)
            else:
                nls[0] += remote_call(g, T, topo, me, c)
            return None
        if left:
            return add("G", f, [x[0] for x in c], None, (0, 1, "send"), lat=(0, 1.5, "dma"),
                       sem=(left, sum(len(e) for e in deal(topo, me, [x[1] for x in c]))))
        return add("G", f, [x[0] for x in c], None, (0, 5 if key == "bulk" else 1, "send"))

    def recv(out, sem, after, hops):
        add("N", None, [], out, (0, 0, "cyc"), sem=(sem, arr[sem]), lat=(0, hops, "hop"), after=after)

    def C(name):
        if name not in cn:
            cn[name] = len(cn)
        return R("col", cn[name], cn[name] + 1)

    def Z(name):
        return R(name, 0, SCRATCH[name][1][1])

    def Wsl(name, i):
        return R(name, 15 - i, 143 - i)

    def H(name, h, n=1):
        return R(name, 128 * h, 128 * (h + n))

    def KL(name, h):
        return R(name, 8 * h, 8 * h + 8)

    def Xt(t, n=128):
        return R("X", XW * t, XW * t + n)

    def G8(name):
        return R(name, 0, 128, 16)

    def C16(h):
        return R("c16", 160 * h, 160 * h + 128)

    def compact(h, n=8):
        group([[(R("B7", 0, n), Wsl("E0w", b), R("c16", 160 * h + b, 160 * h + 16 * n, 16)) for b in range(16)]])

    load("Y", R("P32", 1024, M), T.ptr[:, 1024:M], "dp0")
    load("S", R("P32", 0, 512), T.ptr[:, 0:512], "dp1")
    load("Y", R("P32", 512, 1024), T.ptr[:, 512:1024], "dp2")
    load("S", R("F", FO, FO + M), T.fr[:], "dfr")
    load("Y", R("F", FO + M, FO + M + 128), T.nw[:, 0:128], "df0")
    load("Y", Xt(0), T.nw[:, 0:128], "dn0")
    load("Y", R("thi", 0, 1), T.th[:], "dth")
    load("Y", R("hwi", 0, 1), T.hw[:], "dhw")
    for t in range(1, NT):
        load("Y", Xt(t), T.nw[:, 128 * t:128 * t + 128], "dn%d" % t)
    store("Y", T.yx[:, 0:128], Xt(0), "dx0", 0)
    J128, one = R("J", 0, 128), R("ones", 0, 128)
    fill(Z("ones"), 1.0)
    iota(R("pi", 0, 1), [[0, 1]], 0, 1)
    iota(Z("J"), [[1, 144]], 0)
    iota(Z("J16"), [[16, 8], [0, 16]], 0)
    iota(Z("KH"), [[0, 2], [1024, 16], [0, 2]], 0)
    iota(R("NV", 0, 128), [[1, 128]], M)
    iota(R("NV", 128, 512), [[1, 384]], M + 128)
    iota(Z("tq"), [[0, 8], [16, 8]], 0)
    iota(Z("J8"), [[16, 8], [0, 8]], 0)
    fill(R("P32", M, 1672), E)
    gfill(R("F", FO + M + 128, FO + 1680), FAR)
    for t in range(NT):
        gfill(R("X", XW * t + 128, XW * t + XW), 0)
    for t in range(3):
        gfill(R("FB%d" % t, FO + M + 128 * (t + 1), FO + 1680), FAR)
    gfill(R("CO", 128, XW), 0)
    iota(Z("VM"), [[0, HM // 128], [1, 128]], M)
    cp(C("p"), R("pi", 0, 1))
    ts(R("pi", 4, 5), R("pi", 0, 1), 15, ALU.bitwise_and)
    cp(C("i"), R("pi", 4, 5))
    tt(C("g16"), C("p"), C("i"), ALU.subtract)
    ts(C("r0"), C("i"), 0.0, ALU.is_equal)
    ts(C("r1"), C("i"), 1.0, ALU.is_equal)
    lin(C("nr1"), C("r1"), -1.0, 1.0)
    ts(Z("W1"), R("J", 0, 144), C("g16"), ALU.subtract, 15.0, ALU.is_equal)
    ts(Z("E0w"), Z("W1"), C("r0"), ALU.mult)
    lin(C("hi"), C("r0"), -float(E), float(E))
    lin(C("lo"), C("r1"), -float(E), C("hi"))
    lin(R("A", M, E - 128), R("NV", 128, 512), C("r1"), C("lo"))
    scaled(R("A", E - 128, E), one, C("hi"))
    gfill(R("A", E, 1800), E)
    scaled(Z("R1V"), R("NV", 0, 128), C("r1"))
    cp(C16(2), R("P32", 1024, M))
    ts(Z("tB"), R("P32", 1024, M), C("nr1"), ALU.mult)
    tt(R("P32", 1024, M), Z("tB"), Z("R1V"), ALU.max)
    for a, b in ((0, 256), (256, 512), (512, 768), (768, 1024), (1024, M)):
        cp(R("A", a, b), R("P32", a, b))
    ts(Z("Id"), J128, C("p"), ALU.is_equal)
    ts(Z("BO"), Z("J16"), C("g16"), ALU.is_equal)
    for o, i, s in (("BOn", "BO", -1.0), ("BO2", "BO", 2.0), ("BOB", "BO", BIG), ("BOBn", "BO", -BIG), ("Idn", "Id", -1.0),
                    ("BOH", "BO", -8 * BIG),
                    ("Id2", "Id", BIG), ("Id4", "Id", 2 * BIG), ("Wp", "W1", 32768.0)):
        scaled(Z(o), Z(i), s)
    keep(Z("T3"), Z("BOB"), [[1, 128]], ALU.is_gt, 0.0, 0, -1)
    keep(Z("T3"), Z("T3"), [[1, 128]], ALU.not_equal, -BIG, 0, -1)
    take(G8("T3"), G8("BOB"))
    scaled(Z("T3n"), Z("T3"), -1.0)
    gfill(H("PV", 0), 0)
    scaled(H("PV", 1), J128, 1.0 / BIG)
    scaled(H("PV", 2), one, C("r0"))
    fill(Z("LT"), 0.0)
    ts(Z("Wd"), R("J", 0, 48), C("i"), ALU.subtract, 16.0, ALU.is_equal)
    ts(Z("G64"), Z("J8"), C("g16"), ALU.is_equal)
    ts(Z("MK"), Z("tq"), C("g16"), ALU.is_equal)
    for j in range(2):
        lin(C("c%d" % j), C("i"), -BIG, (31 - 16 * j) * BIG)
        ts(R("Wc", 64 * j, 64 * j + 64), Z("G64"), C("c%d" % j), ALU.mult)
    lin(R("cs", 0, 4), R("J", 0, 4), 1.0 / 16, 1 + M / BIG)
    scaled(R("cs", 4, 8), R("cs", 0, 4), C("r0"))
    for n in sorted(set(ONV)):
        o = "BOx%d" % ONV.index(n)
        keep(Z(o), Z("BOn"), [[0, 32], [1, 4]], ALU.is_ge, 0.0, min(n, 3) - 4, 0)
        for a, step in SETS[3:n]:
            cp(R(o, a, 128, step), R("BOn", a, 128, step))
    for j in (1, 2):
        keep(Z("BK%d" % j), Z("BOB"), [[0, 8], [1, 16]], ALU.is_ge, 0.0, -j, 0)
        scaled(C("n%d" % j), C("r0"), 128.0 * j)
    ts(C("r3"), C("i"), 3.0, ALU.is_lt)
    scaled(Z("BO3"), Z("BO"), C("r3"))
    scaled(Z("BO3n"), Z("BOn"), C("r3"))
    iota(Z("K1"), [[1, 2], [0, 32]], -1)
    gfill(R("ks", 0, 32), 2 ** 24 - 1)
    ts(Z("RB"), R("KH", 0, 64, 2), 1024.0, ALU.is_equal, float(2 ** 25), ALU.mult)
    gfill(Z("K2"), 16384 * 16 * FAR // int(2 * BIG))
    scaled(C("i2"), C("i"), 2.0)
    ts(Z("KC"), R("J", 0, 32), 1.0 / 16, ALU.mult, C("i2"), ALU.add)
    ts(Z("I32h"), Z("Id"), 32.0, ALU.mult)
    gfill(R("esc", 128, XW), 1)
    lin(Z("PC"), R("tq", 0, 24), 1.0, C("i"))
    lin(Z("DUM"), Z("PC"), 1.0, float(E + 2))
    lin(C("cu"), C("r0"), -3 * BIG - E, BIG + E)
    scaled(Z("CUd"), Z("Id"), C("cu"))
    for a in range(2):
        lin(C("s%d" % a), C("i"), 1.0, 16 * a + 0.5)
    cp(C("th"), R("thi", 0, 1))
    cp(C("w"), R("hwi", 0, 1))
    scaled(Z("THd"), Z("Idn"), C("th"))
    scaled(R("F", 0, 144), Z("W1"), C("w"))
    scaled(R("F", 144, FO), Z("BO2"), C("w"))
    sx = {0: send("bulk")}
    sq, sa = {}, {}
    AW, AS, FW = R("A", 0, E + 1), R("A", 0, E + 130), R("F", FO, FO + E + 1)
    bank = ["B1", "B2", "B3"]
    stage = [0]

    def ra(h, i):
        return R("raw", 2048 * h + i, 2048 * (h + 1), 16)

    compact(2)
    cp(KL("KL", 0), R("B7", 0, 8))
    for t in range(NT):
        n0 = M + 128 * t
        x = Xt(t)
        if t < 3:
            at(t, "snap")
            sa[t] = send("a%d" % t, "lA%d" % t)
        for h in range(3):
            at(t, "cu%d" % h)
            cp(H("CU", h), ind(AW if t else R("P32", 0, E + 1), KL("KL", h)))
            if h < 2:
                cp(C16(h), H("CU", h))
                compact(h, 10 if t and not h else 8)
                cp(KL("KL", h + 1), R("B7", 0, 8))
                if t and not h:
                    ts(R("QM", 0, 2), R("B7", 8, 10), 128.0 - n0, ALU.add)
            if h == 2:
                at(t, "sp")
                ts(Z("sp"), Z("CU"), n0 - 0.5, ALU.is_ge, R("cs", 4 + t, 5 + t), ALU.max)
            at(t, "raw%d" % h)
            a = 128 * h
            for n in CHH[h]:
                take(R("raw", 16 * a, 16 * (a + n)), ind(FW, R("CU", a, a + n)))
                a += n
        at(t, "sl")
        ts(Z("KI"), Z("KL"), 1.0 + 1.0 / 3200, ALU.mult)
        ts(Z("L0"), Z("KI"), 127, ALU.bitwise_and)
        cp(Z("L0u"), Z("L0"))
        tt(Z("nq"), Z("L0"), Z("PC"), ALU.not_equal)
        tt(R("tq", 0, 24), Z("nq"), Z("DUM"), ALU.mult)
        tt(Z("nq"), R("tq", 0, 24), Z("KI"), ALU.max)
        cp(Z("SL"), Z("nq"))
        dg = []
        for h in range(3):
            at(t, "wn%d" % h)
            sums = [(R(bank[h], i, 128, 16), ra(h, i), G8("BOn")) for a, step in SETS[:ONV[h]] for i in range(a, 16, step)]
            dg.append(group([(R(bank[h], 0, 128), one, Z("THd")), sums[:4], sums[4:]]))
        if t > 0:
            s = t - 1
            at(t, "ans")
            hops = 2 if calls["c%d" % s][0][1] in hands else 1
            recv(H("WQ", s), "aWQ%d" % s, [sq[s]], hops)
            tt(Z("eq"), ind(H("WQ", s), R("QM", 0, 2)), Z("qb"), ALU.is_equal)
            group([(R("B6", 384, 448), Z("Id"), Z("K1")),
                   [(R("B6", 384, 416), Z("BO3"), Z("eq")), (R("B6", 416, 448), Z("BO3n"), Z("eq"))]])
            tt(Z("dm"), Z("di"), R("B6", 384, 448), ALU.mult)
            tt(ind(Xt(t, XW), R("INV", 4, 6)), R("dm", 0, 32), R("dm", 32, 64), ALU.add)
            if t < 3:
                sx[t] = send("x%d" % t)
            store("Y", T.yx[:, 128 * t:128 * t + 128], x, "dx%d" % t, 0)
        mm(groups[0], [(R("B0", j, 512, 4), Z("Id"), x) for j in range(4)], 1)
        for h0, n in TSPLIT if t else [(1, 2)]:
            at(t, "t%d" % h0)
            take(H("a0", h0, n), ind(x, R("L0u", 8 * h0, 8 * (h0 + n))))
            st = "B%d" % (4 + stage[0] % 2)
            stage[0] += 1
            mm(groups[0], [y for j in range(n) for y in ((H(st, j), Z("Idn"), x), (H(st, j), Z("Id"), H("a0", h0 + j)))], 2)
            act(H("m0", h0, n), H(st, 0, n), ACT.Abs)
            mm(groups[0], [y for h in range(h0, h0 + n) for y in ((H("B7", h), one, Z("THd")), (H("B7", h), H("m0", h), Z("BO")))], 2)
            act(H("sg", 3 + h0, n), H("B7", h0, n), ACT.Sign, bias=0.5, scale=-1.0)
        for h in range(3):
            D = R(bank[h], 0, 128)
            at(t, "d%d" % h)
            mm(dg[h], [(D, x, Z("BOx%d" % ONV.index(ONV[h])))])
            rows = [i for a, step in SETS[ONV[h]:] for i in range(a, 16, step)]
            nch, o = (len(rows) + 3) // 4, 2048 * h
            for c in range(nch):
                some = rows[len(rows) * c // nch:len(rows) * (c + 1) // nch]
                st = "B%d" % (4 + stage[0] % 2)
                stage[0] += 1
                mm(groups[0], [y for j, i in enumerate(some) for y in ((H(st, j), Z("Id"), ra(h, i)), (H(st, j), Z("Idn"), x))], 2)
                act(R("mx", o, o + 128 * len(some)), H(st, 0, len(some)), ACT.Abs)
                mm(dg[h], [(R(bank[h], i, 128, 16), R("mx", o + 128 * j, o + 128 * j + 128), G8("BO")) for j, i in enumerate(some)])
                o += 128 * len(some)
            for a, step in SETS[:ONV[h]]:
                n = 16 // step
                tt(R("mx", o, o + 128 * n), R("raw", 2048 * h + a, 2048 * (h + 1), step), R("B0", 0, 512, step // 4), ALU.max)
                mm(dg[h], [(R(bank[h], a + step * j, 128, 16), R("mx", o + j, o + 128 * n, n), G8("BO2")) for j in range(n)])
                o += 128 * n
            at(t, "s%d" % h)
            act(H("sg", h), D, ACT.Sign, bias=0.5, scale=-1.0)
        if t < 3:
            at(t, "q")
            if t:
                move(R("F", FO + n0, FO + n0 + 128), x, "df%d" % t)
            fb, ab = "FB%d" % t, "AB%d" % t
            recv(R(fb, 0, FO + M + 128), "aFB%d" % t, [sx[0]], 3)
            if t:
                recv(R(fb, FO + M + 128, FO + n0 + 128), "aFX%d" % t, [sx[t]], 2)
            recv(Z(ab), "aAB%d" % t, [sa[t]], 2)
            move(Z(ab), Z("VM"), "da%d" % t, slice(0, 128, 16))
            group([[(R("B7", 0, 8), Wsl(fb, b), R("X", XW * t + b, XW * t + 128, 16)) for b in range(a, a + 4)]
                   for a in range(0, 16, 4)])
            cp(Z("QI"), R("B7", 0, 8))
            ts(Z("QA"), Z("QI"), HM - 1, ALU.bitwise_and)
            cp(Z("QL"), Z("QA"))
            at(t, "co")
            if t:
                lin(H("CO", 0), ind(Z(ab), Z("QL")), 1.0, C("n%d" % t))
            else:
                take(H("CO", 0), ind(Z(ab), Z("QL")))
        for h in range(3):
            at(t, "h%d" % h)
            U = H("B6", h)
            group([(U, Z("CUd"), H("sp", h))] + [(U, H("sg", 3 + h), Z("Id2"))] * (t + h > 0)
                  + [(U, Z("BOH"), H("mm", j)) for j in range(h)] + [(U, H("sg", h), Z("Id4"))])
            cc = H("cc", h) if h else C16(0)
            if h:
                take(cc, ind(AW, KL("KL", h)))
            tt(H("mm", h), cc, U, ALU.is_lt)
            Wr, Fs = H(bank[h], 1), H(bank[max(h - 1, 0)], 2)
            group([[(Wr, Z("Id2"), H("PV", 1)), (Wr, Z("T3"), H("sp", h))]] + [(Wr, Z("BOB"), H("mm", j)) for j in range(h + 1)])
            if h:
                act(H("nv", h), Wr, ACT.Relu, bias=float(E), scale=-1.0)
            else:
                tt(H("nv", h), cc, Wr, ALU.min)
            at(t, "p%d" % h)
            group([(Fs, Z("Id2"), H("PV", 2)), (Fs, Z("BOBn"), H("mm", 0)), (Fs, Z("BOBn"), H("mm", 1))] * (h // 2)
                  + [(Fs, Z("T3n"), H("mm", h))])
            tt(H("fc", h), cc, Fs, ALU.min)
            if h == 2 and t < 3:
                at(t, "wk")
                WK, Zp = H("B7", 0), H("B0", 0)
                group([[(WK, Z("LT"), Z("I32h")) if t else (WK, Wsl("E0w", 0), C16(2))]
                       + [(WK, Wsl("E0w", j + 1), C16(j)) for j in range(2)]]
                      + [(WK, Z(l), H("mm", j)) for j, l in enumerate(("BOB", "BK1", "BK2"))])
                group([(Zp, Z("BO"), H("mm", j)) for j in range(3)])
                ts(R("esc", 0, 128), Zp, 0.5, ALU.is_lt)
                act(R("esc", 0, 128), Zp, ACT.Relu, bias=1.0, scale=-1.0)
                either()
                take(H("WK", t), WK)
                sq[t] = send("c%d" % t)
            at(t, "w%d" % h)
            if h:
                tt(ind(AS, KL("SL", h)), cc, H("nv", h), ALU.subtract)
            else:
                cp(ind(AS, KL("SL", h)), H("nv", h))
        if t == 3:
            half = (n0 - 128) // 2
            store("Y", T.yp[:, 0:half], R("A", 0, half), "dy0", 128 * (n0 - 128) * 4)
            store("S", T.yp[:, half:n0 - 128], R("A", half, n0 - 128), "dy1", 128 * (n0 - 128) * 4)
        at(t, "link")
        LK = R("B1", 384, 448)
        group([(LK, H("mm", j), R("Wc", 64 * (j // 2), 64 * (j // 2) + 64)) for j in range(3)]
              + [(LK, H("fc", j), Z("G64")) for j in range(3)])
        if t < 3:
            tt(Z("RR"), Z("MK"), LK, ALU.mult)
            mm(groups[0], [(R("B2", 384, 392) + (32 * (a // 2),), R("Wd", 16 - 16 * (a % 2), 48 - 16 * (a % 2)),
                            R("RR", 8 * a, 8 * a + 8)) for a in range(8)], 2)
            cp(KL("KL", 0), R("B2", 384, 392))
        at(t, "lw")
        ts(G8("LT"), R("B1", 384, 448, 8), 1.0 / 32, ALU.mult)
        group([(H("B4", 0), Z("LT"), Z("I32h"))])
        tt(R("A", n0, n0 + 128), R("A", n0, n0 + 128), H("B4", 0), ALU.add)
        if t == 2:
            store("Y", T.yp[:, n0:n0 + 128], R("A", n0, n0 + 128), "dy3", 128 * 512)
        if t == 3:
            store("Y", T.yp[:, n0:E], R("A", n0, E), "dy2", 128 * 512)
            break
        at(t, "ask")
        scan(Z("cnt"), Z("ones"), Z("esc"), 0.0, ALU.mult, ALU.add)
        for a in range(2):
            act(R("junk", XW * a, XW * a + XW), Z("cnt"), ACT.Sign, bias=C("s%d" % a), scale=-1.0, acc=R("acc", a, a + 1))
        ts(R("INV", 0, 3, 2), R("acc", 0, 2), 0.5, ALU.mult, XW / 2.0, ALU.add)
        ts(R("INV", 4, 6), R("acc", 0, 2), 0.5, ALU.mult, XW / 2.0, ALU.add)
        at(t, "xz")
        for a in range(2):
            scaled(R("xz", a, 32, 2), ind(Xt(t, XW), R("INV", 2 * a, 2 * a + 1)), 0.5)
        dif = group([(Z("B0"), H("PV", 0), R("F", FO, FO + 512)), [(R("B0", i, 512, 16), Z("Id"), Z("xz")) for i in range(16)]])
        lin(Z("xo"), ind(Xt(t + 1, XW), R("INV", 4, 6)), 0.5, -0.25)
        at(t, "qs")
        QS = R("B3", 384, 416)
        hashed = [(R("B3", 384 + 16 * a, 400 + 16 * a), R("FB%d" % t, 144, FO), R("xz", a, 32, 2)) for a in range(2)]
        mm(groups[0], hashed, 1)
        lin(Z("qr"), QS, 1.0, 128.0 * HM + HM / 2 + 0.5)
        group([[(QS, Z("Idn"), Z("qr"))] + hashed])
        lin(Z("qb"), QS, 1.0, 129.0 * HM)
        at(t, "near")
        FBW = R("FB%d" % t, FO, FO + E + 1)
        for a in range(2):
            cp(R("cqu", a, 32, 2), ind(Z("CO"), R("INV", 2 * a, 2 * a + 1)))
        at(t, "qm")
        cp(R("c16", 128, 160), ind(Z("CO"), R("INV", 4, 6)))
        at(t, "near")
        for c in range(2):
            scaled(R("dd", 512 * c, 512 * c + 512, 2), ind(FBW, R("cqu", 16 * c, 16 * c + 16)), -0.5)
            mm(dif, [(R("B0", 256 * c, 256 * c + 256), Z("Id"), R("dd", 512 * c, 512 * c + 512, 2))])
        act(R("dd", 1, 1024, 2), Z("B0"), ACT.Abs)
        both, hole, key = R("B4", 0, 64), R("B4", 0, 64, 2), R("B4", 1, 64, 2)
        group([[(both, Z("Id"), Z("KH")), (hole, Z("Id4"), Z("K2")), (key, Z("I32h"), Z("KC"))],
               [(both, Wsl("Wp", b), R("dd", 64 * b, 64 * b + 64)) for b in range(16)]])
        scan(R("ks", 64, 96), Z("RB"), hole, 0.0, ALU.add, ALU.min)
        scan(R("ks", 32, 64), Z("RB"), key, 0.0, ALU.add, ALU.min)
        tt(R("ks", 79, 96, 16), R("ks", 79, 96, 16), R("B4", 1, 64, 32), ALU.add)
        tt(R("b1", 0, 4), R("ks", 47, 96, 16), R("ks", 15, 64, 16), ALU.min)
        ts(R("b2", 0, 4), R("b1", 0, 4), 1023, ALU.bitwise_and)
        cp(R("BL", 0, 4), R("b2", 0, 4))
        for a in range(2):
            tt(R("di", 32 * a, 32 * a + 32), ind(Z("dd"), R("BL", 2 * a, 2 * a + 2)), Z("xo"), ALU.subtract)
    return ops, nls


def hazards(ops):
    hist, runs, preds = {}, {}, []
    for j, o in enumerate(ops):
        pr = {}
        both = [(False, r) for r in o["r"]] + [(True, r) for r in o["w"]]
        for wr, r in both:
            if SCRATCH[r[0]][0] == "psum":
                st = runs.setdefault(r[0], {"key": None, "cur": [], "old": [], "by": {}})
                key = (o["e"] if len(o["alt"]) == 1 else j, o["grp"])
                if o["grp"] is not None and o["grp"] in st["by"] and st["key"] != key:
                    raise ValueError("group cut on " + r[0])
                if st["key"] != key:
                    st["key"], st["old"], st["cur"] = key, st["cur"], []
                    st["by"][o["grp"]] = True
                for i in st["old"]:
                    pr[i] = True
                if o["grp"] is not None and st["cur"] and st["cur"][0] != j:
                    pr[st["cur"][0]] = True
                if j not in st["cur"]:
                    st["cur"].append(j)
                if o["e"] == "P":
                    continue
            for (a, b, i, w2, sp) in hist.get(r[0], []):
                apart = sp == r[3] and (a - r[1]) % sp != 0
                if i != j and a < r[2] and r[1] < b and (wr or w2) and not apart:
                    pr[i] = pr.get(i, False) or w2
        for wr, r in both:
            if SCRATCH[r[0]][0] == "psum" and o["e"] == "P":
                hist[r[0]] = []
                continue
            lst = hist.setdefault(r[0], [])
            if wr and r[3] == 1:
                lst[:] = [z for z in lst if not (r[1] <= z[0] and z[1] <= r[2])]
            lst.append((r[1], r[2], j, wr, r[3]))
        preds.append(pr)
    return preds


def figures(ops, preds, fig):
    cost = [{e: price(v[1], fig) + fig["fix"] * {"V": 1, "S": SFIX}.get(e, 0) for e, v in o["alt"].items()} for o in ops]
    lat = [o["lat"][0] / fig["bw"] + o["lat"][1] * fig[o["lat"][2]] for o in ops]
    pre = [[(i, 0.0 if o["e"] == "N" or ops[i]["e"] == o["e"] == "P" else fig["sync"]) for i in list(p) + o["after"]]
           for o, p in zip(ops, preds)]
    return cost, lat, pre


def ordered(key, before):
    done, out = [False] * len(key), []
    for j in sorted(range(len(key)), key=lambda j: key[j]):
        if done[j]:
            continue
        stack = [j]
        while stack:
            u = stack[-1]
            miss = [] if done[u] else [i for i, gap in before[u] if not done[i]]
            if miss:
                stack += miss
            else:
                if not done[u]:
                    done[u] = True
                    out.append(u)
                stack.pop()
    return out


def lay(seq, before, cost, head, tail, lean):
    start, end, eng = [0.0] * len(seq), [0.0] * len(seq), [None] * len(seq)
    lines = {e: [] for e in "VSPGYN"}
    for j in seq:
        r = 0.0
        for i, gap in before[j]:
            if end[i] + gap > r:
                r = end[i] + gap
        r += head[j]
        best = None
        for e, c in cost[j].items():
            line, t = lines[e], r
            k = m = len(line)
            while k and line[k - 1][1] > r:
                k -= 1
            while k < m and line[k][0] < t + c:
                t = line[k][1]
                k += 1
            key = t + c + (lean[j] if e == "V" else 0.0)
            if best is None or key < best[0]:
                best = (key, t, k, e, c)
        key, t, k, e, c = best
        if e != "N":
            lines[e].insert(k, (t, t + c))
        start[j], eng[j], end[j] = t - head[j], e, t + c + tail[j]
    return start, end, eng


def replay(order, eng, cost, lat, pre, a=0, old=None):
    end, free, why = [list(v) for v in old] if old else [[0.0] * len(order) for _ in range(3)]
    now, last, k = {e: 0.0 for e in "VSPGYN"}, {}, a - 1
    while k >= 0 and len(last) < 5:
        e = eng[order[k]]
        if e != "N" and e not in last:
            now[e], last[e] = free[order[k]], order[k]
        k -= 1
    for j in order[a:]:
        e = eng[j]
        r, w = now[e], -1 - last.get(e, j)
        for i, gap in pre[j]:
            if end[i] + gap > r:
                r, w = end[i] + gap, i
        r += cost[j][e]
        if e != "N":
            now[e], last[e] = r, j
        free[j], end[j], why[j] = r, r + lat[j], w
    return end, free, why


def worth(runs):
    return sum((max(r[0]) + MEAN * sum(r[0]) / len(r[0])) / f["norm"] for r, f in zip(runs, FIGS))


def blocked(run):
    j, out = run[0].index(max(run[0])), []
    while True:
        i = run[2][j]
        if i < 0:
            i = -1 - i
            if i == j:
                return out
            out.append((i, j))
        j = i


def ahead(order, eng, pre, a, b):
    j = order[b]
    need, queues, along = {i for i, gap in pre[j]}, set(), []
    for u in reversed(order[a:b]):
        if u in need or eng[u] in queues:
            if eng[u] == eng[j]:
                return None
            along.append(u)
            need.update(i for i, gap in pre[u])
            if eng[u] != "N":
                queues.add(eng[u])
    moved = set(along)
    return order[:a] + along[::-1] + [j] + [u for u in order[a:b] if u not in moved] + order[b + 1:]


def behind(order, eng, pre, a, b):
    i = order[a]
    moved, queues, along = {i}, set(), []
    for u in order[a + 1:b + 1]:
        if eng[u] in queues or any(p in moved for p, gap in pre[u]):
            if eng[u] == eng[i]:
                return None
            along.append(u)
            moved.add(u)
            if eng[u] != "N":
                queues.add(eng[u])
    return order[:a] + [u for u in order[a + 1:b + 1] if u not in moved] + [i] + along + order[b + 1:]


def polish(order, eng, sets, pick, swaps, slack):
    cost, lat, pre = sets[0]
    runs = [replay(order, eng, *s) for s in sets]
    cur, held = worth(runs), None
    best = (cur, order, eng)
    for r in range(swaps):
        if held is None:
            held, pos = [blocked(u) for u in runs], {j: k for k, j in enumerate(order)}
        f = pick(range(len(sets)))
        (i, j), how, far = pick(held[f]), pick(range(6)), pick(FARS)
        a, b, on = pos[i], pos[j], eng
        free = [u for u in (i, j) if len(cost[u]) > 1]
        if how >= 4 and free:
            u, on = pick(free), list(eng)
            on[u] = "S" if eng[u] == "V" else "V"
            new, a = order, pos[u]
        elif how % 2:
            while far and a > 0:
                a -= 1
                far -= eng[order[a]] == eng[j]
            new = ahead(order, eng, pre, a, b)
        else:
            while far and b < len(order) - 1:
                b += 1
                far -= eng[order[b]] == eng[j]
            new = behind(order, eng, pre, a, b)
        if new is None:
            continue
        room = slack * pick(range(100)) / 100 * (1 - r / swaps)
        first = replay(new, on, *sets[f], a, runs[f])
        if max(first[0]) > max(runs[f][0]) + room * FIGS[f]["norm"] / 2:
            continue
        tried = [first if k == f else replay(new, on, *sets[k], a, runs[k]) for k in range(len(sets))]
        v = worth(tried)
        if v <= cur + room:
            cur, order, eng, runs, held = v, new, on, tried, None
            if v < best[0]:
                best = (v, order, eng)
    return best[1], best[2], best[0]


def repeat(ops, order, eng, sets):
    cost, lat, pre = sets[0]
    free = replay(order, eng, *sets[0])[1]
    start = [free[j] - cost[j][eng[j]] for j in range(len(ops))]
    seen, name = {}, []
    for o in ops:
        k = o["d"] + tuple(sorted(o["alt"]))
        seen[k] = seen.get(k, -1) + 1
        name.append(k[1:] + (seen[k],))
    edge = [start[j] for j, o in enumerate(ops) if name[j] == ("p2", "V", 0)]
    s = min(range(1, NT), key=lambda u: edge[u] - edge[u - 1] + (SHORT if u == NT - 1 else 0.0))
    span = edge[s] - edge[s - 1]
    model = {name[j]: j for j in range(len(ops)) if edge[s - 1] <= start[j] < edge[s]}
    key, on = list(start), list(eng)
    for j, o in enumerate(ops):
        u = len([b for b in edge if b <= start[j]])
        if u:
            key[j] = edge[0] + span * (u - 1) + (start[j] - edge[u - 1]) * (1 if u == NT else span / (edge[u] - edge[u - 1]))
        i = model.get(name[j])
        if i is not None and 1 <= o["d"][0] - ops[i]["d"][0] + s < NT and o["d"][1] != "c":
            key[j], on[j] = start[i] - edge[s - 1] + edge[0] + span * (o["d"][0] - ops[i]["d"][0] + s - 1), eng[i]
    return ordered(key, pre), on


def schedule(ops, preds):
    n = len(ops)
    sets = [figures(ops, preds, f) for f in FIGS]
    cost, lat, pre = sets[0]
    suc, zero, parts, seed = [[] for _ in range(n)], [0.0] * n, {}, [SEED]
    for j in range(n):
        parts.setdefault(ops[j]["d"], []).append(j)
        for i, gap in pre[j]:
            suc[i].append((j, gap))
    names = list(parts)

    def pick(seq):
        seed[0] = (seed[0] * 1103515245 + 12345) % 2 ** 31
        return seq[(seed[0] >> 8) % len(seq)]

    def judge(key, lean, old=None):
        start, end, eng = lay(ordered(key, pre), pre, cost, zero, lat, lean)
        if old and start == old[1]:
            return old
        if old and max(end) > max(old[2]) + FAIL:
            return [old[0] + 1e9]
        order = sorted(range(n), key=lambda j: start[j])
        runs = [replay(order, eng, *s) for s in sets]
        return worth(runs), start, end, order, eng, runs
    key = [0.0] * n
    for j in range(n - 1, -1, -1):
        key[j] = min([key[k] - gap for k, gap in suc[j]] + [0.0]) - min(cost[j].values()) - lat[j]
    lean, free = [LEAN] * n, [j for j in range(n) if len(cost[j]) > 1]
    cur = best = judge(key, lean)
    held = None
    for r in range(ROUNDS):
        how, tilt = pick(range(24)), lean
        if how >= 12:
            held = held or [blocked(u) for u in cur[5]]
            (i, j), new, d = pick(pick(held)), list(key), pick([10, 100, 300, 1000])
            if len(cost[i]) > 1 and how % 3:
                tilt = list(lean)
                tilt[i] = 5000.0 if cur[4][i] == "V" else -5000.0
            elif how % 3:
                new[j] = min(new[i], new[j]) - d
            else:
                new[i] = max(new[i], new[j]) + d
        elif how == 0:
            new = [-v for v in lay(ordered([-v for v in cur[2]], suc), suc, cost, lat, zero, lean)[1]]
        elif how > 9:
            new, tilt, a = key, list(lean), pick(range(len(free)))
            for j in free[a:a + pick([1, 1, 2])]:
                tilt[j] = pick([-3000.0, 0.0, LEAN, 3000.0])
        else:
            new = list(cur[1] if how == 1 else key)
            for _ in range(pick([1, 1, 2, 4])):
                name, d = pick(names), pick([-1, 1]) * pick([100, 200, 400, 800, 1500, 3000])
                some = [name] if pick([0, 1]) else [k for k in names if k[1] == name[1]]
                a, b = 0, n
                if pick(range(5)) < 2:
                    a = pick(range(len(parts[name])))
                    b = a + pick([1, 2, 4, 8])
                for k in some:
                    for j in parts[k][a:b]:
                        new[j] += d
        res = judge(new, tilt, cur)
        if res[0] <= cur[0] + SLACK * pick(range(100)) / 100 * (1 - r / ROUNDS):
            cur, key, lean, held = res, new, tilt, held if res is cur else None
            if cur[0] < best[0]:
                best = cur
    found = polish(best[3], best[4], sets, pick, *SWAPS[0])
    for swaps in SWAPS[1:]:
        again = polish(*repeat(ops, found[0], found[1], sets), sets, pick, *swaps)
        found = again if again[2] < found[2] else found
    return found[:2]


def emit(g, T, ops, preds, order, nls):
    queue = {"V": g.vector, "S": g.scalar, "P": g.tensor, "G": g, "Y": g.sync}
    pos, cnt, final = {}, {}, {}
    at = {j: k for k, j in enumerate(order)}
    for j in order:
        e = ops[j]["e"]
        cnt[e] = cnt.get(e, 0) + 1
        pos[j] = cnt[e]
        if ops[j]["grp"] is not None:
            final[ops[j]["grp"]] = j
    for j in final.values():
        ops[j]["stop"] = True
    known, clock, waits, target = {}, {}, {}, set()
    for j in order:
        o = ops[j]
        e = o["e"]
        if e == "N":
            clock[j] = {}
            continue
        kn = known.setdefault(e, {})
        need = {}
        for i, raw in preds[j].items():
            p = ops[i]
            if p["sem"] is not None:
                key, val = p["sem"][0], 1
            elif p["e"] == "G" and not p["w"]:
                continue
            else:
                if p["e"] == e and (e == "P" or not (raw or SAME_WAR)):
                    continue
                key, val = p["e"], pos[i]
            if key not in need or val > need[key][0]:
                need[key] = (val, i)
        ws = []
        for key, (val, i) in sorted(need.items(), key=lambda z: -at[z[1][1]]):
            if kn.get(key, 0) >= val:
                continue
            ws.append(i)
            target.add(i)
            kn[key] = val
            for k2, v2 in clock[i].items():
                kn[k2] = max(kn.get(k2, 0), v2)
        waits[j] = ws
        clock[j] = dict(kn)
    count, total = {}, {}
    for j in order:
        o = ops[j]
        if o["sem"] is not None:
            total[o["sem"][0]] = o["sem"][1]
        elif j in target:
            s = ESEM[o["e"]]
            total[s] = total.get(s, 0) + 1
            count[j] = total[s]
    for j in order:
        o = ops[j]
        if o["e"] == "N":
            continue
        q = queue[o["e"]]
        for i in waits[j]:
            p = ops[i]
            if p["sem"] is not None:
                q.wait_ge(T.sem[p["sem"][0]], p["sem"][1])
            else:
                q.wait_ge(T.sem[ESEM[p["e"]]], count[i])
        ins = o["alt"][o["e"]][0]()
        if ins is None:
            continue
        if o["sem"] is not None:
            ins.then_inc(T.sem[o["sem"][0]], o["sem"][1])
        elif j in target:
            ins.then_inc(T.sem[ESEM[o["e"]]], 1)
    g.wait_ge(T.sem["ls"], nls[0])
    for s, v in total.items():
        g.wait_ge(T.sem[s], v)


def rank_program(g, core, T, topo):
    rank = T.rank_of(core)
    if rank is None:
        for r in range(len(T.cores)):
            if core not in topo.cores_of(T.cores[r]):
                continue
            mine = plan(T, topo, r)[2].get(core, [])
            if mine:
                arr, seen, n = arrivals(T, topo, core), [], 0
                for w, c in mine:
                    if w not in seen:
                        g.wait_ge(T.sem[w], arr[w])
                        seen.append(w)
                    n += remote_call(g, T, topo, core, c)
                g.wait_ge(T.sem["ls"], n)
        return
    ops, nls = build(g, T, topo, rank)
    preds = hazards(ops)
    if "o" not in _ORDER:
        _ORDER["o"] = schedule(ops, preds)
    order, eng = _ORDER["o"]
    for o, e in zip(ops, eng):
        o["e"] = e
    emit(g, T, ops, preds, order, nls)
